import numpy as np, ml_dtypes
CORES = [23,119,17,113]
N = 4
import mx_ref
BF = ml_dtypes.bfloat16
def gcols(t, e):
    v = np.concatenate([t.reshape(8, 16, -1, 4), np.zeros((8, 16, 1, 4), BF)], axis=2)
    return np.ascontiguousarray(np.stack([v[g][:, e[g]] for g in range(8)])).reshape(128, -1)
def tile(rs):
    return np.stack(rs, axis=2).reshape(128, -1).astype(BF)
def pick(q, e):
    c = np.concatenate([q[0].reshape(128, -1, 4), np.zeros((128, 1, 4), np.uint8)], axis=1); s = np.concatenate([q[1], np.ones((16, 1), np.uint8)], axis=1)
    return (np.ascontiguousarray(c[:, e].reshape(128, -1)), np.ascontiguousarray(s[:, e]))
def join(*qs):
    return (np.concatenate([q[0] for q in qs], axis=1), np.concatenate([q[1] for q in qs], axis=1))
def put(q, e, v):
    c, s = q[0].reshape(128, -1, 4).copy(), q[1].copy(); c[:, e] = v[0].reshape(128, -1, 4); s[:, e] = v[1]
    return (c.reshape(128, -1), s)
def pk(c, s):
    return (np.ascontiguousarray(c), mx_ref.live(s))
def emit(q):
    return q[0], q[1]
def packed(v, rng):
    q = [mx_ref.quantize(np.ascontiguousarray(v[r])) for r in range(N)]
    return np.stack([a for a, b in q]), np.stack([mx_ref.plane(b, rng) for a, b in q])
def values_of_codes():
    e, c = np.zeros((128, 128, 4), np.float32), np.zeros((128, 2, 4), np.uint8)
    e[np.arange(128), np.arange(128), 0] = 1
    c[:127, :, 0] = np.arange(256).reshape(2, 128).T[:127]
    return mx_ref.matmul(mx_ref.quantize(e.reshape(128, 512).astype(BF)), (c.reshape(128, 8), np.full((16, 2), 127, np.uint8))).T.reshape(-1).astype(np.float64)
CODE_VALUE, SCALE_VALUE = values_of_codes(), 2.0 ** (np.arange(256) - 127.0)
def decode(q):
    return (CODE_VALUE[q[0]].reshape(16, 8, -1, 4) * SCALE_VALUE[q[1]][:, None, :, None] + 0.0).reshape(128, -1).astype(np.float32)
def f(rng, *shape):
    return mx_ref.flush((rng.standard_normal(shape, dtype=np.float32) * np.exp2(rng.integers(-2, 3, shape[:-1] + (1,)))).astype(BF))
def wide(rng, *shape, cols=0):
    v = rng.standard_normal(shape, dtype=np.float32) * np.exp2(rng.integers(-12, 13, shape)).astype(np.float32)
    if cols: v *= np.repeat(np.exp2(rng.integers(-cols, cols + 1, shape[:-2] + (1, shape[-1] // 4))) * (rng.random(shape[:-2] + (1, shape[-1] // 4)) > 0.0625), 4, axis=-1).astype(np.float32)
    return mx_ref.flush(v.astype(BF))
C, K, P, R = 320, 160, 480, 3
ODD = np.arange(1, C, 2)
REFS = np.full((K + 127) // 128 * 128, -1)
REFS[:K] = ODD
def layers(rng):
    return np.array(f(rng, N, 128, 2048)).reshape(N, 8, 16, 4, 8, 16, 4)
def weights(rng, w):
    c, s = packed(np.ascontiguousarray(w).reshape(N, 128, 2048), rng)
    return {"wc": c, "ws": s}
def full(rng, x, w):
    return {"x": np.ascontiguousarray(x).astype(np.float32).reshape(N, 128, 4 * C).astype(BF), "v": np.array(f(rng, N, 128, 512)), **weights(rng, w)}
def apart(rng):
    x = np.array(f(rng, N, 128, 4 * C)).astype(np.float32).reshape(N, 8, 16, C, 4)
    h = rng.permutation(8)[:2]
    x[:, :, :, 1::2] = 0
    x[:, h] = 0
    w = layers(rng)
    w[:, h] = 0
    w[:, :, :, :, h] = 0
    return x, int(h[0]), int(h[1]), w
def setup_inputs(rng):
    return full(rng, np.array(f(rng, N, 128, 4 * C)), layers(rng))
def setup_inputs_ties(rng):
    x, a, b, w = apart(rng)
    x[:, a, :2, ::2] = rng.integers(0, 3, (N, 2, K, 4))
    s = rng.integers(0, 2, (N, 2, K, 4)) * 2.0 ** -8
    s[:, 0, :, 0] = 2.0 ** -8
    x[:, a, :2, 1::2] = s
    for r in range(N):
        k = 2 * int(rng.integers(K)) + 1
        x[r, a, :2, k] = 0
        x[r, a, 0, k, 0] = -2.0 ** -8
    o = rng.permutation(N)
    x[o[0], :, :, 1::2] = 0
    i = [g for g in (2, 4, 6) if g not in (a, b)][0]
    w[o[0], [g for g in range(8) if g != i]] = 0
    x[o[1]] = x[o[1]][:, :, :1].copy()
    return full(rng, x, w)
def setup_inputs_near(rng):
    x, a, b, w = apart(rng)
    c, d = [int(g) for g in rng.permutation(8) if g not in (a, b)][:2]
    x[:, a, 0, ::2, 0] = 1
    x[:, a, 8:12, ::2] = rng.integers(0, 2, (N, 4, K, 4)) * np.exp2(np.arange(4) - 23.0)
    x[:, a, 12, ::2, 0] = 2.0 ** -10
    x[:, b, :4, ::2] = (1 + rng.integers(0, 4, (N, 4, K, 4)) * 0.25) * 2.0 ** -30
    o = rng.permutation(N) % 4
    for r in range(N):
        s = rng.integers(0, 2, (4, K, 4)) * 1.0
        s[0, :, 0] = 1
        if o[r] < 2:
            k = 2.0 ** -8 if o[r] == 0 else 2.0 ** -30
            x[r, a, 0, 1::2, 0] = k
            x[r, a, 12, 1::2, 0] = k
            x[r, a, 8:12, 1::2] = s * k
        else: x[r, b, :4, 1::2] = s * 2.0 ** -30
        if o[r] % 2 == 0: x[r, a, 0, 2 * int(rng.integers(K)), 0] = 2.0 ** 29
    x[:, b, 8, ::2, 0] = 1.96875
    x[:, b, 9:11, ::2] = rng.integers(8, 16, (N, 2, K, 4)) * np.exp2(-13.0 - np.arange(4))
    x[:, :, :, 1:16:2] = 0
    for j in range(8): x[:, b, 9 + j // 4, 2 * j + 1, j % 4] = 1
    x[:, c, :8, ::2] = 0
    x[:, c, 0, ::2, 0] = -3.5
    x[:, d, 8, ::2, :2] = 1
    w[:, :, :, :, d] = 0
    w[:, :, :, :, c, :8] = 0
    w[:, d, 8, :, c, :8, 0] = ((2 * rng.integers(4, 8, (N, 4, 8)) + 1) * np.exp2(-8.0 - np.arange(8) % 4)).astype(np.float32).astype(BF)
    w[:, d, 8, 0, c, 0, 0] = 60
    w[:, d, 8, 0, c, 0, 1] = 3
    return full(rng, x, w)
def setup_inputs_huge(rng):
    x = 0.8 + 0.2 * rng.random((N, 8, 16, C, 4))
    for r in range(N): x[r, :, :, 2 * int(rng.integers(K)) + 1] *= -1.0
    x *= 2.0 ** 30 * float(rng.choice([-1.0, 1.0]))
    w = np.zeros((N, 128, 4, 128, 4), np.float32)
    i = np.arange(128)
    for b in range(4): w[:, i, b, i, b] = -1
    return full(rng, x, w.astype(BF))
def setup_inputs_far(rng):
    x = np.exp2(rng.integers(-14, -7, (N, 16, 8, C, 4))) * (1 + (2 * rng.integers(0, 64, (N, 16, 8, C, 4)) + 1) * 2.0 ** -7) * rng.choice([-1.0, 1.0], (N, 16, 8, C, 4))
    x[:, :, int(rng.integers(8)), :, int(rng.integers(4))] = 1.96875
    x *= np.exp2(-rng.integers(0, 3, (N, 16, 1, C, 1)))
    x *= np.exp2(3.0 * rng.permutation(N))[:, None, None, None, None]
    return full(rng, x, layers(rng))
def setup_inputs_spread(rng):
    return full(rng, wide(rng, N, 128, 4 * C, cols=6), layers(rng))
def check_inputs(d):
    b = []
    for k in ("x", "v"):
        a = np.abs(d[k].astype(np.float32))
        if not (np.isfinite(a).all() and ((a == 0) | (a >= 2.0 ** -30) & (a <= 2.0 ** 30)).all()): b.append("a value of " + k)
    none, least, most = [emit(mx_ref.quantize(np.full((128, 16), k, np.float32).astype(BF)))[1][0, 0] for k in (0.0, 2.0 ** -30, 2.0 ** 30)]
    for r in range(N):
        if ((d["wc"][r] == 0x7F) | (d["wc"][r] == 0xFF)).any(): b.append("wc: a code that is no number")
        s = mx_ref.live(d["ws"][r])
        if ((s != none) & ((s < least) | (s > most))).any(): b.append("ws: a scale out of range")
    return b
def reference(x, v, wc, ws):
    lay = [pk(wc[r], ws[r]) for r in range(N)]
    now = [x[r] for r in range(N)]
    for t in range(R):
        q = [mx_ref.quantize(now[r]) for r in range(N)]
        named, back = [], []
        for r in range(N):
            win = join(q[r], pick(q[(r + 1 + t) % N], np.arange(0, C, 2)))
            s = np.concatenate([mx_ref.matmul(pick(q[r], REFS[i:i + 128]), win) for i in range(0, len(REFS), 128)])[:K] + np.float32(0.0)
            s[np.arange(K), ODD] = -np.inf
            m = np.ascontiguousarray(np.argsort(-s, axis=1, kind="stable")[:, :8].T)
            z = mx_ref.quantize(gcols(decode(win).astype(BF), m))
            h = tile([mx_ref.matmul(pick(lay[r], np.arange(128 * b, 128 * b + 128)), z) * np.float32(0.03125) for b in range(4)])
            named.append(m)
            back.append(mx_ref.quantize(h))
        for r in range(N):
            e = (r - 1 - t) % N
            n = np.full((8, C), -1)
            for k in range(K - 1, -1, -1):
                m = named[e][:, k]
                g = np.nonzero(m >= C)[0]
                n[g, 2 * (m[g] - C)] = K + k
            for k in range(K - 1, -1, -1):
                m = named[r][:, k]
                g = np.nonzero(m < C)[0]
                n[g, m[g]] = k
            a = gcols(decode(join(back[r], back[e])).astype(BF), n)
            now[r] = (decode(q[r]) + a.astype(np.float32)).astype(BF)
    y, op = np.zeros((N, 128, C), np.float32), np.zeros((N, 8, K), np.float32)
    oc, osc = np.zeros((N, 128, 4 * C), np.uint8), np.zeros((N, 16, C), np.uint8)
    for r in range(N):
        last = mx_ref.quantize(now[r])
        y[r] = mx_ref.matmul(mx_ref.quantize(v[r]), last)
        op[r] = named[r]
        oc[r], osc[r] = emit(last)
    return {"y": y, "op": op, "oc": oc, "osc": osc}

@@ -1,0 +1,436 @@
+from concourse.mybir import dt, AluOpType, ActivationFunctionType
+
+ALU = AluOpType
+ACT = ActivationFunctionType
+C, K, PL, R = 320, 160, 480, 3
+BIG = 1e29
+KB = 100.0
+W1, W2, W3, WK, WD = 484, 84, 196, 124, 36
+LAND = 416
+EW = 352
+OWN = 176
+X4, U8, BF, F32, F16, I32, U16 = "float8_e4m3fn_x4", "uint8", "bfloat16", "float32", "float16", "int32", "uint16"
+
+
+def _sb(n, d):
+    return ("sbuf", [128, n], d)
+
+
+SCRATCH = {
+    "xin": _sb(4 * C, BF), "xt": _sb(4 * LAND, BF), "xf": _sb(4 * C, BF), "vin": _sb(512, BF), "zer": _sb(512, BF),
+    "lc": _sb(512, X4), "ls": _sb(512, U8), "vc": _sb(128, X4), "vs": _sb(128, U8),
+    "et": _sb(2048, BF), "ec": _sb(512, X4), "es": _sb(512, U8), "one": _sb(128, BF), "idn": _sb(128, BF),
+    "fc": _sb(C, X4), "fs": _sb(C, U8), "ysb": _sb(C, F32),
+    "s1": _sb(PL, F32), "s2": _sb(120, F32), "m1": _sb(8 * W1, F32), "m2": _sb(8 * W2, F32), "cv": _sb(192, F32), "md": _sb(8 * W3, F32),
+    "big": _sb(192, F32), "mk1": _sb(K, F32), "mk2": _sb(80, F32), "neg": _sb(240, F16), "neg32": _sb(32, F32),
+    "e1": _sb(5 * PL, F16), "e2": _sb(600, F16), "k1": _sb(5 * PL, F16), "k2": _sb(600, F16), "rs5": _sb(600, F16),
+    "n1": _sb(8 * W1, F16), "n2": _sb(8 * WK, F16), "b2": _sb(32, F32), "bb": _sb(32 + 8 * WD, F32),
+    "in1": _sb(64, F32), "out1": _sb(64, F32), "o32": _sb(64, F32), "lw0": _sb(16, I32), "lwi": _sb(16, I32), "lwu": _sb(16, U16),
+    "vp": _sb(4 * PL, BF), "zt": _sb(4 * K, BF), "zc": _sb(K, X4), "zs": _sb(K, U8), "ht": _sb(4 * K, BF), "est": _sb(4 * EW, BF),
+    "idt": _sb(512, F32), "jt": _sb(PL, F32), "tm": _sb(PL, BF), "p64": _sb(64, F32), "pen": _sb(C, BF), "sval": _sb(K, BF),
+    "lb": _sb(K, F32), "x1": _sb(C, F32), "ne": _sb(C, BF), "kp": _sb(C, BF), "rs16": _sb(K, BF),
+    "uu": _sb(16, F32), "ku": _sb(16, F32), "dm": _sb(16, F32), "so": _sb(16, U16), "val": _sb(K, BF), "sw": _sb(512, BF), "ns": _sb(PL, BF),
+    "ff": _sb(16, F32), "oo": _sb(16, F32), "em": _sb(16, F32), "offe": _sb(16, U16), "offo": _sb(16, U16),
+    "pi": _sb(8, I32), "pf": _sb(20, F32), "sxi": _sb(20, F32), "syi": _sb(20, F32),
+    "selq": _sb(4, U16), "sely": _sb(20, U16), "selx": _sb(20, U16),
+    "opi": _sb(64, I32), "opj": _sb(64, I32), "opf": _sb(64, F32),
+    "ps": ("psum", [128, 4096], F32),
+}
+for _t in range(R):
+    SCRATCH["wc%d" % _t] = _sb(LAND + K, X4)
+    SCRATCH["ws%d" % _t] = _sb(LAND + K, U8)
+    SCRATCH["hc%d" % _t] = _sb(C, X4)
+    SCRATCH["hs%d" % _t] = _sb(C, U8)
+    SCRATCH["gs%d" % _t] = _sb(16, F32)
+    SCRATCH["gl%d" % _t] = _sb(16, F32)
+
+POOL = {"V": 48, "S": 32, "P": 24, "G": 12}
+DMAS = ["dx", "dl", "dls", "dv", "dop", "doc", "dos", "dy"]
+SEMAPHORES = ["%s%d" % (e.lower(), i) for e in POOL for i in range(POOL[e])] + DMAS + ["sent"] + \
+             ["%s%d" % (k, t) for k in ("at", "ah", "ag") for t in range(R)]
+
+
+def rank_program(g, core, T, topo):
+    rank = T.rank_of(core)
+    if rank is None:
+        return
+    n = len(T.cores)
+    Q = {"V": g.vector, "S": g.scalar, "P": g.tensor, "G": g, "Y": g.sync}
+    ops = []
+    known = {e: 0 for e in Q}
+    wr, rd = {}, {}
+    count, last, waited = {}, {}, {}
+
+    def wait(e, j):
+        if not known[e] >> j & 1:
+            s, c, k = ops[j]
+            Q[e].wait_ge(T.sem[s], c)
+            waited[s] = max(waited.get(s, 0), c)
+            known[e] |= k
+
+    def needs(e, r, w):
+        d = set()
+        for t in r:
+            if t in wr: d.add(wr[t])
+            if t.startswith("ps"): d.update(j for (q, j) in rd.get(t, []) if q != e)
+        for t in w:
+            if t in wr: d.add(wr[t])
+            d.update(j for (q, j) in rd.get(t, []))
+        for j in sorted(d, reverse=True): wait(e, j)
+
+    def note(e, s, c, r, w):
+        j = len(ops)
+        ops.append((s, c, known[e] | 1 << j if e else 1 << j))
+        count[s], last[s] = c, j
+        for t in r: rd.setdefault(t, []).append((e, j))
+        for t in w:
+            wr[t] = j
+            rd[t] = []
+
+    def op(e, fn, r=(), w=()):
+        needs(e, r, w)
+        pool = ["%s%d" % (e.lower(), i) for i in range(POOL[e])]
+        free = [s for s in pool if s in last and known[e] >> last[s] & 1] or [s for s in pool if s not in last]
+        if not free:
+            free = [min(pool, key=lambda s: last[s])]
+            wait(e, last[free[0]])
+        s = free[0]
+        fn().then_inc(T.sem[s], 1)
+        note(e, s, count.get(s, 0) + 1, r, w)
+
+    def dma(e, s, pairs, r=(), w=()):
+        needs(e, r, w)
+        for o, i in pairs: Q[e].dma_start(o, i).then_inc(T.sem[s], 16)
+        note(e, s, count.get(s, 0) + 16 * len(pairs), r, w)
+
+    def send(dst, s, pairs, r):
+        needs("G", r, ())
+        rid, pid, _ = topo.addr(dst)
+        for o, i in pairs:
+            g.remote_dma(o, i, T.sem[s], T.sem.sent, pid, rid, topo.mask(core, dst))
+            count["sent"] = count.get("sent", 0) + len(topo.engines(core, dst))
+
+    def arrives(src, s, calls, w):
+        note(None, s, calls * len(topo.engines(src, core)), (), w)
+
+    V, S = g.vector, g.scalar
+
+    def copy(e, o, i, r, w):
+        if e == "V": op("V", lambda: V.tensor_copy(o, i), r, w)
+        else: op("S", lambda: S.activation(o, i, ACT.Copy), r, w)
+
+    def ts(o, i, a, o0, b=None, o1=None, r=(), w=()):
+        if o1 is None: op("V", lambda: V.tensor_scalar(o, i, a, None, o0), r, w)
+        else: op("V", lambda: V.tensor_scalar(o, i, a, b, o0, o1), r, w)
+
+    def tt(o, a, b, o0, r, w):
+        op("V", lambda: V.tensor_tensor(o, a, b, o0), r, w)
+
+    def scan(o, a, b, init, o0, o1, r, w):
+        op("V", lambda: V.tensor_tensor_scan(o, a, b, init, o0, o1), r, w)
+
+    def fill(o, c, w):
+        op("V", lambda: V.memset(o, c), (), w)
+
+    def act(o, i, func, scale, bias, r, w):
+        op("S", lambda: S.activation(o, i, func, bias=bias, scale=scale), r, w)
+
+    def affine(o, i, scale, bias, r, w):
+        act(o, i, ACT.Identity, scale, bias, r, w)
+
+    def sign(o, i, v, r, w):
+        act(o, i, ACT.Sign, -1.0, v, r, w)
+
+    def quant(c, s, a, b, i, r, w):
+        op("V", lambda: V.quantize_mx(c[:, a:b], s[:, a:b], i), r, w)
+
+    def mm(bank, lc, ls, a, rc, rs, b, m, r):
+        op("P", lambda: g.tensor.matmul_mx(T.ps[:, 512 * bank:512 * bank + m], lc[:, a:a + 128], ls[:, a:a + 128],
+                                           rc[:, b:b + m], rs[:, b:b + m], True, True), r, ["ps%d" % bank])
+
+    def ps(bank, a, b, p=0, q=128):
+        return T.ps[p:q, 512 * bank + a:512 * bank + b]
+
+    def iota(o, pat, base, cm, w, flag=True):
+        if flag: op("G", lambda: g.iota(o, pat, base, cm, allow_small_or_imprecise_dtypes=True), (), w)
+        else: op("G", lambda: g.iota(o, pat, base, cm), (), w)
+
+    def spread(src, r, buf, tok, engines):
+        steps = [lambda: copy(engines[0], buf[:, 0:8], src(0, 128), r, [tok + "a"])]
+        for q in range(4):
+            steps.append(lambda q=q: copy(engines[1 + q], buf[32 * q:32 * q + 32, 8:16], src(32 * (q ^ 1), 32 * (q ^ 1) + 32), r, [tok + "b%d" % q]))
+        for h in range(2):
+            o = 1 - h
+            steps.append(lambda h=h, o=o: copy(engines[5 + h], buf[64 * h:64 * h + 64, 16:32], buf[64 * o:64 * o + 64, 0:16],
+                                               [tok + "a", tok + "b%d" % (2 * o), tok + "b%d" % (2 * o + 1)], [tok + "c%d" % h]))
+        return steps, [tok + "a", tok + "c0", tok + "c1"] + [tok + "b%d" % q for q in range(4)]
+
+    def level(buf, width, k, a, m, data, first, lo, ops2, r, tok, c):
+        o = k * width
+        prev = first if k == 0 else buf[:, o - width + a:o - width + a + m]
+        init = lo if a == 0 else buf[:, o + a:o + a + 1]
+        rr = list(r) + ["cst"]
+        if k: rr += [tok % (k - 1, c)] + ([tok % (k - 1, c - 1)] if a else [])
+        if a: rr.append(tok % (k, c - 1))
+        scan(buf[:, o + a + 1:o + a + 1 + m], data, prev, init, ops2[0], ops2[1], rr, [tok % (k, c)])
+
+    def weave(*chains):
+        for i in range(max(len(c) for c in chains)):
+            for c in chains:
+                if i < len(c) and c[i]: c[i]()
+
+    UP, DOWN = (ALU.max, ALU.min), (ALU.min, ALU.max)
+    wcs = [(T["wc%d" % t], T["ws%d" % t]) for t in range(R)]
+    hcs = [(T["hc%d" % t], T["hs%d" % t]) for t in range(R)]
+    four = range(4)
+    pf = lambda c: T.pf[:, c:c + 1]
+    j, qq = pf(1), pf(6)
+
+    dma("Y", "dx", [(T.xin[:], T.x[:])], (), ["xin"])
+    iota(T.pi[:, 0:1], [[0, 1]], 0, 1, ["pi0"], False)
+    fill(T.one[:], 1.0, ["one"])
+    fill(T.big[:], BIG, ["big"])
+    op("G", lambda: g.affine_select(T.idn[:], T.one[:], [[-1, 128]], ALU.is_equal, 0.0, 0, 1), ["one"], ["idn"])
+    op("G", lambda: g.affine_select(T.mk1[:], T.big[:, 0:K], [[-1, K]], ALU.not_equal, -BIG, 0, 1), ["big"], ["mk1"])
+    iota(T.idt[:], [[1, 512]], 0, 0, ["idt"])
+    fill(T.et[:], 0.0, ["et"])
+    for b in four:
+        op("S", lambda b=b: S.activation(T.et[:, 513 * b:512 * (b + 1):4], T.idn[:], ACT.Copy), ["idn", "et"], ["et%d" % b])
+    for c, (sh, m) in enumerate([(0, 15), (0, 1), (1, 1), (5, 1), (6, 1), (5, 3), (1, 7)]):
+        ts(T.pi[:, c + 1:c + 2], T.pi[:, 0:1], sh, ALU.logical_shift_right, m, ALU.bitwise_and, ["pi0"], ["pi%d" % (c + 1)])
+    fill(T.m1[:, 0::W1], -BIG, ["c0"])
+    copy("V", T.pf[:, 0:8], T.pi[:, 0:8], ["pi%d" % c for c in range(8)], ["pf"])
+    fill(T.m2[:, 0::W2], -BIG, ["c1"])
+    tt(T.pf[:, 8:10], T.pf[:, 2:4], T.pf[:, 4:6], ALU.not_equal, ["pf"], ["pf8"])
+    fill(T.md[:, 0::W3], -BIG, ["c2"])
+    ts(pf(10), pf(9), 2.0, ALU.mult, pf(8), ALU.add, ["pf8"], ["pf10"])
+    fill(T.mk2[:], BIG, ["mk2"])
+    ts(pf(10), pf(10), 4.0, ALU.mult, qq, ALU.add, ["pf10"], ["pf10"])
+    op("V", lambda: V.memset(T.neg32[:], -KB), ["c0", "c1", "c2", "big"], ["cst"])
+    copy("V", T.mk2[96:128, 48:80], T.mk1[0:32, 0:32], ["mk1"], ["mk2"])
+    needs("Y", ["xin"], ())
+    dma("Y", "dl", [(T.lc[:].bitcast(dt.uint8), T.wc[:])], (), ["lc"])
+    dma("Y", "dls", [(T.ls[:], T.ws[:])], (), ["ls"])
+    dma("Y", "dv", [(T.vin[:], T.v[:])], (), ["vin"])
+    for b in four:
+        copy("V", T.xt[:, b:4 * K:4], T.xin[:, b::8], ["xin"], ["xe%d" % b])
+        copy("S", T.xt[:, 4 * K + b:4 * C:4], T.xin[:, 4 + b::8], ["xin"], ["xo%d" % b])
+    XE, XO = ["xe%d" % b for b in four], ["xo%d" % b for b in four]
+
+    def constants_for_keys():
+        def frac(o, i, w): affine(o, i, 1.0 / 512, 33.0 / 512, ["idt"], [w])
+        frac(T.e1[:, 0:800:5], T.idt[:, 1:C:2], "f0")
+        frac(T.e1[:, 800:1600:5], T.idt[:, 0:C:2], "f1")
+        frac(T.e1[:, 1600:2400:5], T.idt[:, C:PL], "f2")
+        for q in four:
+            a = K * (q % 2) + q // 2
+            frac(T.e2[32 * q:32 * q + 32, 0:400:5], T.idt[32 * q:32 * q + 32, a:a + K - q // 2:2], "f%d" % (3 + q))
+            frac(T.e2[32 * q:32 * q + 32, 400:600:5], T.idt[32 * q:32 * q + 32, C + 40 * q:C + 40 * q + 40], "f%d" % (7 + q))
+        affine(T.n1[:, 0::W1], T.idt[:, 0:8], 0.0, KB, ["idt"], ["c3"])
+        affine(T.n2[:, 0::WK], T.idt[:, 0:8], 0.0, KB, ["idt"], ["c4"])
+        affine(T.bb[:], T.idt[:, 0:C], 0.0, KB, ["idt"], ["c5"])
+        affine(T.neg[:], T.idt[:, 0:240], 0.0, -KB, ["idt"], ["c6"])
+        fill(T.rs5[:], 1.0, ["c7"])
+        quant(T.ec, T.es, 0, 512, T.et[:], ["et%d" % b for b in four], ["ec"])
+        affine(T.rs5[:, 0::5], T.idt[:, 0:120], 0.0, 0.0, ["c3", "c4", "c5", "c6"], ["c7"])
+
+    def constants_for_lists():
+        affine(pf(10), pf(10), 2.0, 0.0, ["pf10"], ["pf10"])
+        affine(pf(11), qq, 72.0, 64.0, ["pf"], ["pf11"])
+        affine(pf(15), j, -2.0, 0.5, ["pf"], ["pf15"])
+        affine(pf(17), j, 1.0, float(PL), ["pf"], ["pf17"])
+        affine(pf(18), j, 1.0, float(PL + 16), ["pf"], ["pf18"])
+        copy("S", T.sval[:], T.idt[:, 1:K + 1], ["idt"], ["sval"])
+        affine(T.zer[:], T.idt[:], 0.0, 0.0, ["idt"], ["zer"])
+        affine(T.rs16[:], T.idt[:, 0:K], 0.0, 1.0, ["idt"], ["rs16"])
+        act(T.jt[:], T.jt[:], ACT.Abs, -1.0, j, ["pf", "jt0", "jt1"], ["jt"])
+        act(T.p64[:], T.p64[:], ACT.Sign, 1.0, pf(15), ["pf15"], ["p64"])
+        copy("S", T.est[:, 0::EW], T.zer[:, 0:4], ["zer"], ["ez"])
+        for b in four: copy("S", T.est[:, b * EW + K + 1:b * EW + OWN + 1], T.zer[:, 0:16], ["zer"], ["ez%d" % b])
+        copy("S", T.rs16[:, 0::16], T.zer[:, 0:10], ["zer"], ["rs16"])
+        affine(T.dm[:, 0:10:2], T.idt[:, 0:5], 0.0, pf(17), ["pf17"], ["dm"])
+        affine(T.dm[:, 1:10:2], T.idt[:, 0:5], 0.0, pf(18), ["pf18"], ["dm1"])
+        act(T.tm[:], T.jt[:], ACT.Relu, -1.0, 1.0, ["jt"], ["tm"])
+        for q in range(5): act(T.pen[:, 64 * q:64 * q + 64], T.p64[:], ACT.Relu, 1.0, 0.0, ["p64"], ["pen%d" % q])
+
+    def static_offsets():
+        return [lambda: ts(pf(12), j, 4.0, ALU.is_ge, r=["pf"], w=["pf12"]),
+                lambda: ts(pf(16), pf(2), -16.0, ALU.mult, pf(7), ALU.subtract, ["pf"], ["pf16"]),
+                lambda: ts(pf(13), pf(11), pf(10), ALU.subtract, pf(12), ALU.mult, ["pf10", "pf11", "pf12"], ["pf13"]),
+                lambda: ts(pf(14), pf(12), 35.0, ALU.mult, 1.0, ALU.add, ["pf12"], ["pf14"]),
+                lambda: ts(T.selq[:, 0:2], T.one[:, 0:2], pf(13), ALU.mult, pf(10), ALU.add, ["pf13"], ["selq0"]),
+                lambda: ts(pf(14), pf(14), pf(13), ALU.add, pf(10), ALU.add, ["pf13", "pf14"], ["pf14"]),
+                lambda: copy("V", T.selx[:], T.sxi[:], ["sxi"], ["selx"]),
+                lambda: ts(T.selq[:, 2:4], T.one[:, 0:2], pf(14), ALU.mult, r=["pf14", "selq0"], w=["selq"]),
+                lambda: ts(T.sely[:], T.syi[:], pf(16), ALU.add, r=["syi", "pf16"], w=["sely"])]
+
+    def lev1(k, c): level(T.m1, W1, k, K * c, K, T.s1[:, K * c:K * c + K] if c < 2 else ps(2, 0, K), T.big[:, 0:K], -BIG, UP,
+                          ["s1_%d" % c if c < 2 else "ps2"], "m1_%d_%d", c)
+
+    def odd_scores(t, between):
+        wc, ws = wcs[t]
+        for i in range(3): copy("S", T.xt[:, 4 * (C + 32 * i):4 * (C + 32 * i + 32)], T.xt[:, 4 * 288:4 * C], XO, ["xr%d" % i])
+        quant(wc, ws, K, C, T.xt[:, 4 * K:4 * C], XO, ["wo"])
+        mm(0, wc, ws, K, wc, ws, K, K, ["wo"])
+        between()
+        tt(T.s1[:, 0:K], ps(0, 0, K), T.mk1[:], ALU.min, ["ps0", "mk1"], ["s1_0"])
+        quant(wc, ws, 288, LAND, T.xt[:, 4 * 288:], XO + ["xr0", "xr1", "xr2"], ["wo"])
+
+    for t in range(R):
+        partner, giver = T.cores[(rank + 1 + t) % n], T.cores[(rank - 1 - t) % n]
+        wc, ws = wcs[t]
+        hc, hs = hcs[t]
+        gs, gl = T["gs%d" % t], T["gl%d" % t]
+        quant(wc, ws, 0, K, T.xt[:, 0:4 * K], XE, ["we"])
+        send(giver, "at%d" % t, [(wc[:, LAND:].bitcast(dt.uint8), wc[:, 0:K].bitcast(dt.uint8)), (ws[:, LAND:], ws[:, 0:K])], ["we"])
+        arrives(partner, "at%d" % t, 2, ["wl"])
+        if t == 0:
+            iota(T.jt[:, 0:C], [[0, 10], [1, 16], [0, 2]], 0, 0, ["jt0"])
+            iota(T.jt[:, C:PL], [[0, 10], [1, 16]], 0, 0, ["jt1"])
+            iota(T.p64[:], [[-1, 2], [-1, 32]], 31, 0, ["p64"])
+            iota(T.sxi[:], [[1, 10], [0, 2]], 0, 0, ["sxi"])
+            iota(T.syi[:], [[32, 5], [0, 2], [-8, 2]], 31, 0, ["syi"])
+            odd_scores(0, lambda: None)
+        mm(1, wc, ws, K, wc, ws, 0, K, ["wo", "we"])
+        mm(3, wc, ws, 288, wc, ws, 0, C, ["wo", "we"])
+        copy("S", T.s1[:, K:C], ps(1, 0, K), ["ps1"], ["s1_1"])
+        for q in range(3): copy("S", T.s2[32 * q:32 * q + 32, 0:80], ps(3, 80 * q, 80 * q + 80, 32 * q, 32 * q + 32), ["ps3"], ["s2_%d" % q])
+        S2 = ["s2_%d" % q for q in four]
+        steps, CV = spread(lambda a, b: T.m2[a:b, 80::W2], ["m2_%d_0" % k for k in range(8)], T.cv, "cv", "SSSSSSS")
+        aa = [lambda: lev1(0, 0), lambda: lev1(1, 0)]
+        for k in range(8): aa += ([lambda k=k: lev1(k + 2, 0)] if k < 6 else []) + [lambda k=k: lev1(k, 1)]
+        bo = [lambda: tt(T.s2[96:128, 0:80], ps(3, 240, C, 96, 128), T.mk2[96:128, :], ALU.min, ["ps3", "mk2"], ["s2_3"])]
+        bo += [lambda k=k: level(T.m2, W2, k, 0, 80, T.s2[:, 0:80], T.big[:, 0:80], -BIG, UP, S2, "m2_%d_%d", 0) for k in range(8)]
+        weave(aa[:14], [None] * 4 + bo)
+        if t == 0: constants_for_keys()
+        aa[14]()
+        for b in four:
+            mm(4 + b, T.ec, T.es, 128 * b, wc, ws, 0, C, ["ec", "we", "wo"])
+            for e in range(2):
+                copy("S", T.vp[:, PL * b + e:PL * b + C:2], ps(4 + b, K * e, K * e + K), ["ps%d" % (4 + b)], ["vp%d_%d" % (b, e)])
+        aa[15]()
+        for f in steps: f()
+        mm(2, wc, ws, K, wc, ws, LAND, K, ["wo", "wl"])
+        mm(0, wc, ws, 288, wc, ws, LAND, K, ["wo", "wl"])
+        mm(1, wc, ws, K, wc, ws, LAND, K, ["wo", "wl"])
+        for b in four: mm(4 + b, T.ec, T.es, 128 * b, wc, ws, LAND, K, ["ec", "wl"])
+        copy("S", T.cv[:, 32:], ps(0, 0, K), ["ps0"], ["cvp"])
+        copy("S", T.s1[:, C:PL], ps(1, 0, K), ["ps1"], ["s1_2"])
+        for q in four: copy("S", T.s2[32 * q:32 * q + 32, 80:120], T.cv[32 * q:32 * q + 32, 32 + 40 * q:72 + 40 * q], ["cvp"], ["s2p%d" % q])
+        S1 = ["s1_0", "s1_1", "s1_2"]
+        S2 = S2 + ["s2p%d" % q for q in four]
+
+        def lev2(k):
+            level(T.md, W3, k, 0, 192, T.cv[:], T.big[:], -BIG, UP, CV + ["cvp"], "md_%d_%d", 0)
+            if k % 2: sign(T.e2[:, 1 + k // 2::5], T.s2[:], T.md[:, k * W3 + 192:k * W3 + 193], S2 + ["md_%d_0" % k], ["e2_%d" % (k // 2)])
+        for k in range(8):
+            if k > 5: lev2(k)
+            lev1(k, 2)
+            if k <= 5: lev2(k)
+            v = T.m1[:, k * W1 + PL:k * W1 + PL + 1]
+            if k == 7:
+                for c in four: sign(T.e1[:, 600 * c + 4:600 * c + 600:5], T.s1[:, 120 * c:120 * c + 120], v, S1 + ["m1_7_2"], ["e1_3_%d" % c])
+            elif k % 2: sign(T.e1[:, 1 + k // 2::5], T.s1[:], v, S1 + ["m1_%d_2" % k], ["e1_%d" % (k // 2)])
+        for b in four: copy("S", T.vp[:, PL * b + C:PL * b + PL], ps(4 + b, 0, K), ["ps%d" % (4 + b)], ["vp%d_2" % b])
+        E1 = ["e1_0", "e1_1", "e1_2", "f0", "f1", "f2", "c7"]
+
+        def sum1(c): scan(T.k1[:, 300 * c:300 * c + 300], T.rs5[:, 0:300], T.e1[:, 300 * c:300 * c + 300], 0.0, ALU.mult, ALU.add,
+                          E1 + ["e1_3_%d" % (c // 2)], ["k1_%d" % c])
+
+        def key1(k, c): level(T.n1, W1, k, 240 * c, 240, T.k1[:, 1200 * c + 4:1200 * c + 1200:5], T.neg[:], KB, DOWN,
+                              ["k1_%d" % i for i in range(4 * c, 4 * c + 4)], "n1_%d_%d", c)
+
+        def merge2(k):
+            o = 32 + k * WD
+            prev = T.neg32[:] if k == 0 else T.bb[:, o - WD:o - WD + 32]
+            scan(T.bb[:, o + 1:o + 33], T.b2[:], prev, KB, ALU.min, ALU.max, B2 + ["c5"] + (["d2_%d" % (k - 1)] if k else []), ["d2_%d" % k])
+        scan(T.k2[:], T.rs5[:], T.e2[:], 0.0, ALU.mult, ALU.add, ["e2_%d" % i for i in four] + ["f%d" % i for i in range(3, 11)] + ["c7"], ["k2"])
+        steps1, B1 = spread(lambda a, b: T.n1[a:b, PL::W1], ["n1_%d_1" % k for k in range(8)] + ["c5"], T.bb, "b1", "VVSVSVS")
+        steps2, B2 = spread(lambda a, b: T.n2[a:b, 120::WK], ["n2_%d_0" % k for k in range(8)], T.b2, "b2", "SSSSSSS")
+        weave([lambda c=c: sum1(c) for c in range(8)],
+              [lambda k=k: level(T.n2, WK, k, 0, 120, T.k2[:, 4::5], T.neg[:, 0:120], KB, DOWN, ["k2"], "n2_%d_%d", 0) for k in range(8)])
+        for f in steps2: f()
+        if t == 0: constants_for_lists()
+        one = [lambda: key1(0, 0), lambda: key1(0, 1)]
+        for k in range(1, 8): one += [lambda k=k: key1(k, 0), lambda k=k: key1(k, 1)]
+        one = [one[0]] + [one[i + d] for i in range(1, 15, 2) for d in (1, 0)] + [one[15]]
+        weave(one, [None] * 7 + [lambda k=k: merge2(k) for k in range(8)], [None] * 6 + static_offsets() if t == 0 else [])
+        for f in steps1: f()
+        ts(T.in1[:], T.bb[:].indirect(T.selq[:]), 512.0, ALU.mult, 2015.0, ALU.add, B1 + ["d2_%d" % k for k in range(8)] + ["selq"], ["in1"])
+        op("V", lambda: V.transpose(T.out1[:], T.in1[:]), ["in1"], ["out1"])
+        for e in range(2):
+            op("V", lambda e=e: V.transpose(T.o32[:, e::2], T.out1[:, e::2]), ["out1"], ["o32_%d" % e])
+        copy("V", T.lw0[:], T.o32[:, 0:16], ["o32_0", "o32_1"], ["lw0"])
+        ts(T.lwi[:], T.lw0[:], 511, ALU.bitwise_and, r=["lw0"], w=["lwi"])
+        copy("V", T.lwu[:], T.lwi[:], ["lwi"], ["lwu"])
+        lw = T.lwu[:, 0:10]
+        for b in (0, 2, 1, 3):
+            copy("VVSS"[b], T.zt[:, b::4], T.vp[:, PL * b:PL * b + PL].indirect(lw), ["lwu"] + ["vp%d_%d" % (b, i) for i in range(3)], ["zt%d" % b])
+        quant(T.zc, T.zs, 0, K, T.zt[:], ["zt%d" % b for b in four], ["zc"])
+        copy("S", T.lb[:], T.idt[:].indirect(lw), ["lwu", "idt"], ["lb"])
+        copy("S", T.x1[:], T.lb[:].indirect(T.sely[:]), ["lb", "sely"], ["x1"])
+        for b in (0, 1, 3, 2): mm(4 + b, T.lc, T.ls, 128 * b, T.zc, T.zs, 0, K, ["lc", "ls", "zc"])
+        tt(T.val[:], T.tm[:].indirect(lw), T.sval[:], ALU.mult, ["lwu", "tm", "sval"], ["val"])
+        for b in (0, 1, 3, 2):
+            if b < 3: ts(T.ht[:, b::4], ps(4 + b, 0, K), 0.03125, ALU.mult, r=["ps%d" % (4 + b)], w=["ht%d" % b])
+            else: op("S", lambda b=b: S.activation(T.ht[:, b::4], ps(4 + b, 0, K), ACT.Copy, scale=0.03125), ["ps%d" % (4 + b)], ["ht%d" % b])
+        copy("S", T.sw[:], T.zer[:], ["zer"], ["sw"])
+        tt(T.uu[:, 0:10], T.lwi[:, 0:10], T.dm[:, 0:10], ALU.subtract, ["lwi", "dm", "dm1"], ["uu"])
+        quant(hc, hs, 0, K, T.ht[:], ["ht%d" % b for b in four], ["ho"])
+        send(partner, "ah%d" % t, [(hc[:, K:C].bitcast(dt.uint8), hc[:, 0:K].bitcast(dt.uint8)), (hs[:, K:C], hs[:, 0:K])], ["ho"])
+        arrives(giver, "ah%d" % t, 2, ["hl"])
+        for b in four:
+            mm(4 + b, T.ec, T.es, 128 * b, hc, hs, 0, K, ["ec", "ho"])
+            copy("S", T.est[:, EW * b + OWN + 1:EW * b + OWN + 1 + K], ps(4 + b, 0, K), ["ps%d" % (4 + b)], ["eo%d" % b])
+        tt(T.ne[:], T.lwi[:].indirect(T.selx[:]), T.x1[:], ALU.not_equal, ["lwi", "selx", "x1"], ["ne"])
+        scan(T.kp[:], T.ne[:], T.pen[:], 0.0, ALU.mult, ALU.max, ["ne"] + ["pen%d" % q for q in range(5)], ["kp"])
+        tt(T.ku[:, 0:10], T.kp[:, 31::32], T.uu[:, 0:10], ALU.mult, ["kp", "uu"], ["ku"])
+        for e in range(2):
+            ts(T.so[:, e:10:2], T.ku[:, e:10:2], T.dm[:, e:e + 1], ALU.add, r=["ku", "dm", "dm1"], w=["so%d" % e])
+        for q in range(4, -1, -1):
+            copy("V", T.sw[:].indirect(T.so[:, 2 * q:2 * q + 2]), T.val[:, 32 * q:32 * q + 32], ["so0", "so1", "val"], ["sw"])
+        scan(T.ns[:, C:PL], T.rs16[:], T.sw[:, C:PL], 0.0, ALU.mult, ALU.add, ["sw", "rs16"], ["ns2"])
+        scan(T.ns[:, K:C], T.rs16[:], T.sw[:, 1:C:2], 0.0, ALU.mult, ALU.add, ["sw", "rs16"], ["ns1"])
+        copy("V", gs[:, 0:10], T.ns[:, C + 15::16], ["ns2"], ["gs"])
+        send(partner, "ag%d" % t, [(gl[:, 0:10], gs[:, 0:10])], ["gs"])
+        arrives(giver, "ag%d" % t, 1, ["gl"])
+        copy("V", T.offo[:, 0:10], T.ns[:, K + 15:C:16], ["ns1"], ["offo"])
+        scan(T.ns[:, 0:K], T.rs16[:], T.sw[:, 0:C:2], 0.0, ALU.mult, ALU.add, ["sw", "rs16"], ["ns0"])
+        final = t == R - 1
+        for b in four:
+            mm(b, T.ec, T.es, 128 * b, hc, hs, K, K, ["ec", "hl"])
+            copy("S", T.est[:, EW * b + 1:EW * b + 1 + K], ps(b, 0, K), ["ps%d" % b], ["eg%d" % b])
+        for b in four:
+            o = T.xf[:, 4 + b::8] if final else T.xt[:, 4 * K + b:4 * C:4]
+            tt(o, T.est[:, EW * b + OWN:EW * b + OWN + 1 + K].indirect(T.offo[:, 0:10]), T.vp[:, PL * b + 1:PL * b + C:2], ALU.add,
+               ["offo", "eo%d" % b, "ez%d" % b, "vp%d_1" % b], ["yo%d" % b if final else "xo%d" % b])
+            if b == 2: ts(T.ff[:, 0:10], T.ns[:, 15:K:16], 0.0, ALU.is_gt, float(OWN), ALU.mult, ["ns0"], ["ff"])
+
+        def own_first(): tt(T.oo[:, 0:10], T.ff[:, 0:10], T.ns[:, 15:K:16], ALU.add, ["ff", "ns0"], ["oo"])
+        if final:
+            copy("V", T.opi[:], T.out1[:], ["out1"], ["opi"])
+            own_first()
+            ts(T.opj[:], T.opi[:], 511, ALU.bitwise_and, r=["opi"], w=["opj"])
+            quant(T.vc, T.vs, 0, 128, T.vin[:], ["vin"], ["vc"])
+            copy("V", T.opf[:], T.opj[:], ["opj"], ["opf"])
+            dma("Y", "dop", [(T.op[2 * q + h, :], T.opf[32 * q:32 * q + 5, 32 * h:32 * h + 32]) for q in four for h in range(2)], ["opf"])
+        else:
+            odd_scores(t + 1, own_first)
+        tt(T.em[:, 0:10], T.oo[:, 0:10], gl[:, 0:10], ALU.max, ["oo", "gl"], ["em"])
+        copy("V", T.offe[:, 0:10], T.em[:, 0:10], ["em"], ["offe"])
+        for b in four:
+            o = T.xf[:, b::8] if final else T.xt[:, b:4 * K:4]
+            tt(o, T.est[:, EW * b:EW * b + OWN + 1 + K].indirect(T.offe[:, 0:10]), T.vp[:, PL * b:PL * b + C:2], ALU.add,
+               ["offe", "eo%d" % b, "eg%d" % b, "ez", "ez%d" % b, "vp%d_0" % b], ["ye%d" % b if final else "xe%d" % b])
+
+    quant(T.fc, T.fs, 0, C, T.xf[:], ["ye%d" % b for b in four] + ["yo%d" % b for b in four], ["fc"])
+    for h in range(2): mm(h, T.vc, T.vs, 0, T.fc, T.fs, K * h, K, ["vc", "fc"])
+    dma("Y", "doc", [(T.oc[:], T.fc[:].bitcast(dt.uint8))], ["fc"])
+    dma("S", "dos", [(T.osc[4 * q:4 * q + 4, :], T.fs[32 * q:32 * q + 4, :]) for q in range(2)], ["fc"])
+    for h in range(2): copy("VS"[h], T.ysb[:, K * h:K * h + K], ps(h, 0, K), ["ps%d" % h], ["ysb%d" % h])
+    dma("Y", "dy", [(T.y[:], T.ysb[:])], ["ysb0", "ysb1"])
+    dma("S", "dos", [(T.osc[4 * q:4 * q + 4, :], T.fs[32 * q:32 * q + 4, :]) for q in range(2, 4)], ["fc"])
+    for s in sorted(count, key=lambda s: s in DMAS):
+        if waited.get(s, 0) < count[s]:
+            e = s[0].upper() if s not in DMAS and s[0].upper() in POOL and s != "sent" else "G"
+            Q[e].wait_ge(T.sem[s], count[s])

@@ -10,40 +10,20 @@ LAND = 416
 EW = 352
 OWN = 176
 X4, U8, BF, F32, F16, I32, U16 = "float8_e4m3fn_x4", "uint8", "bfloat16", "float32", "float16", "int32", "uint16"
-
-
-def _sb(n, d):
-    return ("sbuf", [128, n], d)
-
-
-SCRATCH = {
-    "xin": _sb(4 * C, BF), "xt": _sb(4 * LAND, BF), "xf": _sb(4 * C, BF), "vin": _sb(512, BF), "zer": _sb(512, BF),
-    "lc": _sb(512, X4), "ls": _sb(512, U8), "vc": _sb(128, X4), "vs": _sb(128, U8),
-    "et": _sb(2048, BF), "ec": _sb(512, X4), "es": _sb(512, U8), "one": _sb(128, BF), "idn": _sb(128, BF),
-    "fc": _sb(C, X4), "fs": _sb(C, U8), "ysb": _sb(C, F32),
-    "s1": _sb(PL, F32), "s2": _sb(120, F32), "m1": _sb(8 * W1, F32), "m2": _sb(8 * W2, F32), "cv": _sb(192, F32), "md": _sb(8 * W3, F32),
-    "big": _sb(192, F32), "mk1": _sb(K, F32), "mk2": _sb(80, F32), "neg": _sb(240, F16), "neg32": _sb(32, F32),
-    "e1": _sb(5 * PL, F16), "e2": _sb(600, F16), "k1": _sb(5 * PL, F16), "k2": _sb(600, F16), "rs5": _sb(600, F16),
-    "n1": _sb(8 * W1, F16), "n2": _sb(8 * WK, F16), "b2": _sb(32, F32), "bb": _sb(32 + 8 * WD, F32),
-    "in1": _sb(64, F32), "out1": _sb(64, F32), "o32": _sb(64, F32), "lw0": _sb(16, I32), "lwi": _sb(16, I32), "lwu": _sb(16, U16),
-    "vp": _sb(4 * PL, BF), "zt": _sb(4 * K, BF), "zc": _sb(K, X4), "zs": _sb(K, U8), "ht": _sb(4 * K, BF), "est": _sb(4 * EW, BF),
-    "idt": _sb(512, F32), "jt": _sb(PL, F32), "tm": _sb(PL, BF), "p64": _sb(64, F32), "pen": _sb(C, BF), "sval": _sb(K, BF),
-    "lb": _sb(K, F32), "x1": _sb(C, F32), "ne": _sb(C, BF), "kp": _sb(C, BF), "rs16": _sb(K, BF),
-    "uu": _sb(16, F32), "ku": _sb(16, F32), "dm": _sb(16, F32), "so": _sb(16, U16), "val": _sb(K, BF), "sw": _sb(512, BF), "ns": _sb(PL, BF),
-    "ff": _sb(16, F32), "oo": _sb(16, F32), "em": _sb(16, F32), "offe": _sb(16, U16), "offo": _sb(16, U16),
-    "pi": _sb(8, I32), "pf": _sb(20, F32), "sxi": _sb(20, F32), "syi": _sb(20, F32),
-    "selq": _sb(4, U16), "sely": _sb(20, U16), "selx": _sb(20, U16),
-    "opi": _sb(64, I32), "opj": _sb(64, I32), "opf": _sb(64, F32),
-    "ps": ("psum", [128, 4096], F32),
-}
-for _t in range(R):
-    SCRATCH["wc%d" % _t] = _sb(LAND + K, X4)
-    SCRATCH["ws%d" % _t] = _sb(LAND + K, U8)
-    SCRATCH["hc%d" % _t] = _sb(C, X4)
-    SCRATCH["hs%d" % _t] = _sb(C, U8)
-    SCRATCH["gs%d" % _t] = _sb(16, F32)
-    SCRATCH["gl%d" % _t] = _sb(16, F32)
-
+SCRATCH = {"ps": ("psum", [128, 4096], F32)}
+for _d, _l in {
+    BF: dict(xin=1280, xt=4 * LAND, xf=1280, vin=512, zer=512, et=2048, one=128, idn=128, vp=4 * PL, zt=640, ht=640, est=4 * EW, tm=PL, pen=C,
+             sval=K, ne=C, kp=C, rs16=K, rs32=C, val=K, sw=1024, ns=2 * PL),
+    X4: dict(lc=512, vc=128, ec=512, fc=C, zc=K, wc0=576, wc1=576, wc2=576, hc0=C, hc1=C, hc2=C),
+    U8: dict(ls=512, vs=128, es=512, fs=C, zs=K, ws0=576, ws1=576, ws2=576, hs0=C, hs1=C, hs2=C),
+    F32: dict(ysb=C, s1=PL, s2=120, m1=8 * W1, m2=8 * W2, cv=192, md=8 * W3, big=192, mk1=K, mk2=80, neg32=32, b2=32, bb=32 + 8 * WD, in1=64,
+              out1=64, o32=64, idt=512, jt=PL, p64=C, x1=C, uu=16, ku=16, dm=16, nn=20, ff=16, oo=16, em=16, pf=20, sxi=20, opf=64,
+              gs0=16, gs1=16, gs2=16, gl0=16, gl1=16, gl2=16),
+    F16: dict(neg=240, e1=5 * PL, e2=600, k1=5 * PL, k2=600, rs5=600, n1=8 * W1, n2=8 * WK),
+    I32: dict(lw0=16, lwi=16, pi=8, opi=64, opj=64),
+    U16: dict(lwu=16, so=16, offe=16, offo=16, selq=4, selx=20),
+}.items():
+    for _k, _n in _l.items(): SCRATCH[_k] = ("sbuf", [128, _n], _d)
 POOL = {"V": 48, "S": 32, "P": 24, "G": 12}
 DMAS = ["dx", "dl", "dls", "dv", "dop", "doc", "dos", "dy"]
 SEMAPHORES = ["%s%d" % (e.lower(), i) for e in POOL for i in range(POOL[e])] + DMAS + ["sent"] + \
@@ -110,9 +90,7 @@ def rank_program(g, core, T, topo):
             g.remote_dma(o, i, T.sem[s], T.sem.sent, pid, rid, topo.mask(core, dst))
             count["sent"] = count.get("sent", 0) + len(topo.engines(core, dst))
 
-    def arrives(src, s, calls, w):
-        note(None, s, calls * len(topo.engines(src, core)), (), w)
-
+    def arrives(src, s, calls, w): note(None, s, calls * len(topo.engines(src, core)), (), w)
     V, S = g.vector, g.scalar
 
     def copy(e, o, i, r, w):
@@ -123,33 +101,19 @@ def rank_program(g, core, T, topo):
         if o1 is None: op("V", lambda: V.tensor_scalar(o, i, a, None, o0), r, w)
         else: op("V", lambda: V.tensor_scalar(o, i, a, b, o0, o1), r, w)
 
-    def tt(o, a, b, o0, r, w):
-        op("V", lambda: V.tensor_tensor(o, a, b, o0), r, w)
-
-    def scan(o, a, b, init, o0, o1, r, w):
-        op("V", lambda: V.tensor_tensor_scan(o, a, b, init, o0, o1), r, w)
-
-    def fill(o, c, w):
-        op("V", lambda: V.memset(o, c), (), w)
-
-    def act(o, i, func, scale, bias, r, w):
-        op("S", lambda: S.activation(o, i, func, bias=bias, scale=scale), r, w)
-
-    def affine(o, i, scale, bias, r, w):
-        act(o, i, ACT.Identity, scale, bias, r, w)
-
-    def sign(o, i, v, r, w):
-        act(o, i, ACT.Sign, -1.0, v, r, w)
-
-    def quant(c, s, a, b, i, r, w):
-        op("V", lambda: V.quantize_mx(c[:, a:b], s[:, a:b], i), r, w)
+    def tt(o, a, b, o0, r, w): op("V", lambda: V.tensor_tensor(o, a, b, o0), r, w)
+    def scan(o, a, b, init, o0, o1, r, w): op("V", lambda: V.tensor_tensor_scan(o, a, b, init, o0, o1), r, w)
+    def fill(o, c, w): op("V", lambda: V.memset(o, c), (), w)
+    def act(o, i, func, scale, bias, r, w): op("S", lambda: S.activation(o, i, func, bias=bias, scale=scale), r, w)
+    def affine(o, i, scale, bias, r, w): act(o, i, ACT.Identity, scale, bias, r, w)
+    def sign(o, i, v, r, w): act(o, i, ACT.Sign, -1.0, v, r, w)
+    def quant(c, s, a, b, i, r, w): op("V", lambda: V.quantize_mx(c[:, a:b], s[:, a:b], i), r, w)
 
     def mm(bank, lc, ls, a, rc, rs, b, m, r):
         op("P", lambda: g.tensor.matmul_mx(T.ps[:, 512 * bank:512 * bank + m], lc[:, a:a + 128], ls[:, a:a + 128],
                                            rc[:, b:b + m], rs[:, b:b + m], True, True), r, ["ps%d" % bank])
 
-    def ps(bank, a, b, p=0, q=128):
-        return T.ps[p:q, 512 * bank + a:512 * bank + b]
+    def ps(bank, a, b, p=0, q=128): return T.ps[p:q, 512 * bank + a:512 * bank + b]
 
     def iota(o, pat, base, cm, w, flag=True):
         if flag: op("G", lambda: g.iota(o, pat, base, cm, allow_small_or_imprecise_dtypes=True), (), w)
@@ -196,10 +160,10 @@ def rank_program(g, core, T, topo):
     fill(T.et[:], 0.0, ["et"])
     for b in four:
         op("S", lambda b=b: S.activation(T.et[:, 513 * b:512 * (b + 1):4], T.idn[:], ACT.Copy), ["idn", "et"], ["et%d" % b])
-    for c, (sh, m) in enumerate([(0, 15), (0, 1), (1, 1), (5, 1), (6, 1), (5, 3), (1, 7)]):
+    for c, (sh, m) in enumerate([(0, 15), (0, 1), (1, 1), (5, 1), (6, 1), (5, 3)]):
         ts(T.pi[:, c + 1:c + 2], T.pi[:, 0:1], sh, ALU.logical_shift_right, m, ALU.bitwise_and, ["pi0"], ["pi%d" % (c + 1)])
     fill(T.m1[:, 0::W1], -BIG, ["c0"])
-    copy("V", T.pf[:, 0:8], T.pi[:, 0:8], ["pi%d" % c for c in range(8)], ["pf"])
+    copy("V", T.pf[:, 0:7], T.pi[:, 0:7], ["pi%d" % c for c in range(7)], ["pf"])
     fill(T.m2[:, 0::W2], -BIG, ["c1"])
     tt(T.pf[:, 8:10], T.pf[:, 2:4], T.pf[:, 4:6], ALU.not_equal, ["pf"], ["pf8"])
     fill(T.md[:, 0::W3], -BIG, ["c2"])
@@ -212,9 +176,8 @@ def rank_program(g, core, T, topo):
     dma("Y", "dl", [(T.lc[:].bitcast(dt.uint8), T.wc[:])], (), ["lc"])
     dma("Y", "dls", [(T.ls[:], T.ws[:])], (), ["ls"])
     dma("Y", "dv", [(T.vin[:], T.v[:])], (), ["vin"])
-    for b in four:
-        copy("V", T.xt[:, b:4 * K:4], T.xin[:, b::8], ["xin"], ["xe%d" % b])
-        copy("S", T.xt[:, 4 * K + b:4 * C:4], T.xin[:, 4 + b::8], ["xin"], ["xo%d" % b])
+    for b in four: copy("VVVS"[b], T.xt[:, b:4 * K:4], T.xin[:, b::8], ["xin"], ["xe%d" % b])
+    for b in four: copy("S", T.xt[:, 4 * K + b:4 * C:4], T.xin[:, 4 + b::8], ["xin"], ["xo%d" % b])
     XE, XO = ["xe%d" % b for b in four], ["xo%d" % b for b in four]
 
     def constants_for_keys():
@@ -230,39 +193,34 @@ def rank_program(g, core, T, topo):
         affine(T.n2[:, 0::WK], T.idt[:, 0:8], 0.0, KB, ["idt"], ["c4"])
         affine(T.bb[:], T.idt[:, 0:C], 0.0, KB, ["idt"], ["c5"])
         affine(T.neg[:], T.idt[:, 0:240], 0.0, -KB, ["idt"], ["c6"])
-        fill(T.rs5[:], 1.0, ["c7"])
-        quant(T.ec, T.es, 0, 512, T.et[:], ["et%d" % b for b in four], ["ec"])
         affine(T.rs5[:, 0::5], T.idt[:, 0:120], 0.0, 0.0, ["c3", "c4", "c5", "c6"], ["c7"])
 
-    def constants_for_lists():
+    def constants_for_offsets():
         affine(pf(10), pf(10), 2.0, 0.0, ["pf10"], ["pf10"])
         affine(pf(11), qq, 72.0, 64.0, ["pf"], ["pf11"])
         affine(pf(15), j, -2.0, 0.5, ["pf"], ["pf15"])
         affine(pf(17), j, 1.0, float(PL), ["pf"], ["pf17"])
         affine(pf(18), j, 1.0, float(PL + 16), ["pf"], ["pf18"])
-        copy("S", T.sval[:], T.idt[:, 1:K + 1], ["idt"], ["sval"])
-        affine(T.zer[:], T.idt[:], 0.0, 0.0, ["idt"], ["zer"])
-        affine(T.rs16[:], T.idt[:, 0:K], 0.0, 1.0, ["idt"], ["rs16"])
+        affine(T.sval[:], T.idt[:, 0:K], -1.0, float(K), ["idt"], ["sval"])
+
+    def constants_for_lists():
         act(T.jt[:], T.jt[:], ACT.Abs, -1.0, j, ["pf", "jt0", "jt1"], ["jt"])
-        act(T.p64[:], T.p64[:], ACT.Sign, 1.0, pf(15), ["pf15"], ["p64"])
-        copy("S", T.est[:, 0::EW], T.zer[:, 0:4], ["zer"], ["ez"])
-        for b in four: copy("S", T.est[:, b * EW + K + 1:b * EW + OWN + 1], T.zer[:, 0:16], ["zer"], ["ez%d" % b])
+        act(T.p64[:], T.p64[:], ACT.Sign, 1.0, pf(15), ["pf15", "p64_0", "p64_1"], ["p64"])
         copy("S", T.rs16[:, 0::16], T.zer[:, 0:10], ["zer"], ["rs16"])
         affine(T.dm[:, 0:10:2], T.idt[:, 0:5], 0.0, pf(17), ["pf17"], ["dm"])
         affine(T.dm[:, 1:10:2], T.idt[:, 0:5], 0.0, pf(18), ["pf18"], ["dm1"])
         act(T.tm[:], T.jt[:], ACT.Relu, -1.0, 1.0, ["jt"], ["tm"])
-        for q in range(5): act(T.pen[:, 64 * q:64 * q + 64], T.p64[:], ACT.Relu, 1.0, 0.0, ["p64"], ["pen%d" % q])
+        act(T.pen[:], T.p64[:], ACT.Relu, 1000.0, 0.0, ["p64"], ["pen"])
+        copy("S", T.rs32[:, 0::32], T.one[:, 0:10], ["one"], ["rs32"])
 
     def static_offsets():
         return [lambda: ts(pf(12), j, 4.0, ALU.is_ge, r=["pf"], w=["pf12"]),
-                lambda: ts(pf(16), pf(2), -16.0, ALU.mult, pf(7), ALU.subtract, ["pf"], ["pf16"]),
                 lambda: ts(pf(13), pf(11), pf(10), ALU.subtract, pf(12), ALU.mult, ["pf10", "pf11", "pf12"], ["pf13"]),
                 lambda: ts(pf(14), pf(12), 35.0, ALU.mult, 1.0, ALU.add, ["pf12"], ["pf14"]),
                 lambda: ts(T.selq[:, 0:2], T.one[:, 0:2], pf(13), ALU.mult, pf(10), ALU.add, ["pf13"], ["selq0"]),
                 lambda: ts(pf(14), pf(14), pf(13), ALU.add, pf(10), ALU.add, ["pf13", "pf14"], ["pf14"]),
                 lambda: copy("V", T.selx[:], T.sxi[:], ["sxi"], ["selx"]),
-                lambda: ts(T.selq[:, 2:4], T.one[:, 0:2], pf(14), ALU.mult, r=["pf14", "selq0"], w=["selq"]),
-                lambda: ts(T.sely[:], T.syi[:], pf(16), ALU.add, r=["syi", "pf16"], w=["sely"])]
+                lambda: ts(T.selq[:, 2:4], T.one[:, 0:2], pf(14), ALU.mult, r=["pf14", "selq0"], w=["selq"])]
 
     def lev1(k, c): level(T.m1, W1, k, K * c, K, T.s1[:, K * c:K * c + K] if c < 2 else ps(2, 0, K), T.big[:, 0:K], -BIG, UP,
                           ["s1_%d" % c if c < 2 else "ps2"], "m1_%d_%d", c)
@@ -287,31 +245,36 @@ def rank_program(g, core, T, topo):
         if t == 0:
             iota(T.jt[:, 0:C], [[0, 10], [1, 16], [0, 2]], 0, 0, ["jt0"])
             iota(T.jt[:, C:PL], [[0, 10], [1, 16]], 0, 0, ["jt1"])
-            iota(T.p64[:], [[-1, 2], [-1, 32]], 31, 0, ["p64"])
-            iota(T.sxi[:], [[1, 10], [0, 2]], 0, 0, ["sxi"])
-            iota(T.syi[:], [[32, 5], [0, 2], [-8, 2]], 31, 0, ["syi"])
-            odd_scores(0, lambda: None)
+            for e in range(2): iota(T.p64[:, K * e:K * e + K], [[0, 5], [1, 2], [2, 16]], -e, 0, ["p64_%d" % e])
+            iota(T.sxi[:], [[1, 2], [2, 5], [0, 2]], 0, 0, ["sxi"])
+            odd_scores(0, lambda: quant(T.ec, T.es, 0, 512, T.et[:], ["et%d" % b for b in four], ["ec"]))
+            lev1(0, 0)
+            fill(T.rs5[:], 1.0, ["c7"])
         mm(1, wc, ws, K, wc, ws, 0, K, ["wo", "we"])
         mm(3, wc, ws, 288, wc, ws, 0, C, ["wo", "we"])
         copy("S", T.s1[:, K:C], ps(1, 0, K), ["ps1"], ["s1_1"])
         for q in range(3): copy("S", T.s2[32 * q:32 * q + 32, 0:80], ps(3, 80 * q, 80 * q + 80, 32 * q, 32 * q + 32), ["ps3"], ["s2_%d" % q])
         S2 = ["s2_%d" % q for q in four]
         steps, CV = spread(lambda a, b: T.m2[a:b, 80::W2], ["m2_%d_0" % k for k in range(8)], T.cv, "cv", "SSSSSSS")
-        aa = [lambda: lev1(0, 0), lambda: lev1(1, 0)]
-        for k in range(8): aa += ([lambda k=k: lev1(k + 2, 0)] if k < 6 else []) + [lambda k=k: lev1(k, 1)]
+        aa = [lambda: lev1(1, 0), lambda: lev1(2, 0)]
+        for k in range(8): aa += ([lambda k=k: lev1(k + 3, 0)] if k < 5 else []) + [lambda k=k: lev1(k, 1)]
         bo = [lambda: tt(T.s2[96:128, 0:80], ps(3, 240, C, 96, 128), T.mk2[96:128, :], ALU.min, ["ps3", "mk2"], ["s2_3"])]
         bo += [lambda k=k: level(T.m2, W2, k, 0, 80, T.s2[:, 0:80], T.big[:, 0:80], -BIG, UP, S2, "m2_%d_%d", 0) for k in range(8)]
-        weave(aa[:14], [None] * 4 + bo)
         if t == 0: constants_for_keys()
-        aa[14]()
         for b in four:
             mm(4 + b, T.ec, T.es, 128 * b, wc, ws, 0, C, ["ec", "we", "wo"])
             for e in range(2):
                 copy("S", T.vp[:, PL * b + e:PL * b + C:2], ps(4 + b, K * e, K * e + K), ["ps%d" % (4 + b)], ["vp%d_%d" % (b, e)])
-        aa[15]()
+        weave(aa, [None] * 3 + bo)
         for f in steps: f()
-        mm(2, wc, ws, K, wc, ws, LAND, K, ["wo", "wl"])
+        if t == 0:
+            fill(T.zer[:], 0.0, ["zer"])
+            fill(T.rs16[:], 1.0, ["rs16"])
+            fill(T.rs32[:], 0.0, ["rs32"])
+            fill(T.est[:, OWN + K::EW], 0.0, ["ez"])
+            for b in four: fill(T.est[:, b * EW + K:b * EW + OWN], 0.0, ["ez%d" % b])
         mm(0, wc, ws, 288, wc, ws, LAND, K, ["wo", "wl"])
+        mm(2, wc, ws, K, wc, ws, LAND, K, ["wo", "wl"])
         mm(1, wc, ws, K, wc, ws, LAND, K, ["wo", "wl"])
         for b in four: mm(4 + b, T.ec, T.es, 128 * b, wc, ws, LAND, K, ["ec", "wl"])
         copy("S", T.cv[:, 32:], ps(0, 0, K), ["ps0"], ["cvp"])
@@ -332,13 +295,14 @@ def rank_program(g, core, T, topo):
                 for c in four: sign(T.e1[:, 600 * c + 4:600 * c + 600:5], T.s1[:, 120 * c:120 * c + 120], v, S1 + ["m1_7_2"], ["e1_3_%d" % c])
             elif k % 2: sign(T.e1[:, 1 + k // 2::5], T.s1[:], v, S1 + ["m1_%d_2" % k], ["e1_%d" % (k // 2)])
         for b in four: copy("S", T.vp[:, PL * b + C:PL * b + PL], ps(4 + b, 0, K), ["ps%d" % (4 + b)], ["vp%d_2" % b])
+        if t == 0: constants_for_offsets()
         E1 = ["e1_0", "e1_1", "e1_2", "f0", "f1", "f2", "c7"]
 
-        def sum1(c): scan(T.k1[:, 300 * c:300 * c + 300], T.rs5[:, 0:300], T.e1[:, 300 * c:300 * c + 300], 0.0, ALU.mult, ALU.add,
-                          E1 + ["e1_3_%d" % (c // 2)], ["k1_%d" % c])
+        def sum1(c): scan(T.k1[:, 600 * c:600 * c + 600], T.rs5[:], T.e1[:, 600 * c:600 * c + 600], 0.0, ALU.mult, ALU.add,
+                          E1 + ["e1_3_%d" % c], ["k1_%d" % c])
 
         def key1(k, c): level(T.n1, W1, k, 240 * c, 240, T.k1[:, 1200 * c + 4:1200 * c + 1200:5], T.neg[:], KB, DOWN,
-                              ["k1_%d" % i for i in range(4 * c, 4 * c + 4)], "n1_%d_%d", c)
+                              ["k1_%d" % i for i in range(2 * c, 2 * c + 2)], "n1_%d_%d", c)
 
         def merge2(k):
             o = 32 + k * WD
@@ -347,15 +311,14 @@ def rank_program(g, core, T, topo):
         scan(T.k2[:], T.rs5[:], T.e2[:], 0.0, ALU.mult, ALU.add, ["e2_%d" % i for i in four] + ["f%d" % i for i in range(3, 11)] + ["c7"], ["k2"])
         steps1, B1 = spread(lambda a, b: T.n1[a:b, PL::W1], ["n1_%d_1" % k for k in range(8)] + ["c5"], T.bb, "b1", "VVSVSVS")
         steps2, B2 = spread(lambda a, b: T.n2[a:b, 120::WK], ["n2_%d_0" % k for k in range(8)], T.b2, "b2", "SSSSSSS")
-        weave([lambda c=c: sum1(c) for c in range(8)],
+        weave([lambda c=c: sum1(c) for c in four] + [lambda k=k: key1(k, 0) for k in four],
               [lambda k=k: level(T.n2, WK, k, 0, 120, T.k2[:, 4::5], T.neg[:, 0:120], KB, DOWN, ["k2"], "n2_%d_%d", 0) for k in range(8)])
         for f in steps2: f()
         if t == 0: constants_for_lists()
-        one = [lambda: key1(0, 0), lambda: key1(0, 1)]
-        for k in range(1, 8): one += [lambda k=k: key1(k, 0), lambda k=k: key1(k, 1)]
-        one = [one[0]] + [one[i + d] for i in range(1, 15, 2) for d in (1, 0)] + [one[15]]
-        weave(one, [None] * 7 + [lambda k=k: merge2(k) for k in range(8)], [None] * 6 + static_offsets() if t == 0 else [])
-        for f in steps1: f()
+        weave([lambda k=k: key1(k, 0) for k in range(4, 8)] + [lambda k=k: merge2(k) for k in four], [lambda k=k: key1(k, 1) for k in range(8)],
+              static_offsets() if t == 0 else [])
+        weave([lambda k=k: merge2(k) for k in range(4, 8)], steps1[0:2] + [lambda: [f() for f in steps1[2:5]], lambda: [f() for f in steps1[5:]]])
+        for h in range(2): copy("S", T.sw[:, 512 * h:512 * h + 512], T.zer[:], ["zer"], ["sw%d" % h])
         ts(T.in1[:], T.bb[:].indirect(T.selq[:]), 512.0, ALU.mult, 2015.0, ALU.add, B1 + ["d2_%d" % k for k in range(8)] + ["selq"], ["in1"])
         op("V", lambda: V.transpose(T.out1[:], T.in1[:]), ["in1"], ["out1"])
         for e in range(2):
@@ -363,50 +326,64 @@ def rank_program(g, core, T, topo):
         copy("V", T.lw0[:], T.o32[:, 0:16], ["o32_0", "o32_1"], ["lw0"])
         ts(T.lwi[:], T.lw0[:], 511, ALU.bitwise_and, r=["lw0"], w=["lwi"])
         copy("V", T.lwu[:], T.lwi[:], ["lwi"], ["lwu"])
+        tt(T.uu[:, 0:10], T.lwi[:, 0:10], T.dm[:, 0:10], ALU.subtract, ["lwi", "dm", "dm1"], ["uu"])
         lw = T.lwu[:, 0:10]
         for b in (0, 2, 1, 3):
             copy("VVSS"[b], T.zt[:, b::4], T.vp[:, PL * b:PL * b + PL].indirect(lw), ["lwu"] + ["vp%d_%d" % (b, i) for i in range(3)], ["zt%d" % b])
+
+        def listed(e): tt(T.x1[:, K * e:K * e + K], T.idt[:].indirect(lw), T.pen[:, K * e:K * e + K], ALU.add, ["lwu", "idt", "pen"], ["x1_%d" % e])
+        listed(0)
         quant(T.zc, T.zs, 0, K, T.zt[:], ["zt%d" % b for b in four], ["zc"])
-        copy("S", T.lb[:], T.idt[:].indirect(lw), ["lwu", "idt"], ["lb"])
-        copy("S", T.x1[:], T.lb[:].indirect(T.sely[:]), ["lb", "sely"], ["x1"])
-        for b in (0, 1, 3, 2): mm(4 + b, T.lc, T.ls, 128 * b, T.zc, T.zs, 0, K, ["lc", "ls", "zc"])
+        for b in four:
+            mm(4 + b, T.lc, T.ls, 128 * b, T.zc, T.zs, 0, K, ["lc", "ls", "zc"])
+            op("S", lambda b=b: S.activation(T.ht[:, b::4], ps(4 + b, 0, K), ACT.Copy, scale=0.03125), ["ps%d" % (4 + b)], ["ht%d" % b])
+        listed(1)
         tt(T.val[:], T.tm[:].indirect(lw), T.sval[:], ALU.mult, ["lwu", "tm", "sval"], ["val"])
-        for b in (0, 1, 3, 2):
-            if b < 3: ts(T.ht[:, b::4], ps(4 + b, 0, K), 0.03125, ALU.mult, r=["ps%d" % (4 + b)], w=["ht%d" % b])
-            else: op("S", lambda b=b: S.activation(T.ht[:, b::4], ps(4 + b, 0, K), ACT.Copy, scale=0.03125), ["ps%d" % (4 + b)], ["ht%d" % b])
-        copy("S", T.sw[:], T.zer[:], ["zer"], ["sw"])
-        tt(T.uu[:, 0:10], T.lwi[:, 0:10], T.dm[:, 0:10], ALU.subtract, ["lwi", "dm", "dm1"], ["uu"])
+        tt(T.ne[:], T.lwi[:].indirect(T.selx[:]), T.x1[:], ALU.not_equal, ["lwi", "selx", "x1_0", "x1_1"], ["ne"])
+        scan(T.kp[:], T.rs32[:], T.ne[:], 0.0, ALU.max, ALU.mult, ["ne", "rs32"], ["kp"])
         quant(hc, hs, 0, K, T.ht[:], ["ht%d" % b for b in four], ["ho"])
         send(partner, "ah%d" % t, [(hc[:, K:C].bitcast(dt.uint8), hc[:, 0:K].bitcast(dt.uint8)), (hs[:, K:C], hs[:, 0:K])], ["ho"])
         arrives(giver, "ah%d" % t, 2, ["hl"])
         for b in four:
             mm(4 + b, T.ec, T.es, 128 * b, hc, hs, 0, K, ["ec", "ho"])
-            copy("S", T.est[:, EW * b + OWN + 1:EW * b + OWN + 1 + K], ps(4 + b, 0, K), ["ps%d" % (4 + b)], ["eo%d" % b])
-        tt(T.ne[:], T.lwi[:].indirect(T.selx[:]), T.x1[:], ALU.not_equal, ["lwi", "selx", "x1"], ["ne"])
-        scan(T.kp[:], T.ne[:], T.pen[:], 0.0, ALU.mult, ALU.max, ["ne"] + ["pen%d" % q for q in range(5)], ["kp"])
-        tt(T.ku[:, 0:10], T.kp[:, 31::32], T.uu[:, 0:10], ALU.mult, ["kp", "uu"], ["ku"])
+            copy("S", T.est[:, EW * b:EW * b + K], ps(4 + b, 0, K), ["ps%d" % (4 + b)], ["eo%d" % b])
+        for e in range(2): tt(T.ku[:, e:10:2], T.kp[:, K * e + 31:K * e + K:32], T.uu[:, e:10:2], ALU.mult, ["kp", "uu"], ["ku%d" % e])
         for e in range(2):
-            ts(T.so[:, e:10:2], T.ku[:, e:10:2], T.dm[:, e:e + 1], ALU.add, r=["ku", "dm", "dm1"], w=["so%d" % e])
+            ts(T.so[:, e:10:2], T.ku[:, e:10:2], T.dm[:, e:e + 1], ALU.add, r=["ku%d" % e, "dm", "dm1"], w=["so%d" % e])
         for q in range(4, -1, -1):
-            copy("V", T.sw[:].indirect(T.so[:, 2 * q:2 * q + 2]), T.val[:, 32 * q:32 * q + 32], ["so0", "so1", "val"], ["sw"])
-        scan(T.ns[:, C:PL], T.rs16[:], T.sw[:, C:PL], 0.0, ALU.mult, ALU.add, ["sw", "rs16"], ["ns2"])
-        scan(T.ns[:, K:C], T.rs16[:], T.sw[:, 1:C:2], 0.0, ALU.mult, ALU.add, ["sw", "rs16"], ["ns1"])
-        copy("V", gs[:, 0:10], T.ns[:, C + 15::16], ["ns2"], ["gs"])
+            h = q % 2
+            copy("V", T.sw[:, 512 * h:512 * h + 512].indirect(T.so[:, 2 * q:2 * q + 2]), T.val[:, 32 * q:32 * q + 32], ["so0", "so1", "val"], ["sw%d" % h])
+
+        def first(h, i, a, b, c): scan(T.ns[:, PL * h + K * i:PL * h + K * i + K], T.rs16[:], T.sw[:, 512 * h + a:512 * h + b:c], 0.0, ALU.mult, ALU.add,
+                                       ["sw%d" % h, "rs16"], ["ns%d_%d" % (i, h)])
+
+        def both(o, i, w): tt(o, T.ns[:, K * i + 15:K * i + K:16], T.ns[:, PL + K * i + 15:PL + K * i + K:16], ALU.max, ["ns%d_0" % i, "ns%d_1" % i], [w])
+        first(1, 2, C, PL, 1)
+        first(1, 1, 1, C, 2)
+        first(0, 2, C, PL, 1)
+        first(0, 1, 1, C, 2)
+        both(gs[:, 0:10], 2, "gs")
         send(partner, "ag%d" % t, [(gl[:, 0:10], gs[:, 0:10])], ["gs"])
         arrives(giver, "ag%d" % t, 1, ["gl"])
-        copy("V", T.offo[:, 0:10], T.ns[:, K + 15:C:16], ["ns1"], ["offo"])
-        scan(T.ns[:, 0:K], T.rs16[:], T.sw[:, 0:C:2], 0.0, ALU.mult, ALU.add, ["sw", "rs16"], ["ns0"])
+        both(T.nn[:, 10:20], 1, "nn1")
+        first(1, 0, 0, C, 2)
+        first(0, 0, 0, C, 2)
+        ts(T.offo[:, 0:10], T.nn[:, 10:20], -1.0, ALU.mult, float(K), ALU.add, ["nn1"], ["offo"])
+        both(T.nn[:, 0:10], 0, "nn0")
         final = t == R - 1
         for b in four:
-            mm(b, T.ec, T.es, 128 * b, hc, hs, K, K, ["ec", "hl"])
-            copy("S", T.est[:, EW * b + 1:EW * b + 1 + K], ps(b, 0, K), ["ps%d" % b], ["eg%d" % b])
-        for b in four:
             o = T.xf[:, 4 + b::8] if final else T.xt[:, 4 * K + b:4 * C:4]
-            tt(o, T.est[:, EW * b + OWN:EW * b + OWN + 1 + K].indirect(T.offo[:, 0:10]), T.vp[:, PL * b + 1:PL * b + C:2], ALU.add,
+            tt(o, T.est[:, EW * b:EW * b + K + 1].indirect(T.offo[:, 0:10]), T.vp[:, PL * b + 1:PL * b + C:2], ALU.add,
                ["offo", "eo%d" % b, "ez%d" % b, "vp%d_1" % b], ["yo%d" % b if final else "xo%d" % b])
-            if b == 2: ts(T.ff[:, 0:10], T.ns[:, 15:K:16], 0.0, ALU.is_gt, float(OWN), ALU.mult, ["ns0"], ["ff"])
+            if b == 2: ts(T.ff[:, 0:10], T.nn[:, 0:10], 0.0, ALU.is_gt, float(OWN), ALU.mult, ["nn0"], ["ff"])
 
-        def own_first(): tt(T.oo[:, 0:10], T.ff[:, 0:10], T.ns[:, 15:K:16], ALU.add, ["ff", "ns0"], ["oo"])
+        def given(b): copy("VVSS"[b], T.est[:, EW * b + OWN:EW * b + OWN + K], ps(4 + b, 0, K), ["ps%d" % (4 + b)], ["eg%d" % b])
+
+        def own_first():
+            tt(T.oo[:, 0:10], T.ff[:, 0:10], T.nn[:, 0:10], ALU.add, ["ff", "nn0"], ["oo"])
+            for b in (0, 2, 1, 3):
+                mm(4 + b, T.ec, T.es, 128 * b, hc, hs, K, K, ["ec", "hl"])
+                if b > 1: given(b)
         if final:
             copy("V", T.opi[:], T.out1[:], ["out1"], ["opi"])
             own_first()
@@ -416,8 +393,11 @@ def rank_program(g, core, T, topo):
             dma("Y", "dop", [(T.op[2 * q + h, :], T.opf[32 * q:32 * q + 5, 32 * h:32 * h + 32]) for q in four for h in range(2)], ["opf"])
         else:
             odd_scores(t + 1, own_first)
+            lev1(0, 0)
         tt(T.em[:, 0:10], T.oo[:, 0:10], gl[:, 0:10], ALU.max, ["oo", "gl"], ["em"])
-        copy("V", T.offe[:, 0:10], T.em[:, 0:10], ["em"], ["offe"])
+        given(0)
+        ts(T.offe[:, 0:10], T.em[:, 0:10], -1.0, ALU.mult, float(OWN + K), ALU.add, ["em"], ["offe"])
+        given(1)
         for b in four:
             o = T.xf[:, b::8] if final else T.xt[:, b:4 * K:4]
             tt(o, T.est[:, EW * b:EW * b + OWN + 1 + K].indirect(T.offe[:, 0:10]), T.vp[:, PL * b:PL * b + C:2], ALU.add,
@@ -426,10 +406,9 @@ def rank_program(g, core, T, topo):
     quant(T.fc, T.fs, 0, C, T.xf[:], ["ye%d" % b for b in four] + ["yo%d" % b for b in four], ["fc"])
     for h in range(2): mm(h, T.vc, T.vs, 0, T.fc, T.fs, K * h, K, ["vc", "fc"])
     dma("Y", "doc", [(T.oc[:], T.fc[:].bitcast(dt.uint8))], ["fc"])
-    dma("S", "dos", [(T.osc[4 * q:4 * q + 4, :], T.fs[32 * q:32 * q + 4, :]) for q in range(2)], ["fc"])
+    dma("Y", "dos", [(T.osc[4 * q:4 * q + 4, :], T.fs[32 * q:32 * q + 4, :]) for q in four], ["fc"])
     for h in range(2): copy("VS"[h], T.ysb[:, K * h:K * h + K], ps(h, 0, K), ["ps%d" % h], ["ysb%d" % h])
-    dma("Y", "dy", [(T.y[:], T.ysb[:])], ["ysb0", "ysb1"])
-    dma("S", "dos", [(T.osc[4 * q:4 * q + 4, :], T.fs[32 * q:32 * q + 4, :]) for q in range(2, 4)], ["fc"])
+    dma("S", "dy", [(T.y[:], T.ysb[:])], ["ysb0", "ysb1"])
     for s in sorted(count, key=lambda s: s in DMAS):
         if waited.get(s, 0) < count[s]:
             e = s[0].upper() if s not in DMAS and s[0].upper() in POOL and s != "sent" else "G"

@@ -5,29 +5,33 @@ ACT = ActivationFunctionType
 C, K, PL, R = 320, 160, 480, 3
 BIG = 1e29
 KB = 100.0
-W1, W2, W3, WK, WD = 484, 84, 196, 124, 36
+W1, W3, WA, WK, WD = 564, 196, 484, 124, 36
+LOW, HI, PA = 81, 241, 401
 LAND = 416
 EW = 352
 OWN = 176
+SH = 16
+PV, SW = PL + SH, 640
 X4, U8, BF, F32, F16, I32, U16 = "float8_e4m3fn_x4", "uint8", "bfloat16", "float32", "float16", "int32", "uint16"
 SCRATCH = {"ps": ("psum", [128, 4096], F32)}
 for _d, _l in {
-    BF: dict(xin=1280, xt=4 * LAND, xf=1280, vin=512, zer=512, et=2048, one=128, idn=128, vp=4 * PL, zt=640, ht=640, est=4 * EW, tm=PL, pen=C,
-             sval=K, ne=C, kp=C, rs16=K, rs32=C, val=K, sw=1024, ns=2 * PL),
+    BF: dict(xin=1280, xt=4 * LAND, xf=1280, vin=512, et=2048, one=128, idn=128, vp=4 * PV, zt=640, ht=640, est=4 * EW,
+             sval=K, eq=C, kp=C, cm=C, cb=64, i16=K, c16=K, ca=K, cc=K, sw=2 * SW, ns=2 * PL, d0=2400),
     X4: dict(lc=512, vc=128, ec=512, fc=C, zc=K, wc0=576, wc1=576, wc2=576, hc0=C, hc1=C, hc2=C),
     U8: dict(ls=512, vs=128, es=512, fs=C, zs=K, ws0=576, ws1=576, ws2=576, hs0=C, hs1=C, hs2=C),
-    F32: dict(ysb=C, s1=PL, s2=120, m1=8 * W1, m2=8 * W2, cv=192, md=8 * W3, big=192, mk1=K, mk2=80, neg32=32, b2=32, bb=32 + 8 * WD, in1=64,
-              out1=64, o32=64, idt=512, jt=PL, p64=C, x1=C, uu=16, ku=16, dm=16, nn=20, ff=16, oo=16, em=16, pf=20, sxi=20, opf=64,
+    F32: dict(ysb=C, s1=PL, sa=448, m1=8 * W1, cv=192, md=8 * W3, big=192, mk1=K, mk2=32, neg32=32, b2=96, bb=8 * WD,
+              idt=512, x1=K, sf=16, nn=20, ff=16, oo=16, em=16, pf=24, sxi=20, opf=64,
               gs0=16, gs1=16, gs2=16, gl0=16, gl1=16, gl2=16),
-    F16: dict(neg=240, e1=5 * PL, e2=600, k1=5 * PL, k2=600, rs5=600, n1=8 * W1, n2=8 * WK),
+    F16: dict(neg=240, d1=2400, k1=2400, n1=8 * WA, n2=8 * WK, in1=64, out1=64, o32=64),
     I32: dict(lw0=16, lwi=16, pi=8, opi=64, opj=64),
-    U16: dict(lwu=16, so=16, offe=16, offo=16, selq=4, selx=20),
+    U16: dict(lwu=16, so=16, offe=16, offo=16, selk=2, selb=4, selx=20),
 }.items():
     for _k, _n in _l.items(): SCRATCH[_k] = ("sbuf", [128, _n], _d)
-POOL = {"V": 48, "S": 32, "P": 24, "G": 12}
 DMAS = ["dx", "dl", "dls", "dv", "dop", "doc", "dos", "dy"]
-SEMAPHORES = ["%s%d" % (e.lower(), i) for e in POOL for i in range(POOL[e])] + DMAS + ["sent"] + \
-             ["%s%d" % (k, t) for k in ("at", "ah", "ag") for t in range(R)]
+SEMAPHORES = ["v0", "s0", "p0", "g0"] + DMAS + ["sent"] + ["%s%d" % (k, t) for k in ("at", "ah", "ag") for t in range(R)]
+ORDER = """X0 L0 X1 L1 X2 L2 X3 L3 X4 H0 X5 H1 X6 H2 X7 S0 H3 c0 A0 A1 A2 A3 H4 P0 H5 P1 E1 H6 P2 H7 P3 E3
+Q0 P4 Q1 G1 P5 E5 Q2 P6 Q3 G3 P7 F0 F1 Q4 Q5 F2 G5 F3 k0 Q6 k1 Q7 G7 c1 k2 k3 a0 k4 a1 n0 b0 n1 a2 n2 b1 T0 n3 g0 a3 n4 b2 n5 g1 a4 n6 M0
+b3 n7 T1 M1 a5 g2 U0 M2 b4 M3 U1 a6 M4 b5 T2 M5 U2 a7 M6 b6 M7 b7 U3 T3"""
 
 
 def rank_program(g, core, T, topo):
@@ -60,7 +64,7 @@ def rank_program(g, core, T, topo):
 
     def note(e, s, c, r, w):
         j = len(ops)
-        ops.append((s, c, known[e] | 1 << j if e else 1 << j))
+        ops.append((s, c, (known[e] | 1 << j if e else 1 << j) | (ops[last[s]][2] if s in last else 0)))
         count[s], last[s] = c, j
         for t in r: rd.setdefault(t, []).append((e, j))
         for t in w:
@@ -69,12 +73,7 @@ def rank_program(g, core, T, topo):
 
     def op(e, fn, r=(), w=()):
         needs(e, r, w)
-        pool = ["%s%d" % (e.lower(), i) for i in range(POOL[e])]
-        free = [s for s in pool if s in last and known[e] >> last[s] & 1] or [s for s in pool if s not in last]
-        if not free:
-            free = [min(pool, key=lambda s: last[s])]
-            wait(e, last[free[0]])
-        s = free[0]
+        s = e.lower() + "0"
         fn().then_inc(T.sem[s], 1)
         note(e, s, count.get(s, 0) + 1, r, w)
 
@@ -119,248 +118,282 @@ def rank_program(g, core, T, topo):
         if flag: op("G", lambda: g.iota(o, pat, base, cm, allow_small_or_imprecise_dtypes=True), (), w)
         else: op("G", lambda: g.iota(o, pat, base, cm), (), w)
 
-    def spread(src, r, buf, tok, engines):
-        steps = [lambda: copy(engines[0], buf[:, 0:8], src(0, 128), r, [tok + "a"])]
-        for q in range(4):
-            steps.append(lambda q=q: copy(engines[1 + q], buf[32 * q:32 * q + 32, 8:16], src(32 * (q ^ 1), 32 * (q ^ 1) + 32), r, [tok + "b%d" % q]))
-        for h in range(2):
-            o = 1 - h
-            steps.append(lambda h=h, o=o: copy(engines[5 + h], buf[64 * h:64 * h + 64, 16:32], buf[64 * o:64 * o + 64, 0:16],
-                                               [tok + "a", tok + "b%d" % (2 * o), tok + "b%d" % (2 * o + 1)], [tok + "c%d" % h]))
-        return steps, [tok + "a", tok + "c0", tok + "c1"] + [tok + "b%d" % q for q in range(4)]
+    def whole(o, m, c, w): iota(o, [[0, m]], c, 0, w)
+    def select(o, i, pat, cmp, c, base, cm, r, w): op("G", lambda: g.affine_select(o, i, pat, cmp, c, base, cm), r, w)
 
-    def level(buf, width, k, a, m, data, first, lo, ops2, r, tok, c):
+    def level(buf, width, k, a, m, data, first, lo, ops2, r, w, p=128):
         o = k * width
-        prev = first if k == 0 else buf[:, o - width + a:o - width + a + m]
-        init = lo if a == 0 else buf[:, o + a:o + a + 1]
-        rr = list(r) + ["cst"]
-        if k: rr += [tok % (k - 1, c)] + ([tok % (k - 1, c - 1)] if a else [])
-        if a: rr.append(tok % (k, c - 1))
-        scan(buf[:, o + a + 1:o + a + 1 + m], data, prev, init, ops2[0], ops2[1], rr, [tok % (k, c)])
+        prev = first if k == 0 else buf[0:p, o - width + a:o - width + a + m]
+        init = lo if a == 0 else buf[0:p, o + a:o + a + 1]
+        scan(buf[0:p, o + a + 1:o + a + 1 + m], data, prev, init, ops2[0], ops2[1], list(r) + ["cst"], [w])
 
-    def weave(*chains):
-        for i in range(max(len(c) for c in chains)):
-            for c in chains:
-                if i < len(c) and c[i]: c[i]()
-
+    def below(tok, k): return [tok % (k - 1)] if k else []
     UP, DOWN = (ALU.max, ALU.min), (ALU.min, ALU.max)
     wcs = [(T["wc%d" % t], T["ws%d" % t]) for t in range(R)]
     hcs = [(T["hc%d" % t], T["hs%d" % t]) for t in range(R)]
-    four = range(4)
+    four, eight = range(4), range(8)
     pf = lambda c: T.pf[:, c:c + 1]
-    j, qq = pf(1), pf(6)
+    j, qq = pf(1), pf(2)
+    ET = ["et%d" % b for b in four]
+    quarter = lambda q: slice(32 * q, 32 * q + 32)
+    BP, BO, LO = 8, 48, 128
+    XE, XO = ["xe%d" % b for b in four], ["xo%d" % b for b in four]
+    F = ["f%d" % i for i in range(8)]
+    IN = ["in%d_%d" % (q, i) for q in four for i in range(5)]
 
     dma("Y", "dx", [(T.xin[:], T.x[:])], (), ["xin"])
-    iota(T.pi[:, 0:1], [[0, 1]], 0, 1, ["pi0"], False)
     fill(T.one[:], 1.0, ["one"])
-    fill(T.big[:], BIG, ["big"])
-    op("G", lambda: g.affine_select(T.idn[:], T.one[:], [[-1, 128]], ALU.is_equal, 0.0, 0, 1), ["one"], ["idn"])
-    op("G", lambda: g.affine_select(T.mk1[:], T.big[:, 0:K], [[-1, K]], ALU.not_equal, -BIG, 0, 1), ["big"], ["mk1"])
+    iota(T.pi[:, 0:1], [[0, 1]], 0, 1, ["pi0"], False)
+    select(T.idn[:], T.one[:], [[-1, 128]], ALU.is_equal, 0.0, 0, 1, ["one"], ["idn"])
     iota(T.idt[:], [[1, 512]], 0, 0, ["idt"])
     fill(T.et[:], 0.0, ["et"])
-    for b in four:
-        op("S", lambda b=b: S.activation(T.et[:, 513 * b:512 * (b + 1):4], T.idn[:], ACT.Copy), ["idn", "et"], ["et%d" % b])
-    for c, (sh, m) in enumerate([(0, 15), (0, 1), (1, 1), (5, 1), (6, 1), (5, 3)]):
+    fill(T.big[:], BIG, ["big"])
+    for b in four: copy("S", T.et[:, 513 * b:512 * (b + 1):4], T.idn[:], ["idn", "et"], ["et%d" % b])
+    select(T.mk1[:], T.big[:, 0:K], [[-1, K]], ALU.not_equal, -BIG, 0, 1, ["big"], ["mk1"])
+    for c, (sh, m) in enumerate([(0, 15), (5, 3), (0, 1), (1, 7), (5, 1), (6, 1)]):
         ts(T.pi[:, c + 1:c + 2], T.pi[:, 0:1], sh, ALU.logical_shift_right, m, ALU.bitwise_and, ["pi0"], ["pi%d" % (c + 1)])
     fill(T.m1[:, 0::W1], -BIG, ["c0"])
     copy("V", T.pf[:, 0:7], T.pi[:, 0:7], ["pi%d" % c for c in range(7)], ["pf"])
-    fill(T.m2[:, 0::W2], -BIG, ["c1"])
-    tt(T.pf[:, 8:10], T.pf[:, 2:4], T.pf[:, 4:6], ALU.not_equal, ["pf"], ["pf8"])
+    fill(T.m1[:, 4 * W1 + HI::W1], -BIG, ["c1"])
     fill(T.md[:, 0::W3], -BIG, ["c2"])
-    ts(pf(10), pf(9), 2.0, ALU.mult, pf(8), ALU.add, ["pf8"], ["pf10"])
-    fill(T.mk2[:], BIG, ["mk2"])
-    ts(pf(10), pf(10), 4.0, ALU.mult, qq, ALU.add, ["pf10"], ["pf10"])
-    op("V", lambda: V.memset(T.neg32[:], -KB), ["c0", "c1", "c2", "big"], ["cst"])
-    copy("V", T.mk2[96:128, 48:80], T.mk1[0:32, 0:32], ["mk1"], ["mk2"])
-    needs("Y", ["xin"], ())
-    dma("Y", "dl", [(T.lc[:].bitcast(dt.uint8), T.wc[:])], (), ["lc"])
-    dma("Y", "dls", [(T.ls[:], T.ws[:])], (), ["ls"])
-    dma("Y", "dv", [(T.vin[:], T.v[:])], (), ["vin"])
+    fill(T.m1[:, LOW::W1], -BIG, ["c3"])
+    ts(pf(16), pf(5), float(K), ALU.mult, pf(6), ALU.add, ["pf"], ["pf16"])
+    ts(pf(17), qq, 40.0 / 512, ALU.mult, (C + SH) / 512, ALU.add, ["pf"], ["pf17"])
+    ts(pf(18), qq, 40.0, ALU.mult, j, ALU.add, ["pf"], ["pf18"])
+    op("V", lambda: V.memset(T.neg32[:], -KB), ["c0", "c1", "c2", "c3", "big"], ["cst"])
+    ts(pf(16), pf(16), float(SH), ALU.add, 1.0 / 512, ALU.mult, ["pf16"], ["pf16"])
+    quant(T.ec, T.es, 0, 512, T.et[:], ET, ["ec"])
+    copy("V", T.mk2[96:128, :], T.mk1[0:32, 0:32], ["mk1"], ["mk2"])
+    for i, a in enumerate([T.idt[:, 1:C:2], T.idt[:, 0:C:2], T.idt[:, C:PL]]): affine(T.d1[:, 640 * i + 3:640 * i + 640:4], a, 1.0 / 512, SH / 512, ["idt"], ["f%d" % i])
+    affine(T.d1[:, 4 * PL + 3:4 * PL + 160:4], T.idt[:, 0:40], 1.0 / 512, pf(17), ["idt", "pf17"], ["f4"])
+    affine(T.d1[:, 4 * PL + 163::4], T.idt[:, 0:K:2], 1.0 / 512, pf(16), ["idt", "pf16"], ["f5"])
+    iota(T.i16[:], [[0, 10], [1, 16]], 0, 0, ["i16"])
     for b in four: copy("VVVS"[b], T.xt[:, b:4 * K:4], T.xin[:, b::8], ["xin"], ["xe%d" % b])
-    for b in four: copy("S", T.xt[:, 4 * K + b:4 * C:4], T.xin[:, 4 + b::8], ["xin"], ["xo%d" % b])
-    XE, XO = ["xe%d" % b for b in four], ["xo%d" % b for b in four]
+    for b in range(2): copy("S", T.xt[:, 4 * K + b:4 * C:4], T.xin[:, 4 + b::8], ["xin"], ["xo%d" % b])
 
-    def constants_for_keys():
-        def frac(o, i, w): affine(o, i, 1.0 / 512, 33.0 / 512, ["idt"], [w])
-        frac(T.e1[:, 0:800:5], T.idt[:, 1:C:2], "f0")
-        frac(T.e1[:, 800:1600:5], T.idt[:, 0:C:2], "f1")
-        frac(T.e1[:, 1600:2400:5], T.idt[:, C:PL], "f2")
-        for q in four:
-            a = K * (q % 2) + q // 2
-            frac(T.e2[32 * q:32 * q + 32, 0:400:5], T.idt[32 * q:32 * q + 32, a:a + K - q // 2:2], "f%d" % (3 + q))
-            frac(T.e2[32 * q:32 * q + 32, 400:600:5], T.idt[32 * q:32 * q + 32, C + 40 * q:C + 40 * q + 40], "f%d" % (7 + q))
-        affine(T.n1[:, 0::W1], T.idt[:, 0:8], 0.0, KB, ["idt"], ["c3"])
-        affine(T.n2[:, 0::WK], T.idt[:, 0:8], 0.0, KB, ["idt"], ["c4"])
-        affine(T.bb[:], T.idt[:, 0:C], 0.0, KB, ["idt"], ["c5"])
-        affine(T.neg[:], T.idt[:, 0:240], 0.0, -KB, ["idt"], ["c6"])
-        affine(T.rs5[:, 0::5], T.idt[:, 0:120], 0.0, 0.0, ["c3", "c4", "c5", "c6"], ["c7"])
+    def constants(i):
+        if i == 0:
+            fill(T.d1[:, 1::4], 2.0, ["f3"])
+            ts(pf(18), pf(18), -8.0, ALU.add, r=["pf18"], w=["pf18"])
+            fill(T.in1[:], 0.0, IN)
+        if i == 1:
+            ts(T.selb[:, 0:3], T.idt[:, 0:48:16], pf(18), ALU.add, 0.0, ALU.max, ["idt", "pf18"], ["selb"])
+            for c, o in enumerate([T.n1[:, 0::WA], T.n2[:, 0::WK], T.bb[:, 0::WD], T.b2[:]]): fill(o, KB, ["c%d" % (5 + c)])
+        if i == 2:
+            op("V", lambda: V.memset(T.neg[:], -KB), ["c5", "c6", "c7", "c8"], ["ck"])
+            ts(pf(7), j, 1.0, ALU.add, r=["pf"], w=["pf7"])
+            ts(pf(8), j, 4.0, ALU.mult, 512.0, ALU.add, ["pf"], ["pf8"])
+            ts(pf(9), j, 4.0, ALU.mult, 576.0, ALU.add, ["pf"], ["pf9"])
+            ts(pf(19), j, 15.0, ALU.is_equal, r=["pf"], w=["pf19"])
+            for i, (at, by) in enumerate([(j, 4096.0), (j, pf(8)), (pf(7), 4096.0), (j, pf(9))]):
+                ts(T.cb[:, 16 * i:16 * i + 16], T.i16[:, 0:16], at, ALU.is_equal, by, ALU.mult, ["i16", "pf7", "pf8", "pf9"], ["cb%d" % i])
+            ts(pf(12), pf(19), 1 - 2.0 ** -12, ALU.mult, 2.0 ** -12, ALU.add, ["pf19"], ["pf12"])
+            ts(pf(10), pf(3), float(K), ALU.mult, 31.0, ALU.add, ["pf"], ["pf10"])
+            ts(T.cb[:], T.cb[:], 1.0, ALU.max, r=["cb%d" % i for i in four], w=["cb"])
+            ts(pf(13), pf(19), -511.0 / 512, ALU.mult, -1.0 / 512, ALU.add, ["pf19"], ["pf13"])
+            ts(pf(14), pf(19), -255.5, ALU.mult, 256.0, ALU.add, ["pf19"], ["pf14"])
+            ts(pf(15), pf(19), -511.0 * OWN, ALU.mult, 512.0 * OWN, ALU.add, ["pf19"], ["pf15"])
+            ts(T.cb[:, 0::32], T.cb[:, 0::32], 0.0, ALU.mult, r=["cb"], w=["cc0"])
+            ts(T.cb[:, 16:17], T.cb[:, 16:17], 2.0 ** -12, ALU.mult, r=["cb"], w=["cc1"])
+            ts(T.cb[:, 48:49], T.cb[:, 48:49], pf(12), ALU.mult, r=["cb", "pf12"], w=["cc2"])
+            for i in range(10):
+                select(T.cm[:, 32 * i:32 * i + 32], T.cb[:, 32 * (i // 5):32 * (i // 5) + 32], [[0, 32]], ALU.is_equal, 0.0, 0, 0, ["cc0", "cc1", "cc2"], ["cm%d" % i])
+        if i == 3:
+            whole(T.d0[:, 0::4], 600, 0, ["f6"])
+            whole(T.d0[:, 3::4], 600, 1, ["f7"])
+            iota(T.sxi[:], [[1, 2], [2, 5], [0, 2]], 0, 0, ["sxi"])
+            iota(T.sval[:], [[-1, K]], K, 0, ["sval"])
+            for b in four:
+                whole(T.vp[:, PV * b:PV * b + SH], SH, 0, ["vz%d" % b])
+                whole(T.est[:, b * EW + K:b * EW + OWN], OWN - K, 0, ["ez%d" % b])
+            whole(T.est[:, OWN + K::EW], 4, 0, ["ez"])
 
-    def constants_for_offsets():
-        affine(pf(10), pf(10), 2.0, 0.0, ["pf10"], ["pf10"])
-        affine(pf(11), qq, 72.0, 64.0, ["pf"], ["pf11"])
-        affine(pf(15), j, -2.0, 0.5, ["pf"], ["pf15"])
-        affine(pf(17), j, 1.0, float(PL), ["pf"], ["pf17"])
-        affine(pf(18), j, 1.0, float(PL + 16), ["pf"], ["pf18"])
-        affine(T.sval[:], T.idt[:, 0:K], -1.0, float(K), ["idt"], ["sval"])
+    spare_first = [lambda: ts(pf(11), pf(4), 32.0, ALU.mult, pf(10), ALU.add, ["pf10"], ["pf11"]),
+                   lambda: ts(T.ca[:], T.i16[:], j, ALU.not_equal, r=["i16", "pf"], w=["ca"]),
+                   lambda: ts(T.cc[:], T.i16[:], pf(7), ALU.is_equal, 512.0, ALU.mult, ["i16", "pf7"], ["cc"]),
+                   lambda: copy("V", T.selx[:], T.sxi[:], ["sxi"], ["selx"]),
+                   lambda: ts(T.selk[:, 0:1], pf(11), float(C - 1), ALU.min, r=["pf11"], w=["selk"]),
+                   lambda: tt(T.c16[:], T.ca[:], T.cc[:], ALU.max, ["ca", "cc"], ["c16"])]
+    spare_last = [lambda: quant(T.vc, T.vs, 0, 128, T.vin[:], ["vin"], ["vc"]), None,
+                  lambda: ts(T.opi[:], T.out1[:], 512.0, ALU.mult, r=["out1"], w=["opi"]),
+                  lambda: ts(T.opj[:], T.opi[:], 511, ALU.bitwise_and, r=["opi"], w=["opj"]),
+                  lambda: ts(T.opf[:], T.opj[:], -float(SH), ALU.add, r=["opj"], w=["opf"]),
+                  lambda: dma("Y", "dop", [(T.op[2 * q + h, :], T.opf[32 * q:32 * q + 5, 32 * h:32 * h + 32]) for q in four for h in range(2)], ["opf"])]
 
-    def constants_for_lists():
-        act(T.jt[:], T.jt[:], ACT.Abs, -1.0, j, ["pf", "jt0", "jt1"], ["jt"])
-        act(T.p64[:], T.p64[:], ACT.Sign, 1.0, pf(15), ["pf15", "p64_0", "p64_1"], ["p64"])
-        copy("S", T.rs16[:, 0::16], T.zer[:, 0:10], ["zer"], ["rs16"])
-        affine(T.dm[:, 0:10:2], T.idt[:, 0:5], 0.0, pf(17), ["pf17"], ["dm"])
-        affine(T.dm[:, 1:10:2], T.idt[:, 0:5], 0.0, pf(18), ["pf18"], ["dm1"])
-        act(T.tm[:], T.jt[:], ACT.Relu, -1.0, 1.0, ["jt"], ["tm"])
-        act(T.pen[:], T.p64[:], ACT.Relu, 1000.0, 0.0, ["p64"], ["pen"])
-        copy("S", T.rs32[:, 0::32], T.one[:, 0:10], ["one"], ["rs32"])
+    def repeat(i): copy("S", T.xt[:, 4 * (C + 32 * i):4 * (C + 32 * i + 32)], T.xt[:, 4 * 288:4 * C], XO, ["xr%d" % i])
 
-    def static_offsets():
-        return [lambda: ts(pf(12), j, 4.0, ALU.is_ge, r=["pf"], w=["pf12"]),
-                lambda: ts(pf(13), pf(11), pf(10), ALU.subtract, pf(12), ALU.mult, ["pf10", "pf11", "pf12"], ["pf13"]),
-                lambda: ts(pf(14), pf(12), 35.0, ALU.mult, 1.0, ALU.add, ["pf12"], ["pf14"]),
-                lambda: ts(T.selq[:, 0:2], T.one[:, 0:2], pf(13), ALU.mult, pf(10), ALU.add, ["pf13"], ["selq0"]),
-                lambda: ts(pf(14), pf(14), pf(13), ALU.add, pf(10), ALU.add, ["pf13", "pf14"], ["pf14"]),
-                lambda: copy("V", T.selx[:], T.sxi[:], ["sxi"], ["selx"]),
-                lambda: ts(T.selq[:, 2:4], T.one[:, 0:2], pf(14), ALU.mult, r=["pf14", "selq0"], w=["selq"])]
-
-    def lev1(k, c): level(T.m1, W1, k, K * c, K, T.s1[:, K * c:K * c + K] if c < 2 else ps(2, 0, K), T.big[:, 0:K], -BIG, UP,
-                          ["s1_%d" % c if c < 2 else "ps2"], "m1_%d_%d", c)
-
-    def odd_scores(t, between):
+    def odd_columns(t):
         wc, ws = wcs[t]
-        for i in range(3): copy("S", T.xt[:, 4 * (C + 32 * i):4 * (C + 32 * i + 32)], T.xt[:, 4 * 288:4 * C], XO, ["xr%d" % i])
         quant(wc, ws, K, C, T.xt[:, 4 * K:4 * C], XO, ["wo"])
         mm(0, wc, ws, K, wc, ws, K, K, ["wo"])
-        between()
-        tt(T.s1[:, 0:K], ps(0, 0, K), T.mk1[:], ALU.min, ["ps0", "mk1"], ["s1_0"])
-        quant(wc, ws, 288, LAND, T.xt[:, 4 * 288:], XO + ["xr0", "xr1", "xr2"], ["wo"])
+
+    def repeated_columns(t):
+        wc, ws = wcs[t]
+        quant(wc, ws, 288, LAND, T.xt[:, 4 * 288:], XO + ["xr0", "xr1", "xr2"], ["wr", "wo"])
+        mm(3, wc, ws, 288, wc, ws, K, K, ["wo", "wr"])
+        for q in (3, 2): copy("S", T.sa[quarter(q), BO:BO + 80], ps(3, 80 * q - K, 80 * q - 80, 32 * q, 32 * q + 32), ["ps3"], ["s2_%d" % q])
+
+    def best_places(t):
+        wc, ws = wcs[t]
+        big = T.big[:, 0:K]
+        S1, S2 = ["s1_0", "s1_1", "s1_2"], ["s2_%d" % q for q in four]
+        CV = ["cva", "cvb0", "cvb1"] + ["cvc%d" % q for q in four]
+        slot = {1: (T.d1, 0), 3: (T.d0, 2), 5: (T.d0, 1), 7: (T.d1, 2)}
+
+        def low(k): level(T.m1, W1, k, LOW, K, T.sa[:, LO:LO + K], big, -BIG, UP, ["lo"] + below("l%d", k), "l%d" % k)
+        def high(k): level(T.m1, W1, k, HI, K, T.sa[:, LO + K:LO + C], big, -BIG, UP, ["hi", "l%d" % min(k, 3)] + below("h%d", k), "h%d" % k)
+        def far(k): level(T.m1, W1, k, PA, K, ps(2, 0, K), big, -BIG, UP, ["ps2", "h%d" % k] + below("p%d", k), "p%d" % k)
+
+        def signs(k, c=None):
+            d, a = slot[k]
+            c, m = (0, PL) if c is None else (120 * c, 120)
+            sign(d[:, 4 * c + a:4 * (c + m):4], T.s1[:, c:c + m], T.m1[:, k * W1 + PA + K:k * W1 + PA + K + 1], S1 + ["p%d" % k], ["e1_%d_%d" % (k, c // 120)])
+
+        def own2(k): level(T.m1, W1, k, 0, 80, T.sa[:, BO:BO + 80], T.big[:, 0:80], -BIG, UP, S2 + below("x%d", k), "x%d" % k)
+        def far2(k): level(T.md, W3, k, 0, 192, T.cv[:], T.big[:], -BIG, UP, CV + ["cvp"] + below("md%d", k), "md%d" % k)
+
+        def signs2(k):
+            d, a = slot[k]
+            sign(d[:, 4 * PL + a::4], T.sa[:, BP:BP + 120], T.md[:, k * W3 + 192:k * W3 + 193], S2 + ["s2p", "md%d" % k], ["e2_%d" % k])
+
+        def spread(_):
+            X8 = ["x%d" % k for k in eight]
+            copy("S", T.cv[:, 0:8], T.m1[:, 80::W1], X8, ["cva"])
+            for h in range(2): copy("S", T.cv[64 * h:64 * h + 64, 8:16], T.m1[64 - 64 * h:128 - 64 * h, 80::W1], X8, ["cvb%d" % h])
+            for q in four: copy("S", T.cv[quarter(q), 16:32], T.cv[quarter(q ^ 1), 0:16], ["cva", "cvb0", "cvb1"], ["cvc%d" % q])
+
+        def arrived(i):
+            if i == 0:
+                mm(2, wc, ws, K, wc, ws, LAND, K, ["wo", "wl"])
+                mm(0, wc, ws, 288, wc, ws, LAND, K, ["wo", "wr", "wl"])
+                mm(1, wc, ws, K, wc, ws, LAND, K, ["wo", "wl"])
+                if t == 0:
+                    dma("Y", "dl", [(T.lc[:].bitcast(dt.uint8), T.wc[:])], ["wl"], ["lc"])
+                    dma("Y", "dls", [(T.ls[:], T.ws[:])], (), ["ls"])
+                    dma("Y", "dv", [(T.vin[:], T.v[:])], (), ["vin"])
+            if i == 1: copy("S", T.cv[:, 32:], ps(0, 0, K), ["ps0"], ["cvp"])
+            if i == 2: copy("S", T.s1[:, C:PL], ps(1, 0, K), ["ps1"], ["s1_2"])
+            if i == 3: copy("S", T.sa[:, 0:BO], T.cv[:, 32:].indirect(T.selb[:, 0:3]), ["cvp", "selb"], ["s2p"])
+
+        def keys(c): scan(T.k1[:, PL * c:PL * c + PL], T.d0[:, PL * c:PL * c + PL], T.d1[:, PL * c:PL * c + PL], 0.0, ALU.mult, ALU.add,
+                          F + (["e1_1_0", "e1_3_0", "e1_5_0", "e1_7_%d" % c] if c < 4 else ["e2_%d" % i for i in (1, 3, 5, 7)]), ["k%d" % c])
+
+        def key1(k, c=0):
+            level(T.n1, WA, k, 240 * c, 240, T.k1[:, 960 * c + 3:960 * c + 960:4], T.neg[:], KB, DOWN,
+                  ["ck", "k%d" % (2 * c), "k%d" % (2 * c + 1)] + below("n%d_" + str(c), k) + (["n%d_0" % k] if c else []), "n%d_%d" % (k, c))
+
+        def key2(k): level(T.n2, WK, k, 0, 120, T.k1[:, 4 * PL + 3::4], T.neg[:, 0:120], KB, DOWN, ["ck", "k4"] + below("q%d", k), "q%d" % k)
+
+        def gather2(s):
+            m = 2 * s + 4
+            for q in four:
+                copy("VSVS"[q] if s == 2 else "S", T.b2[0:32, 32 * s + 8 * q:32 * s + 8 * q + m], T.n2[quarter(q), 120:m * WK:WK], ["ck", "q%d" % (m - 1)], ["b2_%d_%d" % (s, q)])
+
+        def merge2(k):
+            s = max(k // 2 - 1, 0)
+            level(T.bb, WD, k, 0, 32, T.b2[0:32, 32 * s:32 * s + 32], T.neg32[0:32, :], KB, DOWN, ["b2_%d_%d" % (s, q) for q in four] + below("d%d", k), "d%d" % k, 32)
+
+        def turn(q):
+            for i in four:
+                copy("VSVS"[i] if q == 3 else "S", T.in1[quarter(q), i::32], T.n1[quarter(i), 2 * q * WA + PL:(2 * q + 2) * WA:WA], ["n%d_1" % (2 * q + 1)], ["in%d_%d" % (q, i)])
+
+        def turn2(q): copy("V" if q == 3 else "S", T.in1[quarter(q), 4::32], T.bb[0:32, 2 * q * WD + 32:(2 * q + 2) * WD:WD], ["d%d" % (2 * q + 1)], ["in%d_4" % q])
+
+        def beside(i):
+            if i == 0:
+                for h in range(2): whole(T.sw[:, SW * h + SH:SW * h + PV], PL, 0, ["sw%d" % h])
+            if i == 1:
+                for b in four:
+                    mm(4 + b, T.ec, T.es, 128 * b, wc, ws, LAND, K, ["ec", "wl"])
+                    copy("S", T.vp[:, PV * b + SH + C:PV * b + PV], ps(4 + b, 0, K), ["ps%d" % (4 + b)], ["vp%d_2" % b])
+        step = dict(L=low, H=high, P=far, E=signs, F=lambda c: signs(7, c), X=own2, Q=far2, G=signs2, S=spread, A=arrived, k=keys, a=key1,
+                    b=lambda k: key1(k, 1), n=key2, g=gather2, M=merge2, T=turn, U=turn2, c=beside)
+        for w in ORDER.split(): step[w[0]](int(w[1]))
 
     for t in range(R):
         partner, giver = T.cores[(rank + 1 + t) % n], T.cores[(rank - 1 - t) % n]
         wc, ws = wcs[t]
         hc, hs = hcs[t]
         gs, gl = T["gs%d" % t], T["gl%d" % t]
+        final = t == R - 1
         quant(wc, ws, 0, K, T.xt[:, 0:4 * K], XE, ["we"])
         send(giver, "at%d" % t, [(wc[:, LAND:].bitcast(dt.uint8), wc[:, 0:K].bitcast(dt.uint8)), (ws[:, LAND:], ws[:, 0:K])], ["we"])
         arrives(partner, "at%d" % t, 2, ["wl"])
         if t == 0:
-            iota(T.jt[:, 0:C], [[0, 10], [1, 16], [0, 2]], 0, 0, ["jt0"])
-            iota(T.jt[:, C:PL], [[0, 10], [1, 16]], 0, 0, ["jt1"])
-            for e in range(2): iota(T.p64[:, K * e:K * e + K], [[0, 5], [1, 2], [2, 16]], -e, 0, ["p64_%d" % e])
-            iota(T.sxi[:], [[1, 2], [2, 5], [0, 2]], 0, 0, ["sxi"])
-            odd_scores(0, lambda: quant(T.ec, T.es, 0, 512, T.et[:], ["et%d" % b for b in four], ["ec"]))
-            lev1(0, 0)
-            fill(T.rs5[:], 1.0, ["c7"])
+            constants(3)
+            for b in (2, 3): copy("V", T.xt[:, 4 * K + b:4 * C:4], T.xin[:, 4 + b::8], ["xin"], ["xo%d" % b])
+            for i in range(3): repeat(i)
+            odd_columns(0)
+            constants(0)
         mm(1, wc, ws, K, wc, ws, 0, K, ["wo", "we"])
-        mm(3, wc, ws, 288, wc, ws, 0, C, ["wo", "we"])
-        copy("S", T.s1[:, K:C], ps(1, 0, K), ["ps1"], ["s1_1"])
-        for q in range(3): copy("S", T.s2[32 * q:32 * q + 32, 0:80], ps(3, 80 * q, 80 * q + 80, 32 * q, 32 * q + 32), ["ps3"], ["s2_%d" % q])
-        S2 = ["s2_%d" % q for q in four]
-        steps, CV = spread(lambda a, b: T.m2[a:b, 80::W2], ["m2_%d_0" % k for k in range(8)], T.cv, "cv", "SSSSSSS")
-        aa = [lambda: lev1(1, 0), lambda: lev1(2, 0)]
-        for k in range(8): aa += ([lambda k=k: lev1(k + 3, 0)] if k < 5 else []) + [lambda k=k: lev1(k, 1)]
-        bo = [lambda: tt(T.s2[96:128, 0:80], ps(3, 240, C, 96, 128), T.mk2[96:128, :], ALU.min, ["ps3", "mk2"], ["s2_3"])]
-        bo += [lambda k=k: level(T.m2, W2, k, 0, 80, T.s2[:, 0:80], T.big[:, 0:80], -BIG, UP, S2, "m2_%d_%d", 0) for k in range(8)]
-        if t == 0: constants_for_keys()
-        for b in four:
-            mm(4 + b, T.ec, T.es, 128 * b, wc, ws, 0, C, ["ec", "we", "wo"])
-            for e in range(2):
-                copy("S", T.vp[:, PL * b + e:PL * b + C:2], ps(4 + b, K * e, K * e + K), ["ps%d" % (4 + b)], ["vp%d_%d" % (b, e)])
-        weave(aa, [None] * 3 + bo)
-        for f in steps: f()
+        tt(T.s1[:, 0:K], ps(0, 0, K), T.mk1[:], ALU.min, ["ps0", "mk1"], ["s1_0"])
         if t == 0:
-            fill(T.zer[:], 0.0, ["zer"])
-            fill(T.rs16[:], 1.0, ["rs16"])
-            fill(T.rs32[:], 0.0, ["rs32"])
-            fill(T.est[:, OWN + K::EW], 0.0, ["ez"])
-            for b in four: fill(T.est[:, b * EW + K:b * EW + OWN], 0.0, ["ez%d" % b])
-        mm(0, wc, ws, 288, wc, ws, LAND, K, ["wo", "wl"])
-        mm(2, wc, ws, K, wc, ws, LAND, K, ["wo", "wl"])
-        mm(1, wc, ws, K, wc, ws, LAND, K, ["wo", "wl"])
-        for b in four: mm(4 + b, T.ec, T.es, 128 * b, wc, ws, LAND, K, ["ec", "wl"])
-        copy("S", T.cv[:, 32:], ps(0, 0, K), ["ps0"], ["cvp"])
-        copy("S", T.s1[:, C:PL], ps(1, 0, K), ["ps1"], ["s1_2"])
-        for q in four: copy("S", T.s2[32 * q:32 * q + 32, 80:120], T.cv[32 * q:32 * q + 32, 32 + 40 * q:72 + 40 * q], ["cvp"], ["s2p%d" % q])
-        S1 = ["s1_0", "s1_1", "s1_2"]
-        S2 = S2 + ["s2p%d" % q for q in four]
-
-        def lev2(k):
-            level(T.md, W3, k, 0, 192, T.cv[:], T.big[:], -BIG, UP, CV + ["cvp"], "md_%d_%d", 0)
-            if k % 2: sign(T.e2[:, 1 + k // 2::5], T.s2[:], T.md[:, k * W3 + 192:k * W3 + 193], S2 + ["md_%d_0" % k], ["e2_%d" % (k // 2)])
-        for k in range(8):
-            if k > 5: lev2(k)
-            lev1(k, 2)
-            if k <= 5: lev2(k)
-            v = T.m1[:, k * W1 + PL:k * W1 + PL + 1]
-            if k == 7:
-                for c in four: sign(T.e1[:, 600 * c + 4:600 * c + 600:5], T.s1[:, 120 * c:120 * c + 120], v, S1 + ["m1_7_2"], ["e1_3_%d" % c])
-            elif k % 2: sign(T.e1[:, 1 + k // 2::5], T.s1[:], v, S1 + ["m1_%d_2" % k], ["e1_%d" % (k // 2)])
-        for b in four: copy("S", T.vp[:, PL * b + C:PL * b + PL], ps(4 + b, 0, K), ["ps%d" % (4 + b)], ["vp%d_2" % b])
-        if t == 0: constants_for_offsets()
-        E1 = ["e1_0", "e1_1", "e1_2", "f0", "f1", "f2", "c7"]
-
-        def sum1(c): scan(T.k1[:, 600 * c:600 * c + 600], T.rs5[:], T.e1[:, 600 * c:600 * c + 600], 0.0, ALU.mult, ALU.add,
-                          E1 + ["e1_3_%d" % c], ["k1_%d" % c])
-
-        def key1(k, c): level(T.n1, W1, k, 240 * c, 240, T.k1[:, 1200 * c + 4:1200 * c + 1200:5], T.neg[:], KB, DOWN,
-                              ["k1_%d" % i for i in range(2 * c, 2 * c + 2)], "n1_%d_%d", c)
-
-        def merge2(k):
-            o = 32 + k * WD
-            prev = T.neg32[:] if k == 0 else T.bb[:, o - WD:o - WD + 32]
-            scan(T.bb[:, o + 1:o + 33], T.b2[:], prev, KB, ALU.min, ALU.max, B2 + ["c5"] + (["d2_%d" % (k - 1)] if k else []), ["d2_%d" % k])
-        scan(T.k2[:], T.rs5[:], T.e2[:], 0.0, ALU.mult, ALU.add, ["e2_%d" % i for i in four] + ["f%d" % i for i in range(3, 11)] + ["c7"], ["k2"])
-        steps1, B1 = spread(lambda a, b: T.n1[a:b, PL::W1], ["n1_%d_1" % k for k in range(8)] + ["c5"], T.bb, "b1", "VVSVSVS")
-        steps2, B2 = spread(lambda a, b: T.n2[a:b, 120::WK], ["n2_%d_0" % k for k in range(8)], T.b2, "b2", "SSSSSSS")
-        weave([lambda c=c: sum1(c) for c in four] + [lambda k=k: key1(k, 0) for k in four],
-              [lambda k=k: level(T.n2, WK, k, 0, 120, T.k2[:, 4::5], T.neg[:, 0:120], KB, DOWN, ["k2"], "n2_%d_%d", 0) for k in range(8)])
-        for f in steps2: f()
-        if t == 0: constants_for_lists()
-        weave([lambda k=k: key1(k, 0) for k in range(4, 8)] + [lambda k=k: merge2(k) for k in four], [lambda k=k: key1(k, 1) for k in range(8)],
-              static_offsets() if t == 0 else [])
-        weave([lambda k=k: merge2(k) for k in range(4, 8)], steps1[0:2] + [lambda: [f() for f in steps1[2:5]], lambda: [f() for f in steps1[5:]]])
-        for h in range(2): copy("S", T.sw[:, 512 * h:512 * h + 512], T.zer[:], ["zer"], ["sw%d" % h])
-        ts(T.in1[:], T.bb[:].indirect(T.selq[:]), 512.0, ALU.mult, 2015.0, ALU.add, B1 + ["d2_%d" % k for k in range(8)] + ["selq"], ["in1"])
-        op("V", lambda: V.transpose(T.out1[:], T.in1[:]), ["in1"], ["out1"])
-        for e in range(2):
-            op("V", lambda e=e: V.transpose(T.o32[:, e::2], T.out1[:, e::2]), ["out1"], ["o32_%d" % e])
-        copy("V", T.lw0[:], T.o32[:, 0:16], ["o32_0", "o32_1"], ["lw0"])
-        ts(T.lwi[:], T.lw0[:], 511, ALU.bitwise_and, r=["lw0"], w=["lwi"])
-        copy("V", T.lwu[:], T.lwi[:], ["lwi"], ["lwu"])
-        tt(T.uu[:, 0:10], T.lwi[:, 0:10], T.dm[:, 0:10], ALU.subtract, ["lwi", "dm", "dm1"], ["uu"])
-        lw = T.lwu[:, 0:10]
-        for b in (0, 2, 1, 3):
-            copy("VVSS"[b], T.zt[:, b::4], T.vp[:, PL * b:PL * b + PL].indirect(lw), ["lwu"] + ["vp%d_%d" % (b, i) for i in range(3)], ["zt%d" % b])
-
-        def listed(e): tt(T.x1[:, K * e:K * e + K], T.idt[:].indirect(lw), T.pen[:, K * e:K * e + K], ALU.add, ["lwu", "idt", "pen"], ["x1_%d" % e])
-        listed(0)
-        quant(T.zc, T.zs, 0, K, T.zt[:], ["zt%d" % b for b in four], ["zc"])
+            repeated_columns(0)
+            constants(1)
+        mm(0, wc, ws, 288, wc, ws, 0, K, ["wo", "wr", "we"])
+        mm(2, wc, ws, K, wc, ws, 0, K, ["wo", "we"])
+        for q in range(2): copy("S", T.sa[quarter(q), BO:BO + 80], ps(0, 80 * q, 80 * q + 80, 32 * q, 32 * q + 32), ["ps0"], ["s2_%d" % q])
+        copy("S", T.s1[:, K:C], ps(2, 0, K), ["ps2"], ["s1_1"])
+        own = T.sa[96:128, BO + 48:BO + 80]
+        if t: tt(own, own, T.mk2[96:128, :], ALU.min, ["s2_3", "mk2"], ["s2_3"])
+        tt(T.sa[:, LO:LO + K], ps(1, 0, K), T.s1[:, 0:K], ALU.min, ["ps1", "s1_0"], ["lo"])
+        tt(T.sa[:, LO + K:LO + C], ps(1, 0, K), T.s1[:, 0:K], ALU.max, ["ps1", "s1_0"], ["hi"])
+        if t == 0:
+            tt(own, own, T.mk2[96:128, :], ALU.min, ["s2_3", "mk2"], ["s2_3"])
+            constants(2)
         for b in four:
-            mm(4 + b, T.lc, T.ls, 128 * b, T.zc, T.zs, 0, K, ["lc", "ls", "zc"])
-            op("S", lambda b=b: S.activation(T.ht[:, b::4], ps(4 + b, 0, K), ACT.Copy, scale=0.03125), ["ps%d" % (4 + b)], ["ht%d" % b])
-        listed(1)
-        tt(T.val[:], T.tm[:].indirect(lw), T.sval[:], ALU.mult, ["lwu", "tm", "sval"], ["val"])
-        tt(T.ne[:], T.lwi[:].indirect(T.selx[:]), T.x1[:], ALU.not_equal, ["lwi", "selx", "x1_0", "x1_1"], ["ne"])
-        scan(T.kp[:], T.rs32[:], T.ne[:], 0.0, ALU.max, ALU.mult, ["ne", "rs32"], ["kp"])
+            mm(4 + b, T.ec, T.es, 128 * b, wc, ws, 0, C, ["ec", "we", "wo", "wr"])
+            for e in range(2):
+                copy("S", T.vp[:, PV * b + SH + e:PV * b + SH + C:2], ps(4 + b, K * e, K * e + K), ["ps%d" % (4 + b)], ["vp%d_%d" % (b, e)])
+        best_places(t)
+        lw = T.lwu[:, 0:10]
+        chain = [lambda: op("V", lambda: V.transpose(T.out1[:], T.in1[:]), IN, ["out1"]),
+                 lambda: [op("V", lambda e=e: V.transpose(T.o32[:, e::2], T.out1[:, e::2]), ["out1"], ["o32_%d" % e]) for e in range(2)],
+                 lambda: ts(T.lw0[:], T.o32[:, 0:16], 512.0, ALU.mult, r=["o32_0", "o32_1"], w=["lw0"]),
+                 lambda: ts(T.lwi[:], T.lw0[:], 511, ALU.bitwise_and, r=["lw0"], w=["lwi"]),
+                 lambda: copy("V", T.lwu[:], T.lwi[:], ["lwi"], ["lwu"]), None]
+        for f, h in zip(spare_first if t == 0 else spare_last if final else [None] * 6, chain):
+            if f: f()
+            if h: h()
+        copy("S", T.x1[:], T.idt[:].indirect(lw), ["lwu", "idt"], ["x1"])
+        for b in (0, 2, 1, 3):
+            copy("VVSS"[b], T.zt[:, b::4], T.vp[:, PV * b:PV * b + PV].indirect(lw), ["lwu", "vz%d" % b] + ["vp%d_%d" % (b, i) for i in range(3)], ["zt%d" % b])
+        for e in range(2): tt(T.eq[:, K * e:K * e + K], T.lwi[:].indirect(T.selx[:, 10 * e:10 * e + 10]), T.x1[:], ALU.is_equal, ["lwi", "selx", "x1"], ["eq%d" % e])
+        quant(T.zc, T.zs, 0, K, T.zt[:], ["zt%d" % b for b in four], ["zc"])
+        for b in four: mm(4 + b, T.lc, T.ls, 128 * b, T.zc, T.zs, 0, K, ["lc", "ls", "zc"])
+
+        def cast(b):
+            if b < 2: ts(T.ht[:, b::4], ps(4 + b, 0, K), 0.03125, ALU.mult, r=["ps%d" % (4 + b)], w=["ht%d" % b])
+            else: op("S", lambda: S.activation(T.ht[:, b::4], ps(4 + b, 0, K), ACT.Copy, scale=0.03125), ["ps%d" % (4 + b)], ["ht%d" % b])
+
+        def scatter(q):
+            h = q % 2
+            copy("V", T.sw[:, SW * h:SW * h + SW].indirect(T.so[:, 2 * q:2 * q + 2]), T.sval[:, 32 * q:32 * q + 32], ["so", "sval"], ["sw%d" % h])
+        scan(T.kp[:], T.cm[:], T.eq[:], 0.0, ALU.mult, ALU.max, ["eq0", "eq1"] + ["cm%d" % i for i in range(10)], ["kp"])
+        cast(2)
+        cast(3)
+        tt(T.sf[:], T.kp[:].indirect(T.selk[:, 0:1]), T.lwi[:], ALU.max, ["kp", "selk", "lwi"], ["sf"])
+        cast(0)
+        copy("V", T.so[:], T.sf[:], ["sf"], ["so"])
+        cast(1)
+        scatter(4)
+        scatter(3)
         quant(hc, hs, 0, K, T.ht[:], ["ht%d" % b for b in four], ["ho"])
         send(partner, "ah%d" % t, [(hc[:, K:C].bitcast(dt.uint8), hc[:, 0:K].bitcast(dt.uint8)), (hs[:, K:C], hs[:, 0:K])], ["ho"])
         arrives(giver, "ah%d" % t, 2, ["hl"])
+        for q in (2, 1, 0): scatter(q)
         for b in four:
             mm(4 + b, T.ec, T.es, 128 * b, hc, hs, 0, K, ["ec", "ho"])
             copy("S", T.est[:, EW * b:EW * b + K], ps(4 + b, 0, K), ["ps%d" % (4 + b)], ["eo%d" % b])
-        for e in range(2): tt(T.ku[:, e:10:2], T.kp[:, K * e + 31:K * e + K:32], T.uu[:, e:10:2], ALU.mult, ["kp", "uu"], ["ku%d" % e])
-        for e in range(2):
-            ts(T.so[:, e:10:2], T.ku[:, e:10:2], T.dm[:, e:e + 1], ALU.add, r=["ku%d" % e, "dm", "dm1"], w=["so%d" % e])
-        for q in range(4, -1, -1):
-            h = q % 2
-            copy("V", T.sw[:, 512 * h:512 * h + 512].indirect(T.so[:, 2 * q:2 * q + 2]), T.val[:, 32 * q:32 * q + 32], ["so0", "so1", "val"], ["sw%d" % h])
 
-        def first(h, i, a, b, c): scan(T.ns[:, PL * h + K * i:PL * h + K * i + K], T.rs16[:], T.sw[:, 512 * h + a:512 * h + b:c], 0.0, ALU.mult, ALU.add,
-                                       ["sw%d" % h, "rs16"], ["ns%d_%d" % (i, h)])
+        def first(h, i, a, b, c):
+            o = SW * h + SH
+            scan(T.ns[:, PL * h + K * i:PL * h + K * i + K], T.c16[:], T.sw[:, o + a:o + b:c], 0.0, ALU.mult, ALU.max, ["sw%d" % h, "c16"], ["ns%d_%d" % (i, h)])
 
         def both(o, i, w): tt(o, T.ns[:, K * i + 15:K * i + K:16], T.ns[:, PL + K * i + 15:PL + K * i + K:16], ALU.max, ["ns%d_0" % i, "ns%d_1" % i], [w])
         first(1, 2, C, PL, 1)
-        first(1, 1, 1, C, 2)
         first(0, 2, C, PL, 1)
+        first(1, 1, 1, C, 2)
         first(0, 1, 1, C, 2)
         both(gs[:, 0:10], 2, "gs")
         send(partner, "ag%d" % t, [(gl[:, 0:10], gs[:, 0:10])], ["gs"])
@@ -368,40 +401,27 @@ def rank_program(g, core, T, topo):
         both(T.nn[:, 10:20], 1, "nn1")
         first(1, 0, 0, C, 2)
         first(0, 0, 0, C, 2)
-        ts(T.offo[:, 0:10], T.nn[:, 10:20], -1.0, ALU.mult, float(K), ALU.add, ["nn1"], ["offo"])
+        ts(T.offo[:, 0:10], T.nn[:, 10:20], pf(13), ALU.mult, K + 0.4, ALU.add, ["nn1", "pf13"], ["offo"])
         both(T.nn[:, 0:10], 0, "nn0")
-        final = t == R - 1
         for b in four:
             o = T.xf[:, 4 + b::8] if final else T.xt[:, 4 * K + b:4 * C:4]
-            tt(o, T.est[:, EW * b:EW * b + K + 1].indirect(T.offo[:, 0:10]), T.vp[:, PL * b + 1:PL * b + C:2], ALU.add,
+            tt(o, T.est[:, EW * b:EW * b + K + 1].indirect(T.offo[:, 0:10]), T.vp[:, PV * b + SH + 1:PV * b + SH + C:2], ALU.add,
                ["offo", "eo%d" % b, "ez%d" % b, "vp%d_1" % b], ["yo%d" % b if final else "xo%d" % b])
-            if b == 2: ts(T.ff[:, 0:10], T.nn[:, 0:10], 0.0, ALU.is_gt, float(OWN), ALU.mult, ["nn0"], ["ff"])
-
-        def given(b): copy("VVSS"[b], T.est[:, EW * b + OWN:EW * b + OWN + K], ps(4 + b, 0, K), ["ps%d" % (4 + b)], ["eg%d" % b])
-
-        def own_first():
-            tt(T.oo[:, 0:10], T.ff[:, 0:10], T.nn[:, 0:10], ALU.add, ["ff", "nn0"], ["oo"])
-            for b in (0, 2, 1, 3):
-                mm(4 + b, T.ec, T.es, 128 * b, hc, hs, K, K, ["ec", "hl"])
-                if b > 1: given(b)
-        if final:
-            copy("V", T.opi[:], T.out1[:], ["out1"], ["opi"])
-            own_first()
-            ts(T.opj[:], T.opi[:], 511, ALU.bitwise_and, r=["opi"], w=["opj"])
-            quant(T.vc, T.vs, 0, 128, T.vin[:], ["vin"], ["vc"])
-            copy("V", T.opf[:], T.opj[:], ["opj"], ["opf"])
-            dma("Y", "dop", [(T.op[2 * q + h, :], T.opf[32 * q:32 * q + 5, 32 * h:32 * h + 32]) for q in four for h in range(2)], ["opf"])
-        else:
-            odd_scores(t + 1, own_first)
-            lev1(0, 0)
+            if b == 1: ts(T.ff[:, 0:10], T.nn[:, 0:10], pf(14), ALU.is_ge, pf(15), ALU.mult, ["nn0", "pf14", "pf15"], ["ff"])
+            if b == 2: tt(T.oo[:, 0:10], T.ff[:, 0:10], T.nn[:, 0:10], ALU.add, ["ff", "nn0"], ["oo"])
+        for b in four:
+            mm(4 + b, T.ec, T.es, 128 * b, hc, hs, K, K, ["ec", "hl"])
+            copy("S", T.est[:, EW * b + OWN:EW * b + OWN + K], ps(4 + b, 0, K), ["ps%d" % (4 + b)], ["eg%d" % b])
         tt(T.em[:, 0:10], T.oo[:, 0:10], gl[:, 0:10], ALU.max, ["oo", "gl"], ["em"])
-        given(0)
-        ts(T.offe[:, 0:10], T.em[:, 0:10], -1.0, ALU.mult, float(OWN + K), ALU.add, ["em"], ["offe"])
-        given(1)
+        if not final:
+            for i in range(3): repeat(i)
+            odd_columns(t + 1)
+        ts(T.offe[:, 0:10], T.em[:, 0:10], pf(13), ALU.mult, OWN + K + 0.4, ALU.add, ["em", "pf13"], ["offe"])
         for b in four:
             o = T.xf[:, b::8] if final else T.xt[:, b:4 * K:4]
-            tt(o, T.est[:, EW * b:EW * b + OWN + 1 + K].indirect(T.offe[:, 0:10]), T.vp[:, PL * b:PL * b + C:2], ALU.add,
+            tt(o, T.est[:, EW * b:EW * b + OWN + 1 + K].indirect(T.offe[:, 0:10]), T.vp[:, PV * b + SH:PV * b + SH + C:2], ALU.add,
                ["offe", "eo%d" % b, "eg%d" % b, "ez", "ez%d" % b, "vp%d_0" % b], ["ye%d" % b if final else "xe%d" % b])
+        if not final: repeated_columns(t + 1)
 
     quant(T.fc, T.fs, 0, C, T.xf[:], ["ye%d" % b for b in four] + ["yo%d" % b for b in four], ["fc"])
     for h in range(2): mm(h, T.vc, T.vs, 0, T.fc, T.fs, K * h, K, ["vc", "fc"])
@@ -411,5 +431,4 @@ def rank_program(g, core, T, topo):
     dma("S", "dy", [(T.y[:], T.ysb[:])], ["ysb0", "ysb1"])
     for s in sorted(count, key=lambda s: s in DMAS):
         if waited.get(s, 0) < count[s]:
-            e = s[0].upper() if s not in DMAS and s[0].upper() in POOL and s != "sent" else "G"
-            Q[e].wait_ge(T.sem[s], count[s])
+            Q[s[0].upper() if s in ("v0", "s0", "p0") else "G"].wait_ge(T.sem[s], count[s])

@@ -15,23 +15,23 @@ PV, SW = PL + SH, 640
 X4, U8, BF, F32, F16, I32, U16 = "float8_e4m3fn_x4", "uint8", "bfloat16", "float32", "float16", "int32", "uint16"
 SCRATCH = {"ps": ("psum", [128, 4096], F32)}
 for _d, _l in {
-    BF: dict(xin=1280, xt=4 * LAND, xf=1280, vin=512, et=2048, one=128, idn=128, vp=4 * PV, zt=640, ht=640, est=4 * EW,
-             sval=K, eq=C, kp=C, cm=C, cb=64, i16=K, c16=K, ca=K, cc=K, sw=2 * SW, ns=2 * PL, d0=2400),
+    BF: dict(xin=1280, xt=4 * LAND, xf=1280, vin=512, et=516, vp=4 * PV, zt=640, ht=640, est=4 * EW,
+             sval=K, ao=C, eq=C, kp=C, cm=C, cb=64, i16=K, c16=K, ca=K, cc=K, sw=2 * SW, ns=2 * PL, d0=1920),
     X4: dict(lc=512, vc=128, ec=512, fc=C, zc=K, wc0=576, wc1=576, wc2=576, hc0=C, hc1=C, hc2=C),
     U8: dict(ls=512, vs=128, es=512, fs=C, zs=K, ws0=576, ws1=576, ws2=576, hs0=C, hs1=C, hs2=C),
-    F32: dict(ysb=C, s1=PL, sa=448, m1=8 * W1, cv=192, md=8 * W3, big=192, mk1=K, mk2=32, neg32=32, b2=96, bb=8 * WD,
+    F32: dict(ysb=C, s1=PL, sa=448, m1=8 * W1, cv=192, md=8 * W3, big=192, mk1=K, mk2=32,
               idt=512, x1=K, sf=16, nn=20, ff=16, oo=16, em=16, pf=24, sxi=20, opf=64,
               gs0=16, gs1=16, gs2=16, gl0=16, gl1=16, gl2=16),
-    F16: dict(neg=240, d1=2400, k1=2400, n1=8 * WA, n2=8 * WK, in1=64, out1=64, o32=64),
+    F16: dict(neg=240, b2=64, bb=8 * WD, d1=1920, k1=1920, n1=8 * WA, n2=8 * WK, in1=64, out1=64, o32=64),
     I32: dict(lw0=16, lwi=16, pi=8, opi=64, opj=64),
     U16: dict(lwu=16, so=16, offe=16, offo=16, selk=2, selb=4, selx=20),
 }.items():
     for _k, _n in _l.items(): SCRATCH[_k] = ("sbuf", [128, _n], _d)
 DMAS = ["dx", "dl", "dls", "dv", "dop", "doc", "dos", "dy"]
 SEMAPHORES = ["v0", "s0", "p0", "g0"] + DMAS + ["sent"] + ["%s%d" % (k, t) for k in ("at", "ah", "ag") for t in range(R)]
-ORDER = """X0 L0 X1 L1 X2 L2 X3 L3 X4 H0 X5 H1 X6 H2 X7 S0 H3 c0 A0 A1 A2 A3 H4 P0 H5 P1 E1 H6 P2 H7 P3 E3
-Q0 P4 Q1 G1 P5 E5 Q2 P6 Q3 G3 P7 F0 F1 Q4 Q5 F2 G5 F3 k0 Q6 k1 Q7 G7 c1 k2 k3 a0 k4 a1 n0 b0 n1 a2 n2 b1 T0 n3 g0 a3 n4 b2 n5 g1 a4 n6 M0
-b3 n7 T1 M1 a5 g2 U0 M2 b4 M3 U1 a6 M4 b5 T2 M5 U2 a7 M6 b6 M7 b7 U3 T3"""
+ORDER = """L0 X0 L1 X1 H0 X2 L2 X3 H1 X4 c2 L3 X5 H2 X6 H3 X7 S0 c0 A0 A1 A2 A4 S1 H4 c3 P0 H5 P1 E1 H6 P2 H7 P3 E3 O0
+Q0 P4 Q1 P5 E5 Q2 P6 Q3 P7 F0 F1 F2 F3 G1 G3 Q4 Q5 G5 k0 Q6 k1 Q7 G7 c4 c1 k2 a0 k4 a1 n0 b0 n1 a2 n2 b1 n3 g0 T0 a3 n4 b2 n5 a4 n6
+b3 M0 n7 g1 T1 a5 M1 U0 b4 M2 a6 M3 U1 b5 M4 T2 a7 M5 U2 b6 M6 b7 M7 T3 U3"""
 
 
 def rank_program(g, core, T, topo):
@@ -134,73 +134,77 @@ def rank_program(g, core, T, topo):
     four, eight = range(4), range(8)
     pf = lambda c: T.pf[:, c:c + 1]
     j, qq = pf(1), pf(2)
-    ET = ["et%d" % b for b in four]
+    ET = ["et0"]
     quarter = lambda q: slice(32 * q, 32 * q + 32)
     BP, BO, LO = 8, 48, 128
     XE, XO = ["xe%d" % b for b in four], ["xo%d" % b for b in four]
-    F = ["f%d" % i for i in range(8)]
+    F = ["f%d" % i for i in range(9)]
     IN = ["in%d_%d" % (q, i) for q in four for i in range(5)]
 
     dma("Y", "dx", [(T.xin[:], T.x[:])], (), ["xin"])
-    fill(T.one[:], 1.0, ["one"])
     iota(T.pi[:, 0:1], [[0, 1]], 0, 1, ["pi0"], False)
-    select(T.idn[:], T.one[:], [[-1, 128]], ALU.is_equal, 0.0, 0, 1, ["one"], ["idn"])
     iota(T.idt[:], [[1, 512]], 0, 0, ["idt"])
     fill(T.et[:], 0.0, ["et"])
     fill(T.big[:], BIG, ["big"])
-    for b in four: copy("S", T.et[:, 513 * b:512 * (b + 1):4], T.idn[:], ["idn", "et"], ["et%d" % b])
     select(T.mk1[:], T.big[:, 0:K], [[-1, K]], ALU.not_equal, -BIG, 0, 1, ["big"], ["mk1"])
     for c, (sh, m) in enumerate([(0, 15), (5, 3), (0, 1), (1, 7), (5, 1), (6, 1)]):
         ts(T.pi[:, c + 1:c + 2], T.pi[:, 0:1], sh, ALU.logical_shift_right, m, ALU.bitwise_and, ["pi0"], ["pi%d" % (c + 1)])
     fill(T.m1[:, 0::W1], -BIG, ["c0"])
     copy("V", T.pf[:, 0:7], T.pi[:, 0:7], ["pi%d" % c for c in range(7)], ["pf"])
     fill(T.m1[:, 4 * W1 + HI::W1], -BIG, ["c1"])
-    fill(T.md[:, 0::W3], -BIG, ["c2"])
     fill(T.m1[:, LOW::W1], -BIG, ["c3"])
     ts(pf(16), pf(5), float(K), ALU.mult, pf(6), ALU.add, ["pf"], ["pf16"])
     ts(pf(17), qq, 40.0 / 512, ALU.mult, (C + SH) / 512, ALU.add, ["pf"], ["pf17"])
     ts(pf(18), qq, 40.0, ALU.mult, j, ALU.add, ["pf"], ["pf18"])
-    op("V", lambda: V.memset(T.neg32[:], -KB), ["c0", "c1", "c2", "c3", "big"], ["cst"])
+    op("V", lambda: V.memset(T.md[:, 0::W3 + 4], -BIG), ["c0", "c1", "c3", "big"], ["cst"])
+    ts(T.et[:, 3:515:4], T.idt[:, 0:128], pf(0), ALU.is_equal, r=["idt", "pf", "et"], w=ET)
     ts(pf(16), pf(16), float(SH), ALU.add, 1.0 / 512, ALU.mult, ["pf16"], ["pf16"])
-    quant(T.ec, T.es, 0, 512, T.et[:], ET, ["ec"])
-    copy("V", T.mk2[96:128, :], T.mk1[0:32, 0:32], ["mk1"], ["mk2"])
-    for i, a in enumerate([T.idt[:, 1:C:2], T.idt[:, 0:C:2], T.idt[:, C:PL]]): affine(T.d1[:, 640 * i + 3:640 * i + 640:4], a, 1.0 / 512, SH / 512, ["idt"], ["f%d" % i])
-    affine(T.d1[:, 4 * PL + 3:4 * PL + 160:4], T.idt[:, 0:40], 1.0 / 512, pf(17), ["idt", "pf17"], ["f4"])
-    affine(T.d1[:, 4 * PL + 163::4], T.idt[:, 0:K:2], 1.0 / 512, pf(16), ["idt", "pf16"], ["f5"])
-    iota(T.i16[:], [[0, 10], [1, 16]], 0, 0, ["i16"])
+    ts(pf(18), pf(18), -8.0, ALU.add, r=["pf18"], w=["pf18"])
+    ts(pf(19), j, 15.0, ALU.is_equal, r=["pf"], w=["pf19"])
+    for b in four: quant(T.ec, T.es, 128 * b, 128 * b + 128, T.et[:, 3 - b:515 - b], ET, ["ec%d" % b])
+    for c, a in enumerate([T.idt[:, 1:C:2], T.idt[:, 0:C:2], T.idt[:, C:PL]]):
+        affine(T.d1[:, PL * c + 2:PL * c + PL:3], a, 1.0 / 512, 1 + SH / 512, ["idt"], ["f%d" % c])
+    affine(T.d1[:, 3 * PL + 3:3 * PL + 160:4], T.idt[:, 0:40], 1.0 / 512, pf(17), ["idt", "pf17"], ["f4"])
+    affine(T.d1[:, 3 * PL + 163::4], T.idt[:, 0:K:2], 1.0 / 512, pf(16), ["idt", "pf16"], ["f5"])
     for b in four: copy("VVVS"[b], T.xt[:, b:4 * K:4], T.xin[:, b::8], ["xin"], ["xe%d" % b])
     for b in range(2): copy("S", T.xt[:, 4 * K + b:4 * C:4], T.xin[:, 4 + b::8], ["xin"], ["xo%d" % b])
 
+    def const(o, m, c, r, w): affine(o, T.et[:, 0:m], 0.0, c, ET + r, w)
+
     def constants(i):
         if i == 0:
-            fill(T.d1[:, 1::4], 2.0, ["f3"])
-            ts(pf(18), pf(18), -8.0, ALU.add, r=["pf18"], w=["pf18"])
+            const(T.d1[:, 3 * PL + 1::4], 120, 2.0, [], ["f3"])
+            copy("V", T.mk2[96:128, :], T.mk1[0:32, 0:32], ["mk1"], ["mk2"])
             fill(T.in1[:], 0.0, IN)
-        if i == 1:
+            for c, (o, m) in enumerate([(T.n1[:, 0::WA], 8), (T.n2[:, 0::WK], 8), (T.bb[:, 0::WD], 8), (T.b2[:], 64)]): const(o, m, KB, [], ["c%d" % (5 + c)])
             ts(T.selb[:, 0:3], T.idt[:, 0:48:16], pf(18), ALU.add, 0.0, ALU.max, ["idt", "pf18"], ["selb"])
-            for c, o in enumerate([T.n1[:, 0::WA], T.n2[:, 0::WK], T.bb[:, 0::WD], T.b2[:]]): fill(o, KB, ["c%d" % (5 + c)])
         if i == 2:
-            op("V", lambda: V.memset(T.neg[:], -KB), ["c5", "c6", "c7", "c8"], ["ck"])
-            ts(pf(7), j, 1.0, ALU.add, r=["pf"], w=["pf7"])
-            ts(pf(8), j, 4.0, ALU.mult, 512.0, ALU.add, ["pf"], ["pf8"])
-            ts(pf(9), j, 4.0, ALU.mult, 576.0, ALU.add, ["pf"], ["pf9"])
-            ts(pf(19), j, 15.0, ALU.is_equal, r=["pf"], w=["pf19"])
-            for i, (at, by) in enumerate([(j, 4096.0), (j, pf(8)), (pf(7), 4096.0), (j, pf(9))]):
-                ts(T.cb[:, 16 * i:16 * i + 16], T.i16[:, 0:16], at, ALU.is_equal, by, ALU.mult, ["i16", "pf7", "pf8", "pf9"], ["cb%d" % i])
-            ts(pf(12), pf(19), 1 - 2.0 ** -12, ALU.mult, 2.0 ** -12, ALU.add, ["pf19"], ["pf12"])
-            ts(pf(10), pf(3), float(K), ALU.mult, 31.0, ALU.add, ["pf"], ["pf10"])
-            ts(T.cb[:], T.cb[:], 1.0, ALU.max, r=["cb%d" % i for i in four], w=["cb"])
-            ts(pf(13), pf(19), -511.0 / 512, ALU.mult, -1.0 / 512, ALU.add, ["pf19"], ["pf13"])
-            ts(pf(14), pf(19), -255.5, ALU.mult, 256.0, ALU.add, ["pf19"], ["pf14"])
-            ts(pf(15), pf(19), -511.0 * OWN, ALU.mult, 512.0 * OWN, ALU.add, ["pf19"], ["pf15"])
-            ts(T.cb[:, 0::32], T.cb[:, 0::32], 0.0, ALU.mult, r=["cb"], w=["cc0"])
-            ts(T.cb[:, 16:17], T.cb[:, 16:17], 2.0 ** -12, ALU.mult, r=["cb"], w=["cc1"])
-            ts(T.cb[:, 48:49], T.cb[:, 48:49], pf(12), ALU.mult, r=["cb", "pf12"], w=["cc2"])
-            for i in range(10):
-                select(T.cm[:, 32 * i:32 * i + 32], T.cb[:, 32 * (i // 5):32 * (i // 5) + 32], [[0, 32]], ALU.is_equal, 0.0, 0, 0, ["cc0", "cc1", "cc2"], ["cm%d" % i])
+            affine(pf(7), j, 1.0, 1.0, ["pf"], ["pf7"])
+            affine(pf(8), j, 4.0, 512.0, ["pf"], ["pf8"])
+            affine(pf(9), j, 4.0, 576.0, ["pf"], ["pf9"])
+            affine(pf(12), pf(19), 1 - 2.0 ** -12, 2.0 ** -12, ["pf19"], ["pf12"])
         if i == 3:
-            whole(T.d0[:, 0::4], 600, 0, ["f6"])
-            whole(T.d0[:, 3::4], 600, 1, ["f7"])
+            for c, (at, by) in enumerate([(j, 4096.0), (j, pf(8)), (pf(7), 4096.0), (j, pf(9))]):
+                ts(T.cb[:, 16 * c:16 * c + 16], T.i16[:, 0:16], at, ALU.is_equal, by, ALU.mult, ["i16", "pf7", "pf8", "pf9"], ["cb%d" % c])
+            ts(T.ca[:], T.i16[:], j, ALU.not_equal, r=["i16", "pf"], w=["ca"])
+            ts(T.cc[:], T.i16[:], pf(7), ALU.is_equal, 512.0, ALU.mult, ["i16", "pf7"], ["cc"])
+            op("V", lambda: V.memset(T.neg[:], -KB), ["c5", "c6", "c7", "c8"], ["ck"])
+            ts(T.cb[:], T.cb[:], 1.0, ALU.max, r=["cb%d" % c for c in four], w=["cb"])
+        if i == 4:
+            affine(T.cb[:, 0::32], T.cb[:, 0::32], 0.0, 0.0, ["cb"], ["cc0"])
+            affine(T.cb[:, 16:17], T.cb[:, 16:17], 2.0 ** -12, 0.0, ["cb"], ["cc1"])
+            affine(T.cb[:, 48:49], T.cb[:, 48:49], pf(12), 0.0, ["cb", "pf12"], ["cc2"])
+            for c in range(10):
+                select(T.cm[:, 32 * c:32 * c + 32], T.cb[:, 32 * (c // 5):32 * (c // 5) + 32], [[0, 32]], ALU.is_equal, 0.0, 0, 0, ["cc0", "cc1", "cc2"], ["cm%d" % c])
+            affine(pf(10), pf(3), float(K), 31.0, ["pf"], ["pf10"])
+            affine(pf(13), pf(19), -511.0 / 512, -1.0 / 512, ["pf19"], ["pf13"])
+            affine(pf(14), pf(19), -255.5, 256.0, ["pf19"], ["pf14"])
+            affine(pf(15), pf(19), -511.0 * OWN, 512.0 * OWN, ["pf19"], ["pf15"])
+        if i == 1:
+            iota(T.i16[:], [[0, 10], [1, 16]], 0, 0, ["i16"])
+            whole(T.d0[:, 0:3 * PL:3], PL, 0, ["f6"])
+            whole(T.d0[:, 3 * PL::4], 120, 0, ["f7"])
+            whole(T.d0[:, 3 * PL + 3::4], 120, 1, ["f8"])
             iota(T.sxi[:], [[1, 2], [2, 5], [0, 2]], 0, 0, ["sxi"])
             iota(T.sval[:], [[-1, K]], K, 0, ["sval"])
             for b in four:
@@ -209,18 +213,20 @@ def rank_program(g, core, T, topo):
             whole(T.est[:, OWN + K::EW], 4, 0, ["ez"])
 
     spare_first = [lambda: ts(pf(11), pf(4), 32.0, ALU.mult, pf(10), ALU.add, ["pf10"], ["pf11"]),
-                   lambda: ts(T.ca[:], T.i16[:], j, ALU.not_equal, r=["i16", "pf"], w=["ca"]),
-                   lambda: ts(T.cc[:], T.i16[:], pf(7), ALU.is_equal, 512.0, ALU.mult, ["i16", "pf7"], ["cc"]),
                    lambda: copy("V", T.selx[:], T.sxi[:], ["sxi"], ["selx"]),
+                   lambda: tt(T.c16[:, 0:80], T.ca[:, 0:80], T.cc[:, 0:80], ALU.max, ["ca", "cc"], ["c16a"]),
                    lambda: ts(T.selk[:, 0:1], pf(11), float(C - 1), ALU.min, r=["pf11"], w=["selk"]),
-                   lambda: tt(T.c16[:], T.ca[:], T.cc[:], ALU.max, ["ca", "cc"], ["c16"])]
+                   lambda: tt(T.c16[:, 80:K], T.ca[:, 80:K], T.cc[:, 80:K], ALU.max, ["ca", "cc", "c16a"], ["c16"]), None]
     spare_last = [lambda: quant(T.vc, T.vs, 0, 128, T.vin[:], ["vin"], ["vc"]), None,
                   lambda: ts(T.opi[:], T.out1[:], 512.0, ALU.mult, r=["out1"], w=["opi"]),
                   lambda: ts(T.opj[:], T.opi[:], 511, ALU.bitwise_and, r=["opi"], w=["opj"]),
                   lambda: ts(T.opf[:], T.opj[:], -float(SH), ALU.add, r=["opj"], w=["opf"]),
                   lambda: dma("Y", "dop", [(T.op[2 * q + h, :], T.opf[32 * q:32 * q + 5, 32 * h:32 * h + 32]) for q in four for h in range(2)], ["opf"])]
 
-    def repeat(i): copy("S", T.xt[:, 4 * (C + 32 * i):4 * (C + 32 * i + 32)], T.xt[:, 4 * 288:4 * C], XO, ["xr%d" % i])
+    def repeat(i, e):
+        o, a = T.xt[:, 4 * (C + 32 * i):4 * (C + 32 * i + 32)], T.xt[:, 4 * 288:4 * C]
+        if e == "G": select(o, a, [[0, 128]], ALU.is_equal, 0.0, 0, 0, XO, ["xr%d" % i])
+        else: copy(e, o, a, XO, ["xr%d" % i])
 
     def odd_columns(t):
         wc, ws = wcs[t]
@@ -233,12 +239,13 @@ def rank_program(g, core, T, topo):
         mm(3, wc, ws, 288, wc, ws, K, K, ["wo", "wr"])
         for q in (3, 2): copy("S", T.sa[quarter(q), BO:BO + 80], ps(3, 80 * q - K, 80 * q - 80, 32 * q, 32 * q + 32), ["ps3"], ["s2_%d" % q])
 
-    def best_places(t):
+    def best_places(t, near):
         wc, ws = wcs[t]
         big = T.big[:, 0:K]
         S1, S2 = ["s1_0", "s1_1", "s1_2"], ["s2_%d" % q for q in four]
         CV = ["cva", "cvb0", "cvb1"] + ["cvc%d" % q for q in four]
-        slot = {1: (T.d1, 0), 3: (T.d0, 2), 5: (T.d0, 1), 7: (T.d1, 2)}
+        slot = {1: (T.d1, 1), 3: (T.d1, 0), 5: (T.d0, 2), 7: (T.d0, 1)}
+        slot2 = {1: (T.d1, 0), 3: (T.d0, 2), 5: (T.d0, 1), 7: (T.d1, 2)}
 
         def low(k): level(T.m1, W1, k, LOW, K, T.sa[:, LO:LO + K], big, -BIG, UP, ["lo"] + below("l%d", k), "l%d" % k)
         def high(k): level(T.m1, W1, k, HI, K, T.sa[:, LO + K:LO + C], big, -BIG, UP, ["hi", "l%d" % min(k, 3)] + below("h%d", k), "h%d" % k)
@@ -247,20 +254,28 @@ def rank_program(g, core, T, topo):
         def signs(k, c=None):
             d, a = slot[k]
             c, m = (0, PL) if c is None else (120 * c, 120)
-            sign(d[:, 4 * c + a:4 * (c + m):4], T.s1[:, c:c + m], T.m1[:, k * W1 + PA + K:k * W1 + PA + K + 1], S1 + ["p%d" % k], ["e1_%d_%d" % (k, c // 120)])
+            sign(d[:, 3 * c + a:3 * (c + m):3], T.s1[:, c:c + m], T.m1[:, k * W1 + PA + K:k * W1 + PA + K + 1], S1 + ["p%d" % k], ["e1_%d_%d" % (k, c // 120)])
 
-        def own2(k): level(T.m1, W1, k, 0, 80, T.sa[:, BO:BO + 80], T.big[:, 0:80], -BIG, UP, S2 + below("x%d", k), "x%d" % k)
-        def far2(k): level(T.md, W3, k, 0, 192, T.cv[:], T.big[:], -BIG, UP, CV + ["cvp"] + below("md%d", k), "md%d" % k)
+        def own2(k):
+            o = (7 - k) * W1
+            scan(T.m1[:, o + 1:o + 81], T.sa[:, BO:BO + 80], T.m1[:, o + W1:o + W1 + 80] if k else T.big[:, 0:80], -BIG, ALU.max, ALU.min,
+                 S2 + below("x%d", k) + ["cst"], ["x%d" % k])
+
+        def far2(k): level(T.md, W3, k, 4 * k, 192 - 4 * k, T.cv[:, 4 * k:], T.big[:], -BIG, UP, CV + ["cvp"] + below("md%d", k), "md%d" % k)
 
         def signs2(k):
-            d, a = slot[k]
-            sign(d[:, 4 * PL + a::4], T.sa[:, BP:BP + 120], T.md[:, k * W3 + 192:k * W3 + 193], S2 + ["s2p", "md%d" % k], ["e2_%d" % k])
+            d, a = slot2[k]
+            sign(d[:, 3 * PL + a::4], T.sa[:, BP:BP + 120], T.md[:, k * W3 + 192:k * W3 + 193], S2 + ["s2p", "md%d" % k], ["e2_%d" % k])
 
-        def spread(_):
+        def lift(_): affine(T.d1[:, 1:3 * PL:3], T.d1[:, 1:3 * PL:3], -1.0, 3.0, [], ["e1_1_0"])
+
+        def spread(i):
+            if near != i: return
             X8 = ["x%d" % k for k in eight]
-            copy("S", T.cv[:, 0:8], T.m1[:, 80::W1], X8, ["cva"])
-            for h in range(2): copy("S", T.cv[64 * h:64 * h + 64, 8:16], T.m1[64 - 64 * h:128 - 64 * h, 80::W1], X8, ["cvb%d" % h])
-            for q in four: copy("S", T.cv[quarter(q), 16:32], T.cv[quarter(q ^ 1), 0:16], ["cva", "cvb0", "cvb1"], ["cvc%d" % q])
+            copy("S", T.cv[:, 0:32:4], T.m1[:, 80::W1], X8, ["cva"])
+            for h in range(2): copy("S", T.cv[64 * h:64 * h + 64, 2:32:4], T.m1[64 - 64 * h:128 - 64 * h, 80::W1], X8, ["cvb%d" % h])
+            if near: arrived(3)
+            for q in four: copy("S", T.cv[quarter(q), 1:32:2], T.cv[quarter(q ^ 1), 0:32:2], ["cva", "cvb0", "cvb1"], ["cvc%d" % q])
 
         def arrived(i):
             if i == 0:
@@ -273,41 +288,44 @@ def rank_program(g, core, T, topo):
                     dma("Y", "dv", [(T.vin[:], T.v[:])], (), ["vin"])
             if i == 1: copy("S", T.cv[:, 32:], ps(0, 0, K), ["ps0"], ["cvp"])
             if i == 2: copy("S", T.s1[:, C:PL], ps(1, 0, K), ["ps1"], ["s1_2"])
-            if i == 3: copy("S", T.sa[:, 0:BO], T.cv[:, 32:].indirect(T.selb[:, 0:3]), ["cvp", "selb"], ["s2p"])
+            if i == 4 - near: copy("S", T.sa[:, 0:BO], T.cv[:, 32:].indirect(T.selb[:, 0:3]), ["cvp", "selb"], ["s2p"])
 
-        def keys(c): scan(T.k1[:, PL * c:PL * c + PL], T.d0[:, PL * c:PL * c + PL], T.d1[:, PL * c:PL * c + PL], 0.0, ALU.mult, ALU.add,
-                          F + (["e1_1_0", "e1_3_0", "e1_5_0", "e1_7_%d" % c] if c < 4 else ["e2_%d" % i for i in (1, 3, 5, 7)]), ["k%d" % c])
+        def keys(c):
+            run = slice(360 * c, 360 * c + {0: 360, 1: 360, 2: 720, 4: PL}[c])
+            scan(T.k1[:, run], T.d0[:, run], T.d1[:, run], 0.0, ALU.mult, ALU.add,
+                 F + (["e1_1_0", "e1_3_0", "e1_5_0", "e1_7_%d" % c, "e1_7_%d" % (c + c // 2)] if c < 4 else ["e2_%d" % i for i in (1, 3, 5, 7)]), ["k%d" % c])
 
         def key1(k, c=0):
-            level(T.n1, WA, k, 240 * c, 240, T.k1[:, 960 * c + 3:960 * c + 960:4], T.neg[:], KB, DOWN,
-                  ["ck", "k%d" % (2 * c), "k%d" % (2 * c + 1)] + below("n%d_" + str(c), k) + (["n%d_0" % k] if c else []), "n%d_%d" % (k, c))
+            level(T.n1, WA, k, 240 * c, 240, T.k1[:, 720 * c + 2:720 * c + 720:3], T.neg[:], KB, DOWN,
+                  ["ck", "k%d" % (2 * c), "k%d" % (c + 1)] + below("n%d_" + str(c), k) + (["n%d_0" % k] if c else []), "n%d_%d" % (k, c))
 
-        def key2(k): level(T.n2, WK, k, 0, 120, T.k1[:, 4 * PL + 3::4], T.neg[:, 0:120], KB, DOWN, ["ck", "k4"] + below("q%d", k), "q%d" % k)
+        def key2(k): level(T.n2, WK, k, 0, 120, T.k1[:, 3 * PL + 3::4], T.neg[:, 0:120], KB, DOWN, ["ck", "k4"] + below("q%d", k), "q%d" % k)
 
         def gather2(s):
-            m = 2 * s + 4
+            m = 4 * s + 4
             for q in four:
-                copy("VSVS"[q] if s == 2 else "S", T.b2[0:32, 32 * s + 8 * q:32 * s + 8 * q + m], T.n2[quarter(q), 120:m * WK:WK], ["ck", "q%d" % (m - 1)], ["b2_%d_%d" % (s, q)])
+                copy("S", T.b2[0:32, 32 * s + 8 * q:32 * s + 8 * q + m], T.n2[quarter(q), 120:m * WK:WK], ["ck", "q%d" % (m - 1)], ["b2_%d_%d" % (s, q)])
 
         def merge2(k):
-            s = max(k // 2 - 1, 0)
-            level(T.bb, WD, k, 0, 32, T.b2[0:32, 32 * s:32 * s + 32], T.neg32[0:32, :], KB, DOWN, ["b2_%d_%d" % (s, q) for q in four] + below("d%d", k), "d%d" % k, 32)
+            s = k // 4
+            level(T.bb, WD, k, 0, 32, T.b2[0:32, 32 * s:32 * s + 32], T.neg[0:32, 0:32], KB, DOWN, ["b2_%d_%d" % (s, q) for q in four] + below("d%d", k), "d%d" % k, 32)
 
         def turn(q):
             for i in four:
-                copy("VSVS"[i] if q == 3 else "S", T.in1[quarter(q), i::32], T.n1[quarter(i), 2 * q * WA + PL:(2 * q + 2) * WA:WA], ["n%d_1" % (2 * q + 1)], ["in%d_%d" % (q, i)])
+                copy("VVVS"[i] if q == 3 else "S", T.in1[quarter(q), i::32], T.n1[quarter(i), 2 * q * WA + PL:(2 * q + 2) * WA:WA], ["n%d_1" % (2 * q + 1)], ["in%d_%d" % (q, i)])
 
         def turn2(q): copy("V" if q == 3 else "S", T.in1[quarter(q), 4::32], T.bb[0:32, 2 * q * WD + 32:(2 * q + 2) * WD:WD], ["d%d" % (2 * q + 1)], ["in%d_4" % q])
 
         def beside(i):
+            if i > 1 and t == 0: constants(i)
             if i == 0:
                 for h in range(2): whole(T.sw[:, SW * h + SH:SW * h + PV], PL, 0, ["sw%d" % h])
             if i == 1:
                 for b in four:
-                    mm(4 + b, T.ec, T.es, 128 * b, wc, ws, LAND, K, ["ec", "wl"])
+                    mm(4 + b, T.ec, T.es, 128 * b, wc, ws, LAND, K, ["ec%d" % b, "wl"])
                     copy("S", T.vp[:, PV * b + SH + C:PV * b + PV], ps(4 + b, 0, K), ["ps%d" % (4 + b)], ["vp%d_2" % b])
         step = dict(L=low, H=high, P=far, E=signs, F=lambda c: signs(7, c), X=own2, Q=far2, G=signs2, S=spread, A=arrived, k=keys, a=key1,
-                    b=lambda k: key1(k, 1), n=key2, g=gather2, M=merge2, T=turn, U=turn2, c=beside)
+                    b=lambda k: key1(k, 1), n=key2, g=gather2, M=merge2, T=turn, U=turn2, c=beside, O=lift)
         for w in ORDER.split(): step[w[0]](int(w[1]))
 
     for t in range(R):
@@ -320,32 +338,27 @@ def rank_program(g, core, T, topo):
         send(giver, "at%d" % t, [(wc[:, LAND:].bitcast(dt.uint8), wc[:, 0:K].bitcast(dt.uint8)), (ws[:, LAND:], ws[:, 0:K])], ["we"])
         arrives(partner, "at%d" % t, 2, ["wl"])
         if t == 0:
-            constants(3)
+            constants(1)
             for b in (2, 3): copy("V", T.xt[:, 4 * K + b:4 * C:4], T.xin[:, 4 + b::8], ["xin"], ["xo%d" % b])
-            for i in range(3): repeat(i)
+            for i in range(3): repeat(i, "S")
             odd_columns(0)
             constants(0)
         mm(1, wc, ws, K, wc, ws, 0, K, ["wo", "we"])
         tt(T.s1[:, 0:K], ps(0, 0, K), T.mk1[:], ALU.min, ["ps0", "mk1"], ["s1_0"])
-        if t == 0:
-            repeated_columns(0)
-            constants(1)
+        if t == 0: repeated_columns(0)
         mm(0, wc, ws, 288, wc, ws, 0, K, ["wo", "wr", "we"])
         mm(2, wc, ws, K, wc, ws, 0, K, ["wo", "we"])
         for q in range(2): copy("S", T.sa[quarter(q), BO:BO + 80], ps(0, 80 * q, 80 * q + 80, 32 * q, 32 * q + 32), ["ps0"], ["s2_%d" % q])
         copy("S", T.s1[:, K:C], ps(2, 0, K), ["ps2"], ["s1_1"])
         own = T.sa[96:128, BO + 48:BO + 80]
-        if t: tt(own, own, T.mk2[96:128, :], ALU.min, ["s2_3", "mk2"], ["s2_3"])
         tt(T.sa[:, LO:LO + K], ps(1, 0, K), T.s1[:, 0:K], ALU.min, ["ps1", "s1_0"], ["lo"])
         tt(T.sa[:, LO + K:LO + C], ps(1, 0, K), T.s1[:, 0:K], ALU.max, ["ps1", "s1_0"], ["hi"])
-        if t == 0:
-            tt(own, own, T.mk2[96:128, :], ALU.min, ["s2_3", "mk2"], ["s2_3"])
-            constants(2)
+        tt(own, own, T.mk2[96:128, :], ALU.min, ["s2_3", "mk2"], ["s2_3"])
         for b in four:
-            mm(4 + b, T.ec, T.es, 128 * b, wc, ws, 0, C, ["ec", "we", "wo", "wr"])
+            mm(4 + b, T.ec, T.es, 128 * b, wc, ws, 0, C, ["ec%d" % b, "we", "wo", "wr"])
             for e in range(2):
                 copy("S", T.vp[:, PV * b + SH + e:PV * b + SH + C:2], ps(4 + b, K * e, K * e + K), ["ps%d" % (4 + b)], ["vp%d_%d" % (b, e)])
-        best_places(t)
+        best_places(t, topo.chip(core) == topo.chip(partner))
         lw = T.lwu[:, 0:10]
         chain = [lambda: op("V", lambda: V.transpose(T.out1[:], T.in1[:]), IN, ["out1"]),
                  lambda: [op("V", lambda e=e: V.transpose(T.o32[:, e::2], T.out1[:, e::2]), ["out1"], ["o32_%d" % e]) for e in range(2)],
@@ -360,7 +373,7 @@ def rank_program(g, core, T, topo):
             copy("VVSS"[b], T.zt[:, b::4], T.vp[:, PV * b:PV * b + PV].indirect(lw), ["lwu", "vz%d" % b] + ["vp%d_%d" % (b, i) for i in range(3)], ["zt%d" % b])
         for e in range(2): tt(T.eq[:, K * e:K * e + K], T.lwi[:].indirect(T.selx[:, 10 * e:10 * e + 10]), T.x1[:], ALU.is_equal, ["lwi", "selx", "x1"], ["eq%d" % e])
         quant(T.zc, T.zs, 0, K, T.zt[:], ["zt%d" % b for b in four], ["zc"])
-        for b in four: mm(4 + b, T.lc, T.ls, 128 * b, T.zc, T.zs, 0, K, ["lc", "ls", "zc"])
+        for b in (0, 2, 1, 3): mm(4 + b, T.lc, T.ls, 128 * b, T.zc, T.zs, 0, K, ["lc", "ls", "zc"])
 
         def cast(b):
             if b < 2: ts(T.ht[:, b::4], ps(4 + b, 0, K), 0.03125, ALU.mult, r=["ps%d" % (4 + b)], w=["ht%d" % b])
@@ -376,14 +389,13 @@ def rank_program(g, core, T, topo):
         cast(0)
         copy("V", T.so[:], T.sf[:], ["sf"], ["so"])
         cast(1)
-        scatter(4)
-        scatter(3)
+        for q in (4, 3): scatter(q)
         quant(hc, hs, 0, K, T.ht[:], ["ht%d" % b for b in four], ["ho"])
         send(partner, "ah%d" % t, [(hc[:, K:C].bitcast(dt.uint8), hc[:, 0:K].bitcast(dt.uint8)), (hs[:, K:C], hs[:, 0:K])], ["ho"])
         arrives(giver, "ah%d" % t, 2, ["hl"])
         for q in (2, 1, 0): scatter(q)
         for b in four:
-            mm(4 + b, T.ec, T.es, 128 * b, hc, hs, 0, K, ["ec", "ho"])
+            mm(4 + b, T.ec, T.es, 128 * b, hc, hs, 0, K, ["ec%d" % b, "ho"])
             copy("S", T.est[:, EW * b:EW * b + K], ps(4 + b, 0, K), ["ps%d" % (4 + b)], ["eo%d" % b])
 
         def first(h, i, a, b, c):
@@ -394,33 +406,42 @@ def rank_program(g, core, T, topo):
         first(1, 2, C, PL, 1)
         first(0, 2, C, PL, 1)
         first(1, 1, 1, C, 2)
-        first(0, 1, 1, C, 2)
         both(gs[:, 0:10], 2, "gs")
         send(partner, "ag%d" % t, [(gl[:, 0:10], gs[:, 0:10])], ["gs"])
         arrives(giver, "ag%d" % t, 1, ["gl"])
-        both(T.nn[:, 10:20], 1, "nn1")
+        first(0, 1, 1, C, 2)
         first(1, 0, 0, C, 2)
+        both(T.nn[:, 10:20], 1, "nn1")
         first(0, 0, 0, C, 2)
         ts(T.offo[:, 0:10], T.nn[:, 10:20], pf(13), ALU.mult, K + 0.4, ALU.add, ["nn1", "pf13"], ["offo"])
         both(T.nn[:, 0:10], 0, "nn0")
+        for b in (2, 3):
+            mm(b, T.ec, T.es, 128 * b, wc, ws, K, K, ["ec%d" % b, "wo"])
+            copy("S", T.ao[:, K * b - C:K * b - K], T.est[:, EW * b:EW * b + K + 1].indirect(T.offo[:, 0:10]), ["offo", "eo%d" % b, "ez%d" % b], ["ao%d" % b])
         for b in four:
-            o = T.xf[:, 4 + b::8] if final else T.xt[:, 4 * K + b:4 * C:4]
-            tt(o, T.est[:, EW * b:EW * b + K + 1].indirect(T.offo[:, 0:10]), T.vp[:, PV * b + SH + 1:PV * b + SH + C:2], ALU.add,
-               ["offo", "eo%d" % b, "ez%d" % b, "vp%d_1" % b], ["yo%d" % b if final else "xo%d" % b])
+            o, w = (T.xf[:, 4 + b::8], ["yo%d" % b]) if final else (T.xt[:, 4 * K + b:4 * C:4], ["xo%d" % b])
+            if b > 1: tt(o, ps(b, 0, K), T.ao[:, K * b - C:K * b - K], ALU.add, ["ps%d" % b, "ao%d" % b], w)
+            else: tt(o, T.est[:, EW * b:EW * b + K + 1].indirect(T.offo[:, 0:10]), T.vp[:, PV * b + SH + 1:PV * b + SH + C:2], ALU.add,
+                     ["offo", "eo%d" % b, "ez%d" % b, "vp%d_1" % b], w)
             if b == 1: ts(T.ff[:, 0:10], T.nn[:, 0:10], pf(14), ALU.is_ge, pf(15), ALU.mult, ["nn0", "pf14", "pf15"], ["ff"])
             if b == 2: tt(T.oo[:, 0:10], T.ff[:, 0:10], T.nn[:, 0:10], ALU.add, ["ff", "nn0"], ["oo"])
         for b in four:
-            mm(4 + b, T.ec, T.es, 128 * b, hc, hs, K, K, ["ec", "hl"])
+            mm(4 + b, T.ec, T.es, 128 * b, hc, hs, K, K, ["ec%d" % b, "hl"])
             copy("S", T.est[:, EW * b + OWN:EW * b + OWN + K], ps(4 + b, 0, K), ["ps%d" % (4 + b)], ["eg%d" % b])
         tt(T.em[:, 0:10], T.oo[:, 0:10], gl[:, 0:10], ALU.max, ["oo", "gl"], ["em"])
         if not final:
-            for i in range(3): repeat(i)
+            for i in range(3): repeat(i, "G")
             odd_columns(t + 1)
         ts(T.offe[:, 0:10], T.em[:, 0:10], pf(13), ALU.mult, OWN + K + 0.4, ALU.add, ["em", "pf13"], ["offe"])
-        for b in four:
-            o = T.xf[:, b::8] if final else T.xt[:, b:4 * K:4]
-            tt(o, T.est[:, EW * b:EW * b + OWN + 1 + K].indirect(T.offe[:, 0:10]), T.vp[:, PV * b + SH:PV * b + SH + C:2], ALU.add,
-               ["offe", "eo%d" % b, "eg%d" % b, "ez", "ez%d" % b, "vp%d_0" % b], ["ye%d" % b if final else "xe%d" % b])
+        mm(1, T.ec, T.es, 384, wc, ws, 0, K, ["ec3", "we"])
+        for b in (3, 0, 1, 2, 4):
+            a = T.est[:, EW * b:EW * b + OWN + 1 + K].indirect(T.offe[:, 0:10]) if b < 4 else None
+            r = ["offe", "eo%d" % b, "eg%d" % b, "ez", "ez%d" % b]
+            c = min(b, 3)
+            o, w = (T.xf[:, c::8], ["ye%d" % c]) if final else (T.xt[:, c:4 * K:4], ["xe%d" % c])
+            if b == 3: copy("S", T.ao[:, 0:K], a, r, ["ao2"])
+            elif b == 4: tt(o, ps(1, 0, K), T.ao[:, 0:K], ALU.add, ["ps1", "ao2"], w)
+            else: tt(o, a, T.vp[:, PV * b + SH:PV * b + SH + C:2], ALU.add, r + ["vp%d_0" % b], w)
         if not final: repeated_columns(t + 1)
 
     quant(T.fc, T.fs, 0, C, T.xf[:], ["ye%d" % b for b in four] + ["yo%d" % b for b in four], ["fc"])

@@ -5,8 +5,8 @@ ACT = ActivationFunctionType
 C, K, PL, R = 320, 160, 480, 3
 BIG = 1e29
 KB = 100.0
-W1, W3, WA, WK, WD = 564, 196, 484, 124, 36
-LOW, HI, PA = 81, 241, 401
+W1, W3, WA, WK, WD = 484, 244, 484, 124, 36
+LOW, HI, PA = 1, 161, 321
 LAND = 416
 EW = 352
 OWN = 176
@@ -16,22 +16,36 @@ X4, U8, BF, F32, F16, I32, U16 = "float8_e4m3fn_x4", "uint8", "bfloat16", "float
 SCRATCH = {"ps": ("psum", [128, 4096], F32)}
 for _d, _l in {
     BF: dict(xin=1280, xt=4 * LAND, xf=1280, vin=512, et=516, vp=4 * PV, zt=640, ht=640, est=4 * EW,
-             sval=K, ao=C, eq=C, kp=C, cm=C, cb=64, i16=K, c16=K, ca=K, cc=K, sw=2 * SW, ns=2 * PL, d0=1920),
+             sval=K, ao=4 * K, ae=4 * K, eq=C, kp=C, cm=C, cb=64, i16=K, c16=K, ca=K, cc=K, sw=2 * SW, ns=2 * PL, d0=1800),
     X4: dict(lc=512, vc=128, ec=512, fc=C, zc=K, wc0=576, wc1=576, wc2=576, hc0=C, hc1=C, hc2=C),
     U8: dict(ls=512, vs=128, es=512, fs=C, zs=K, ws0=576, ws1=576, ws2=576, hs0=C, hs1=C, hs2=C),
-    F32: dict(ysb=C, s1=PL, sa=448, m1=8 * W1, cv=192, md=8 * W3, big=192, mk1=K, mk2=32,
+    F32: dict(ysb=C, s1=PL, sa=448, m1=8 * W1, cv=240, md=9 * W3, big=K, mk1=K, mk2=K, ob=16, vv=64,
               idt=512, x1=K, sf=16, nn=20, ff=16, oo=16, em=16, pf=24, sxi=20, opf=64,
               gs0=16, gs1=16, gs2=16, gl0=16, gl1=16, gl2=16),
-    F16: dict(neg=240, b2=64, bb=8 * WD, d1=1920, k1=1920, n1=8 * WA, n2=8 * WK, in1=64, out1=64, o32=64),
-    I32: dict(lw0=16, lwi=16, pi=8, opi=64, opj=64),
-    U16: dict(lwu=16, so=16, offe=16, offo=16, selk=2, selb=4, selx=20),
+    F16: dict(neg=240, b2=128, bb=8 * WD, d1=1800, k1=1800, n1=8 * WA, n2=8 * WK, in1=64, out1=64, o32=64),
+    I32: dict(lwi=16, pi=8, cl=4, cw=40),
+    U16: dict(lwu=16, so=16, offe=16, offo=16, selk=2, selb=8, selx=20),
 }.items():
     for _k, _n in _l.items(): SCRATCH[_k] = ("sbuf", [128, _n], _d)
 DMAS = ["dx", "dl", "dls", "dv", "dop", "doc", "dos", "dy"]
 SEMAPHORES = ["v0", "s0", "p0", "g0"] + DMAS + ["sent"] + ["%s%d" % (k, t) for k in ("at", "ah", "ag") for t in range(R)]
-ORDER = """L0 X0 L1 X1 H0 X2 L2 X3 H1 X4 c2 L3 X5 H2 X6 H3 X7 S0 c0 A0 A1 A2 A4 S1 H4 c3 P0 H5 P1 E1 H6 P2 H7 P3 E3 O0
-Q0 P4 Q1 P5 E5 Q2 P6 Q3 P7 F0 F1 F2 F3 G1 G3 Q4 Q5 G5 k0 Q6 k1 Q7 G7 c4 c1 k2 a0 k4 a1 n0 b0 n1 a2 n2 b1 n3 g0 T0 a3 n4 b2 n5 a4 n6
-b3 M0 n7 g1 T1 a5 M1 U0 b4 M2 a6 M3 U1 b5 M4 T2 a7 M5 U2 b6 M6 b7 M7 T3 U3"""
+ORDER = {
+    "V": """c0 xe xo we wo wr s1 own* lo own hi l0 x0 l1 x1 h0 l2 x2 h1 l3 x3 h2 c3 x4 h3 Q0 p0 x5 Q1 p1 Q2 h4 x6 Q3 h5 p2 Q4 x7 v1 p3 Q5 h6 Q6
+         p4 Q7 v3 p5 h7 p6 v5 v7 p7 u7 w7 k4 k0 k1 n0 k2 a0 n1 a1 b0 n2 a2 b1 n3 d0 a3 n4 b2 a4 n5 d1 b3 a5 n6 d2 b4 a6 d3 n7 b5 d4 c8 b6 d5
+         a7 w6 d6 b7 u6 d7 fl T3 U3 fr c9 c7 out1 c6 vc o32 lwu lwi""",
+    "S": "xe xo xr c2 r0 s11 c0 vp cv s2p s12 e1 ob4 lift g1 e3 g0 ob8 g3 e5 g5 g7 f0 f1 f2 f3 c4 j0 vq j1 j2 U0 U1 j3 T2 U2 opf",
+    "G": "c0 at c1 sw T0 T1 c4",
+    "P": "moo meo mor mer meo2 dt mpr mp mp2 dp",
+    "Y": "x w op"}
+NEAR = {
+    "V": """zt eq1 eq0 zc kp sf ht0 so ht1 sc4 sc3 sc2 ho sc1 sc0 n11 n21 n10 n20 n00 n01 nn1 gs nn0 offo ff xo1 xo0 oo xo2 xo3
+         em offe wo+ xe0 xe2 xe1 xe3 wr+ fc ysb""",
+    "S": "x1 zt ht2 ht3 eo ao eg ae ysb y",
+    "G": "ah ag xr+",
+    "P": "do mh de mo mg moo+ mor+ my",
+    "Y": "oc"}
+FAR = dict(NEAR, V="""zt eq1 eq0 zc kp sf ht0 so ht1 sc4 sc3 ho sc2 sc1 sc0 n21 n11 n20 n10 n01 n00 gs nn1 nn0 offo ff xo1 xo0 oo xo2 xo3
+         em offe wo+ xe1 xe2 xe0 xe3 wr+ fc ysb""")
 
 
 def rank_program(g, core, T, topo):
@@ -40,19 +54,13 @@ def rank_program(g, core, T, topo):
         return
     n = len(T.cores)
     Q = {"V": g.vector, "S": g.scalar, "P": g.tensor, "G": g, "Y": g.sync}
-    ops = []
-    known = {e: 0 for e in Q}
+    calls = []
     wr, rd = {}, {}
-    count, last, waited = {}, {}, {}
+    narrow = set()
+    now, step = [0], [None]
 
-    def wait(e, j):
-        if not known[e] >> j & 1:
-            s, c, k = ops[j]
-            Q[e].wait_ge(T.sem[s], c)
-            waited[s] = max(waited.get(s, 0), c)
-            known[e] |= k
-
-    def needs(e, r, w):
+    def record(e, issue, r, w):
+        r, w = ([x + str(now[0]) if x in ("we", "wo", "wl", "ho", "hl", "gs", "gl") else x for x in a] for a in (r, w))
         d = set()
         for t in r:
             if t in wr: d.add(wr[t])
@@ -60,40 +68,36 @@ def rank_program(g, core, T, topo):
         for t in w:
             if t in wr: d.add(wr[t])
             d.update(j for (q, j) in rd.get(t, []))
-        for j in sorted(d, reverse=True): wait(e, j)
-
-    def note(e, s, c, r, w):
-        j = len(ops)
-        ops.append((s, c, (known[e] | 1 << j if e else 1 << j) | (ops[last[s]][2] if s in last else 0)))
-        count[s], last[s] = c, j
-        for t in r: rd.setdefault(t, []).append((e, j))
+        calls.append((e, (step[0], now[0]), issue, d))
+        for t in r: rd.setdefault(t, []).append((e, len(calls) - 1))
         for t in w:
-            wr[t] = j
+            wr[t] = len(calls) - 1
             rd[t] = []
 
+    def at(name): step[0] = name
+
     def op(e, fn, r=(), w=()):
-        needs(e, r, w)
         s = e.lower() + "0"
-        fn().then_inc(T.sem[s], 1)
-        note(e, s, count.get(s, 0) + 1, r, w)
+        record(e, lambda: (fn().then_inc(T.sem[s], 1), s, 1), r, w)
 
     def dma(e, s, pairs, r=(), w=()):
-        needs(e, r, w)
-        for o, i in pairs: Q[e].dma_start(o, i).then_inc(T.sem[s], 16)
-        note(e, s, count.get(s, 0) + 16 * len(pairs), r, w)
+        record(e, lambda: ([Q[e].dma_start(o, i).then_inc(T.sem[s], 16) for o, i in pairs], s, 16 * len(pairs)), r, w)
 
-    def send(dst, s, pairs, r):
-        needs("G", r, ())
+    def exchange(dst, src, s, pairs, r, w):
         rid, pid, _ = topo.addr(dst)
-        for o, i in pairs:
-            g.remote_dma(o, i, T.sem[s], T.sem.sent, pid, rid, topo.mask(core, dst))
-            count["sent"] = count.get("sent", 0) + len(topo.engines(core, dst))
-
-    def arrives(src, s, calls, w): note(None, s, calls * len(topo.engines(src, core)), (), w)
+        at(s[:2])
+        record("G", lambda: ([g.remote_dma(o, a, T.sem[s], T.sem.sent, pid, rid, topo.mask(core, dst)) for o, a in pairs],
+                             "sent", len(pairs) * len(topo.engines(core, dst))), r, ())
+        record(None, lambda: (None, s, len(pairs) * len(topo.engines(src, core))), (), w)
     V, S = g.vector, g.scalar
 
-    def copy(e, o, i, r, w):
+    def select(o, i, pat, cmp, c, base, cm, r, w, part=False):
+        op("G", lambda: g.affine_select(o, i, pat, cmp, c, base, cm), r, w)
+        if part: narrow.add(len(calls) - 1)
+
+    def copy(e, o, i, r, w, m=0, part=False):
         if e == "V": op("V", lambda: V.tensor_copy(o, i), r, w)
+        elif e == "G": select(o, i, [[0, m]], ALU.is_equal, 0.0, 0, 0, r, w, part)
         else: op("S", lambda: S.activation(o, i, ACT.Copy), r, w)
 
     def ts(o, i, a, o0, b=None, o1=None, r=(), w=()):
@@ -102,7 +106,7 @@ def rank_program(g, core, T, topo):
 
     def tt(o, a, b, o0, r, w): op("V", lambda: V.tensor_tensor(o, a, b, o0), r, w)
     def scan(o, a, b, init, o0, o1, r, w): op("V", lambda: V.tensor_tensor_scan(o, a, b, init, o0, o1), r, w)
-    def fill(o, c, w): op("V", lambda: V.memset(o, c), (), w)
+    def fill(o, c, w, r=()): op("V", lambda: V.memset(o, c), r, w)
     def act(o, i, func, scale, bias, r, w): op("S", lambda: S.activation(o, i, func, bias=bias, scale=scale), r, w)
     def affine(o, i, scale, bias, r, w): act(o, i, ACT.Identity, scale, bias, r, w)
     def sign(o, i, v, r, w): act(o, i, ACT.Sign, -1.0, v, r, w)
@@ -119,13 +123,12 @@ def rank_program(g, core, T, topo):
         else: op("G", lambda: g.iota(o, pat, base, cm), (), w)
 
     def whole(o, m, c, w): iota(o, [[0, m]], c, 0, w)
-    def select(o, i, pat, cmp, c, base, cm, r, w): op("G", lambda: g.affine_select(o, i, pat, cmp, c, base, cm), r, w)
 
     def level(buf, width, k, a, m, data, first, lo, ops2, r, w, p=128):
         o = k * width
         prev = first if k == 0 else buf[0:p, o - width + a:o - width + a + m]
         init = lo if a == 0 else buf[0:p, o + a:o + a + 1]
-        scan(buf[0:p, o + a + 1:o + a + 1 + m], data, prev, init, ops2[0], ops2[1], list(r) + ["cst"], [w])
+        scan(buf[0:p, o + a + 1:o + a + 1 + m], data, prev, init, ops2[0], ops2[1], r, [w])
 
     def below(tok, k): return [tok % (k - 1)] if k else []
     UP, DOWN = (ALU.max, ALU.min), (ALU.min, ALU.max)
@@ -136,320 +139,374 @@ def rank_program(g, core, T, topo):
     j, qq = pf(1), pf(2)
     ET = ["et0"]
     quarter = lambda q: slice(32 * q, 32 * q + 32)
-    BP, BO, LO = 8, 48, 128
+    half = lambda h: slice(64 * h, 64 * h + 64)
+    BP, LO = 8, 128
     XE, XO = ["xe%d" % b for b in four], ["xo%d" % b for b in four]
-    F = ["f%d" % i for i in range(9)]
+    F = ["f%d" % i for i in range(6)]
     IN = ["in%d_%d" % (q, i) for q in four for i in range(5)]
+    M1, MD = ["c1", "c3", "big"], ["c4", "c9"]
 
+    at("x")
     dma("Y", "dx", [(T.xin[:], T.x[:])], (), ["xin"])
+    at("c0")
     iota(T.pi[:, 0:1], [[0, 1]], 0, 1, ["pi0"], False)
     iota(T.idt[:], [[1, 512]], 0, 0, ["idt"])
     fill(T.et[:], 0.0, ["et"])
     fill(T.big[:], BIG, ["big"])
     select(T.mk1[:], T.big[:, 0:K], [[-1, K]], ALU.not_equal, -BIG, 0, 1, ["big"], ["mk1"])
+    for q in (2, 3): select(T.mk2[quarter(q), :], T.big[quarter(q), 0:K], [[-1, K]], ALU.not_equal, -BIG, 128, 1, ["big"], ["mk%d" % q], True)
     for c, (sh, m) in enumerate([(0, 15), (5, 3), (0, 1), (1, 7), (5, 1), (6, 1)]):
         ts(T.pi[:, c + 1:c + 2], T.pi[:, 0:1], sh, ALU.logical_shift_right, m, ALU.bitwise_and, ["pi0"], ["pi%d" % (c + 1)])
-    fill(T.m1[:, 0::W1], -BIG, ["c0"])
     copy("V", T.pf[:, 0:7], T.pi[:, 0:7], ["pi%d" % c for c in range(7)], ["pf"])
     fill(T.m1[:, 4 * W1 + HI::W1], -BIG, ["c1"])
     fill(T.m1[:, LOW::W1], -BIG, ["c3"])
     ts(pf(16), pf(5), float(K), ALU.mult, pf(6), ALU.add, ["pf"], ["pf16"])
-    ts(pf(17), qq, 40.0 / 512, ALU.mult, (C + SH) / 512, ALU.add, ["pf"], ["pf17"])
-    ts(pf(18), qq, 40.0, ALU.mult, j, ALU.add, ["pf"], ["pf18"])
-    op("V", lambda: V.memset(T.md[:, 0::W3 + 4], -BIG), ["c0", "c1", "c3", "big"], ["cst"])
+    ts(pf(17), qq, 40.0 / 512, ALU.mult, 1 + (C + SH) / 512, ALU.add, ["pf"], ["pf17"])
+    ts(pf(18), pf(5), 40.0, ALU.mult, j, ALU.add, ["pf"], ["pf18"])
+    fill(T.md[:, W3::W3], -BIG, ["c9"])
+    ts(pf(20), pf(5), 80.0, ALU.mult, j, ALU.add, ["pf"], ["pf20"])
     ts(T.et[:, 3:515:4], T.idt[:, 0:128], pf(0), ALU.is_equal, r=["idt", "pf", "et"], w=ET)
-    ts(pf(16), pf(16), float(SH), ALU.add, 1.0 / 512, ALU.mult, ["pf16"], ["pf16"])
-    ts(pf(18), pf(18), -8.0, ALU.add, r=["pf18"], w=["pf18"])
+    ts(pf(16), pf(16), 512.0 + SH, ALU.add, 1.0 / 512, ALU.mult, ["pf16"], ["pf16"])
+    ts(pf(18), pf(18), K - 8.0, ALU.add, r=["pf18"], w=["pf18"])
     ts(pf(19), j, 15.0, ALU.is_equal, r=["pf"], w=["pf19"])
     for b in four: quant(T.ec, T.es, 128 * b, 128 * b + 128, T.et[:, 3 - b:515 - b], ET, ["ec%d" % b])
+    ts(T.selb[:, 0:3], T.idt[:, 0:48:16], pf(18), ALU.add, r=["idt", "pf18"], w=["selb"])
+    ts(T.selb[:, 3:8], T.idt[:, 0:80:16], pf(20), ALU.add, r=["idt", "pf20"], w=["selc"])
+    fill(T.in1[:], 0.0, IN)
     for c, a in enumerate([T.idt[:, 1:C:2], T.idt[:, 0:C:2], T.idt[:, C:PL]]):
         affine(T.d1[:, PL * c + 2:PL * c + PL:3], a, 1.0 / 512, 1 + SH / 512, ["idt"], ["f%d" % c])
-    affine(T.d1[:, 3 * PL + 3:3 * PL + 160:4], T.idt[:, 0:40], 1.0 / 512, pf(17), ["idt", "pf17"], ["f4"])
-    affine(T.d1[:, 3 * PL + 163::4], T.idt[:, 0:K:2], 1.0 / 512, pf(16), ["idt", "pf16"], ["f5"])
+    affine(T.d1[:, 3 * PL + 2:3 * PL + 120:3], T.idt[:, 0:40], 1.0 / 512, pf(17), ["idt", "pf17"], ["f3"])
+    affine(T.d1[:, 3 * PL + 122::3], T.idt[:, 0:K:2], 1.0 / 512, pf(16), ["idt", "pf16"], ["f4"])
+    at("xe")
     for b in four: copy("VVVS"[b], T.xt[:, b:4 * K:4], T.xin[:, b::8], ["xin"], ["xe%d" % b])
-    for b in range(2): copy("S", T.xt[:, 4 * K + b:4 * C:4], T.xin[:, 4 + b::8], ["xin"], ["xo%d" % b])
+    at("xo")
+    for b in four: copy("SSVV"[b], T.xt[:, 4 * K + b:4 * C:4], T.xin[:, 4 + b::8], ["xin"], ["xo%d" % b])
 
-    def const(o, m, c, r, w): affine(o, T.et[:, 0:m], 0.0, c, ET + r, w)
-
-    def constants(i):
-        if i == 0:
-            const(T.d1[:, 3 * PL + 1::4], 120, 2.0, [], ["f3"])
-            copy("V", T.mk2[96:128, :], T.mk1[0:32, 0:32], ["mk1"], ["mk2"])
-            fill(T.in1[:], 0.0, IN)
-            for c, (o, m) in enumerate([(T.n1[:, 0::WA], 8), (T.n2[:, 0::WK], 8), (T.bb[:, 0::WD], 8), (T.b2[:], 64)]): const(o, m, KB, [], ["c%d" % (5 + c)])
-            ts(T.selb[:, 0:3], T.idt[:, 0:48:16], pf(18), ALU.add, 0.0, ALU.max, ["idt", "pf18"], ["selb"])
-        if i == 2:
-            affine(pf(7), j, 1.0, 1.0, ["pf"], ["pf7"])
-            affine(pf(8), j, 4.0, 512.0, ["pf"], ["pf8"])
-            affine(pf(9), j, 4.0, 576.0, ["pf"], ["pf9"])
-            affine(pf(12), pf(19), 1 - 2.0 ** -12, 2.0 ** -12, ["pf19"], ["pf12"])
-        if i == 3:
-            for c, (at, by) in enumerate([(j, 4096.0), (j, pf(8)), (pf(7), 4096.0), (j, pf(9))]):
-                ts(T.cb[:, 16 * c:16 * c + 16], T.i16[:, 0:16], at, ALU.is_equal, by, ALU.mult, ["i16", "pf7", "pf8", "pf9"], ["cb%d" % c])
-            ts(T.ca[:], T.i16[:], j, ALU.not_equal, r=["i16", "pf"], w=["ca"])
-            ts(T.cc[:], T.i16[:], pf(7), ALU.is_equal, 512.0, ALU.mult, ["i16", "pf7"], ["cc"])
-            op("V", lambda: V.memset(T.neg[:], -KB), ["c5", "c6", "c7", "c8"], ["ck"])
-            ts(T.cb[:], T.cb[:], 1.0, ALU.max, r=["cb%d" % c for c in four], w=["cb"])
-        if i == 4:
-            affine(T.cb[:, 0::32], T.cb[:, 0::32], 0.0, 0.0, ["cb"], ["cc0"])
-            affine(T.cb[:, 16:17], T.cb[:, 16:17], 2.0 ** -12, 0.0, ["cb"], ["cc1"])
-            affine(T.cb[:, 48:49], T.cb[:, 48:49], pf(12), 0.0, ["cb", "pf12"], ["cc2"])
-            for c in range(10):
-                select(T.cm[:, 32 * c:32 * c + 32], T.cb[:, 32 * (c // 5):32 * (c // 5) + 32], [[0, 32]], ALU.is_equal, 0.0, 0, 0, ["cc0", "cc1", "cc2"], ["cm%d" % c])
-            affine(pf(10), pf(3), float(K), 31.0, ["pf"], ["pf10"])
-            affine(pf(13), pf(19), -511.0 / 512, -1.0 / 512, ["pf19"], ["pf13"])
-            affine(pf(14), pf(19), -255.5, 256.0, ["pf19"], ["pf14"])
-            affine(pf(15), pf(19), -511.0 * OWN, 512.0 * OWN, ["pf19"], ["pf15"])
-        if i == 1:
-            iota(T.i16[:], [[0, 10], [1, 16]], 0, 0, ["i16"])
-            whole(T.d0[:, 0:3 * PL:3], PL, 0, ["f6"])
-            whole(T.d0[:, 3 * PL::4], 120, 0, ["f7"])
-            whole(T.d0[:, 3 * PL + 3::4], 120, 1, ["f8"])
-            iota(T.sxi[:], [[1, 2], [2, 5], [0, 2]], 0, 0, ["sxi"])
-            iota(T.sval[:], [[-1, K]], K, 0, ["sval"])
-            for b in four:
-                whole(T.vp[:, PV * b:PV * b + SH], SH, 0, ["vz%d" % b])
-                whole(T.est[:, b * EW + K:b * EW + OWN], OWN - K, 0, ["ez%d" % b])
-            whole(T.est[:, OWN + K::EW], 4, 0, ["ez"])
-
-    spare_first = [lambda: ts(pf(11), pf(4), 32.0, ALU.mult, pf(10), ALU.add, ["pf10"], ["pf11"]),
-                   lambda: copy("V", T.selx[:], T.sxi[:], ["sxi"], ["selx"]),
-                   lambda: tt(T.c16[:, 0:80], T.ca[:, 0:80], T.cc[:, 0:80], ALU.max, ["ca", "cc"], ["c16a"]),
-                   lambda: ts(T.selk[:, 0:1], pf(11), float(C - 1), ALU.min, r=["pf11"], w=["selk"]),
-                   lambda: tt(T.c16[:, 80:K], T.ca[:, 80:K], T.cc[:, 80:K], ALU.max, ["ca", "cc", "c16a"], ["c16"]), None]
-    spare_last = [lambda: quant(T.vc, T.vs, 0, 128, T.vin[:], ["vin"], ["vc"]), None,
-                  lambda: ts(T.opi[:], T.out1[:], 512.0, ALU.mult, r=["out1"], w=["opi"]),
-                  lambda: ts(T.opj[:], T.opi[:], 511, ALU.bitwise_and, r=["opi"], w=["opj"]),
-                  lambda: ts(T.opf[:], T.opj[:], -float(SH), ALU.add, r=["opj"], w=["opf"]),
-                  lambda: dma("Y", "dop", [(T.op[2 * q + h, :], T.opf[32 * q:32 * q + 5, 32 * h:32 * h + 32]) for q in four for h in range(2)], ["opf"])]
-
-    def repeat(i, e):
-        o, a = T.xt[:, 4 * (C + 32 * i):4 * (C + 32 * i + 32)], T.xt[:, 4 * 288:4 * C]
-        if e == "G": select(o, a, [[0, 128]], ALU.is_equal, 0.0, 0, 0, XO, ["xr%d" % i])
-        else: copy(e, o, a, XO, ["xr%d" % i])
+    def const(o, m, c, w): affine(o, T.idt[:, 0:m], 0.0, c, ["idt"], w)
+    at("c1")
+    iota(T.i16[:], [[0, 10], [1, 16]], 0, 0, ["i16"])
+    whole(T.d0[:, 0::3], 600, 0, ["f5"])
+    iota(T.sxi[:], [[1, 2], [2, 5], [0, 2]], 0, 0, ["sxi"])
+    iota(T.sval[:], [[-1, K]], K, 0, ["sval"])
+    for b in four:
+        whole(T.vp[:, PV * b:PV * b + SH], SH, 0, ["vz%d" % b])
+        whole(T.est[:, b * EW + K:b * EW + OWN], OWN - K, 0, ["ez%d" % b])
+    whole(T.est[:, OWN + K::EW], 4, 0, ["ez"])
+    at("c2")
+    for c, (o, m) in enumerate([(T.n1[:, 0::WA], 8), (T.n2[:, 0::WK], 8), (T.bb[:, 0::WD], 8), (T.b2[:], 128)]): const(o, m, KB, ["c%d" % (5 + c)])
+    const(T.md[:, 0:W3], W3, BIG, ["c4"])
+    const(T.ob[:, 8:9], 1, BIG, ["ob"])
+    affine(pf(7), j, 1.0, 1.0, ["pf"], ["pf7"])
+    affine(pf(8), j, 4.0, 512.0, ["pf"], ["pf8"])
+    affine(pf(9), j, 4.0, 576.0, ["pf"], ["pf9"])
+    affine(pf(12), pf(19), 1 - 2.0 ** -12, 2.0 ** -12, ["pf19"], ["pf12"])
+    at("c3")
+    for c, (a, by) in enumerate([(j, 4096.0), (j, pf(8)), (pf(7), 4096.0), (j, pf(9))]):
+        ts(T.cb[:, 16 * c:16 * c + 16], T.i16[:, 0:16], a, ALU.is_equal, by, ALU.mult, ["i16", "pf7", "pf8", "pf9"], ["cb%d" % c])
+    ts(T.ca[:], T.i16[:], j, ALU.not_equal, r=["i16", "pf"], w=["ca"])
+    ts(T.cc[:], T.i16[:], pf(7), ALU.is_equal, 512.0, ALU.mult, ["i16", "pf7"], ["cc"])
+    fill(T.neg[:], -KB, ["ck"], ["c5", "c6", "c7", "c8"])
+    ts(T.cb[:], T.cb[:], 1.0, ALU.max, r=["cb%d" % c for c in four], w=["cb"])
+    at("c4")
+    affine(T.cb[:, 0::32], T.cb[:, 0::32], 0.0, 0.0, ["cb"], ["cc0"])
+    affine(T.cb[:, 16:17], T.cb[:, 16:17], 2.0 ** -12, 0.0, ["cb"], ["cc1"])
+    affine(T.cb[:, 48:49], T.cb[:, 48:49], pf(12), 0.0, ["cb", "pf12"], ["cc2"])
+    for c in range(10): copy("G", T.cm[:, 32 * c:32 * c + 32], T.cb[:, 32 * (c // 5):32 * (c // 5) + 32], ["cc0", "cc1", "cc2"], ["cm%d" % c], 32)
+    affine(pf(10), pf(3), float(K), 31.0, ["pf"], ["pf10"])
+    affine(pf(11), pf(4), 32.0, pf(10), ["pf10"], ["pf11"])
+    affine(pf(13), pf(19), -511.0 / 512, -1.0 / 512, ["pf19"], ["pf13"])
+    affine(pf(14), pf(19), -255.5, 256.0, ["pf19"], ["pf14"])
+    affine(pf(15), pf(19), -511.0 * OWN, 512.0 * OWN, ["pf19"], ["pf15"])
+    at("c6")
+    copy("V", T.selx[:], T.sxi[:], ["sxi"], ["selx"])
+    at("c7")
+    tt(T.c16[:, 0:80], T.ca[:, 0:80], T.cc[:, 0:80], ALU.max, ["ca", "cc"], ["c16a"])
+    at("c8")
+    ts(T.selk[:, 0:1], pf(11), float(C - 1), ALU.min, r=["pf11"], w=["selk"])
+    at("c9")
+    tt(T.c16[:, 80:K], T.ca[:, 80:K], T.cc[:, 80:K], ALU.max, ["ca", "cc"], ["c16b"])
 
     def odd_columns(t):
         wc, ws = wcs[t]
+        now[0] = t
+        at("xr")
+        for i in range(3): copy("G" if t else "S", T.xt[:, 4 * (C + 32 * i):4 * (C + 32 * i + 32)], T.xt[:, 4 * 288:4 * C], XO, ["xr%d" % i], 128)
+        at("wo")
         quant(wc, ws, K, C, T.xt[:, 4 * K:4 * C], XO, ["wo"])
+        at("moo")
         mm(0, wc, ws, K, wc, ws, K, K, ["wo"])
+        at("s1")
+        tt(T.s1[:, 0:K], ps(0, 0, K), T.mk1[:], ALU.min, ["ps0", "mk1"], ["s1_0"])
+        at("wr")
+        quant(wc, ws, 288, LAND, T.xt[:, 4 * 288:], XO + ["xr0", "xr1", "xr2"], ["wo"])
+        at("mor")
+        mm(3, wc, ws, 288, wc, ws, K, K, ["wo"])
+        at("own")
+        tt(T.cv[64:128, 0:K], ps(3, 0, K, 64), T.mk2[64:128, :], ALU.min, ["ps3", "mk2", "mk3"], ["cv1"])
+        now[0] = max(t - 1, 0)
 
-    def repeated_columns(t):
-        wc, ws = wcs[t]
-        quant(wc, ws, 288, LAND, T.xt[:, 4 * 288:], XO + ["xr0", "xr1", "xr2"], ["wr", "wo"])
-        mm(3, wc, ws, 288, wc, ws, K, K, ["wo", "wr"])
-        for q in (3, 2): copy("S", T.sa[quarter(q), BO:BO + 80], ps(3, 80 * q - K, 80 * q - 80, 32 * q, 32 * q + 32), ["ps3"], ["s2_%d" % q])
-
-    def best_places(t, near):
+    def best_places(t):
         wc, ws = wcs[t]
         big = T.big[:, 0:K]
-        S1, S2 = ["s1_0", "s1_1", "s1_2"], ["s2_%d" % q for q in four]
-        CV = ["cva", "cvb0", "cvb1"] + ["cvc%d" % q for q in four]
+        S1 = ["s1_0", "s1_1", "s1_2"]
+        for k in four:
+            at("l%d" % k)
+            level(T.m1, W1, k, LOW, K, T.sa[:, LO:LO + K], big, None, UP, M1 + ["lo"] + below("l%d", k), "l%d" % k)
+        for k in eight:
+            at("h%d" % k)
+            level(T.m1, W1, k, HI, K, T.sa[:, LO + K:LO + C], big, None, UP, M1 + ["hi", "l%d" % min(k, 3)] + below("h%d", k), "h%d" % k)
+        for k in eight:
+            at("x%d" % k)
+            level(T.md, W3, k + 1, 0, K, T.cv[:, 0:K], None, T.md[:, (k + 1) * W3:(k + 1) * W3 + 1], UP, MD + ["cv0", "cv1"] + below("x%d", k), "x%d" % k)
+        for name, bank, a in (("mp", 2, K), ("mpr", 0, 288), ("mp2", 3, K)):
+            at(name)
+            mm(bank, wc, ws, a, wc, ws, LAND, K, ["wo", "wl"])
+        if t == 0:
+            at("w")
+            dma("Y", "dl", [(T.lc[:].bitcast(dt.uint8), T.wc[:])], ["wl"], ["lc"])
+            dma("Y", "dls", [(T.ls[:], T.ws[:])], (), ["ls"])
+            dma("Y", "dv", [(T.vin[:], T.v[:])], (), ["vin"])
+        at("cv")
+        for h in range(2): copy("S", T.cv[half(h), K:240], ps(0, 80 * h, 80 * h + 80, 64 * h, 64 * h + 64), ["ps0"], ["cvp%d" % h])
+        at("s12")
+        copy("S", T.s1[:, C:PL], ps(3, 0, K), ["ps3"], ["s1_2"])
+        at("s2p")
+        copy("S", T.sa[:, 0:LO], T.cv[:].indirect(T.selb[:]), ["cv0", "cv1", "cvp0", "cvp1", "selb", "selc"], ["s2p"])
+        for k in eight:
+            at("p%d" % k)
+            level(T.m1, W1, k, PA, K, ps(2, 0, K), big, -BIG, UP, M1 + ["ps2", "h%d" % k] + below("p%d", k), "p%d" % k)
+        for k in eight:
+            at("Q%d" % k)
+            level(T.md, W3, k + 1, K, 80, T.cv[:, K:240], None, None, UP, MD + ["cvp0", "cvp1", "x%d" % k] + below("md%d", k), "md%d" % k)
+        for lo, hi in ((0, 4), (4, 8)):
+            at("ob%d" % hi)
+            for h in range(2): copy("S", T.ob[half(h), 8 - hi:8 - lo], T.md[half(1 - h), hi * W3 + 240:lo * W3 + 240:-W3], ["md%d" % (hi - 1)], ["ob%d_%d" % (h, hi)])
+        vv = lambda k: T.vv[:, 9 * k - 7:9 * k - 6]
+        for k in (1, 3, 5, 7):
+            at("v%d" % k)
+            scan(T.vv[:, 8 * k - 8:9 * k - 6], T.md[:, 240:(k + 1) * W3 + 241:W3], T.ob[:, 7 - k:9], -BIG, ALU.max, ALU.min,
+                 MD + ["ob", "md%d" % k] + ["ob%d_%d" % (h, hi) for h in range(2) for hi in (4, 8)[:k // 4 + 1]], ["v%d" % k])
         slot = {1: (T.d1, 1), 3: (T.d1, 0), 5: (T.d0, 2), 7: (T.d0, 1)}
-        slot2 = {1: (T.d1, 0), 3: (T.d0, 2), 5: (T.d0, 1), 7: (T.d1, 2)}
-
-        def low(k): level(T.m1, W1, k, LOW, K, T.sa[:, LO:LO + K], big, -BIG, UP, ["lo"] + below("l%d", k), "l%d" % k)
-        def high(k): level(T.m1, W1, k, HI, K, T.sa[:, LO + K:LO + C], big, -BIG, UP, ["hi", "l%d" % min(k, 3)] + below("h%d", k), "h%d" % k)
-        def far(k): level(T.m1, W1, k, PA, K, ps(2, 0, K), big, -BIG, UP, ["ps2", "h%d" % k] + below("p%d", k), "p%d" % k)
-
-        def signs(k, c=None):
+        for k in (1, 3, 5, 7):
             d, a = slot[k]
-            c, m = (0, PL) if c is None else (120 * c, 120)
-            sign(d[:, 3 * c + a:3 * (c + m):3], T.s1[:, c:c + m], T.m1[:, k * W1 + PA + K:k * W1 + PA + K + 1], S1 + ["p%d" % k], ["e1_%d_%d" % (k, c // 120)])
-
-        def own2(k):
-            o = (7 - k) * W1
-            scan(T.m1[:, o + 1:o + 81], T.sa[:, BO:BO + 80], T.m1[:, o + W1:o + W1 + 80] if k else T.big[:, 0:80], -BIG, ALU.max, ALU.min,
-                 S2 + below("x%d", k) + ["cst"], ["x%d" % k])
-
-        def far2(k): level(T.md, W3, k, 4 * k, 192 - 4 * k, T.cv[:, 4 * k:], T.big[:], -BIG, UP, CV + ["cvp"] + below("md%d", k), "md%d" % k)
-
-        def signs2(k):
-            d, a = slot2[k]
-            sign(d[:, 3 * PL + a::4], T.sa[:, BP:BP + 120], T.md[:, k * W3 + 192:k * W3 + 193], S2 + ["s2p", "md%d" % k], ["e2_%d" % k])
-
-        def lift(_): affine(T.d1[:, 1:3 * PL:3], T.d1[:, 1:3 * PL:3], -1.0, 3.0, [], ["e1_1_0"])
-
-        def spread(i):
-            if near != i: return
-            X8 = ["x%d" % k for k in eight]
-            copy("S", T.cv[:, 0:32:4], T.m1[:, 80::W1], X8, ["cva"])
-            for h in range(2): copy("S", T.cv[64 * h:64 * h + 64, 2:32:4], T.m1[64 - 64 * h:128 - 64 * h, 80::W1], X8, ["cvb%d" % h])
-            if near: arrived(3)
-            for q in four: copy("S", T.cv[quarter(q), 1:32:2], T.cv[quarter(q ^ 1), 0:32:2], ["cva", "cvb0", "cvb1"], ["cvc%d" % q])
-
-        def arrived(i):
-            if i == 0:
-                mm(2, wc, ws, K, wc, ws, LAND, K, ["wo", "wl"])
-                mm(0, wc, ws, 288, wc, ws, LAND, K, ["wo", "wr", "wl"])
-                mm(1, wc, ws, K, wc, ws, LAND, K, ["wo", "wl"])
-                if t == 0:
-                    dma("Y", "dl", [(T.lc[:].bitcast(dt.uint8), T.wc[:])], ["wl"], ["lc"])
-                    dma("Y", "dls", [(T.ls[:], T.ws[:])], (), ["ls"])
-                    dma("Y", "dv", [(T.vin[:], T.v[:])], (), ["vin"])
-            if i == 1: copy("S", T.cv[:, 32:], ps(0, 0, K), ["ps0"], ["cvp"])
-            if i == 2: copy("S", T.s1[:, C:PL], ps(1, 0, K), ["ps1"], ["s1_2"])
-            if i == 4 - near: copy("S", T.sa[:, 0:BO], T.cv[:, 32:].indirect(T.selb[:, 0:3]), ["cvp", "selb"], ["s2p"])
-
-        def keys(c):
-            run = slice(360 * c, 360 * c + {0: 360, 1: 360, 2: 720, 4: PL}[c])
+            for c, m in ([(0, PL)] if k < 7 else [(c, 120) for c in four]):
+                at("e%d" % k if k < 7 else "f%d" % c)
+                o = d[:, 360 * c + a:360 * c + 3 * m:3]
+                sign(o, T.s1[:, 120 * c:120 * c + m], T.m1[:, k * W1 + PA + K:k * W1 + PA + K + 1], S1 + ["p%d" % k], ["e1_%d_%d" % (k, c)])
+            at("lift")
+            if k == 1: affine(o, o, -1.0, 3.0, [], ["e1_1_0"])
+            at("g%d" % k)
+            sign(d[:, 3 * PL + a::3], T.sa[:, BP:BP + 120], vv(k), ["s2p", "v%d" % k], ["e2_%d" % k])
+        at("g0")
+        affine(T.d1[:, 3 * PL + 1::3], T.d1[:, 3 * PL + 1::3], -1.0, 3.0, [], ["e2_1"])
+        at("w7")
+        ts(T.cl[:, 1:2], T.m1[:, 7 * W1 + PA + K:7 * W1 + PA + K + 1], T.m1[:, 5 * W1 + PA + K:5 * W1 + PA + K + 1], ALU.is_lt, 2.0, ALU.mult, ["p7"], ["cl1"])
+        at("u7")
+        ts(T.cl[:, 3:4], vv(7), vv(5), ALU.is_lt, 2.0, ALU.mult, ["v5", "v7"], ["cl3"])
+        for b in four:
+            at("dp")
+            mm(4 + b, T.ec, T.es, 128 * b, wc, ws, LAND, K, ["ec%d" % b, "wl"])
+            at("vq")
+            copy("S", T.vp[:, PV * b + SH + C:PV * b + PV], ps(4 + b, 0, K), ["ps%d" % (4 + b)], ["vp%d_2" % b])
+        for c, m in ((0, 360), (1, 360), (2, 720), (4, 360)):
+            at("k%d" % c)
+            run = slice(360 * c, 360 * c + m)
             scan(T.k1[:, run], T.d0[:, run], T.d1[:, run], 0.0, ALU.mult, ALU.add,
                  F + (["e1_1_0", "e1_3_0", "e1_5_0", "e1_7_%d" % c, "e1_7_%d" % (c + c // 2)] if c < 4 else ["e2_%d" % i for i in (1, 3, 5, 7)]), ["k%d" % c])
-
-        def key1(k, c=0):
-            level(T.n1, WA, k, 240 * c, 240, T.k1[:, 720 * c + 2:720 * c + 720:3], T.neg[:], KB, DOWN,
-                  ["ck", "k%d" % (2 * c), "k%d" % (c + 1)] + below("n%d_" + str(c), k) + (["n%d_0" % k] if c else []), "n%d_%d" % (k, c))
-
-        def key2(k): level(T.n2, WK, k, 0, 120, T.k1[:, 3 * PL + 3::4], T.neg[:, 0:120], KB, DOWN, ["ck", "k4"] + below("q%d", k), "q%d" % k)
-
-        def gather2(s):
-            m = 4 * s + 4
-            for q in four:
-                copy("S", T.b2[0:32, 32 * s + 8 * q:32 * s + 8 * q + m], T.n2[quarter(q), 120:m * WK:WK], ["ck", "q%d" % (m - 1)], ["b2_%d_%d" % (s, q)])
-
-        def merge2(k):
-            s = k // 4
-            level(T.bb, WD, k, 0, 32, T.b2[0:32, 32 * s:32 * s + 32], T.neg[0:32, 0:32], KB, DOWN, ["b2_%d_%d" % (s, q) for q in four] + below("d%d", k), "d%d" % k, 32)
-
-        def turn(q):
+        for k in eight:
+            for c in range(2):
+                at("ab"[c] + str(k))
+                level(T.n1, WA, k, 240 * c, 240, T.k1[:, 720 * c + 2:720 * c + 720:3], T.neg[:], KB, DOWN,
+                      ["ck", "k%d" % (2 * c), "k%d" % (c + 1)] + below("n%d_" + str(c), k) + (["n%d_0" % k] if c else []), "n%d_%d" % (k, c))
+            at("n%d" % k)
+            level(T.n2, WK, k, 0, 120, T.k1[:, 3 * PL + 2::3], T.neg[:, 0:120], KB, DOWN, ["ck", "k4"] + below("q%d", k), "q%d" % k)
+        for s in four:
+            at("j%d" % s)
+            m = 2 * s + 2
+            for q in four: copy("S", T.b2[0:32, 32 * s + 8 * q:32 * s + 8 * q + m], T.n2[quarter(q), 120:m * WK:WK], ["ck", "q%d" % (m - 1)], ["b2_%d_%d" % (s, q)])
+        for k in eight:
+            s = k // 2
+            at("d%d" % k)
+            level(T.bb, WD, k, 0, 32, T.b2[0:32, 32 * s:32 * s + 32], T.neg[0:32, 0:32], KB, DOWN, ["ck"] + ["b2_%d_%d" % (s, q) for q in four] + below("d%d", k), "d%d" % k, 32)
+        for q in range(3):
+            at("T%d" % q)
             for i in four:
-                copy("VVVS"[i] if q == 3 else "S", T.in1[quarter(q), i::32], T.n1[quarter(i), 2 * q * WA + PL:(2 * q + 2) * WA:WA], ["n%d_1" % (2 * q + 1)], ["in%d_%d" % (q, i)])
+                copy("GGS"[q], T.in1[quarter(q), i::32], T.n1[quarter(i), 2 * q * WA + PL:(2 * q + 2) * WA:WA], ["n%d_1" % (2 * q + 1)], ["in%d_%d" % (q, i)], 2, True)
+            at("U%d" % q)
+            copy("S", T.in1[quarter(q), 4::32], T.bb[0:32, 2 * q * WD + 32:(2 * q + 2) * WD:WD], ["d%d" % (2 * q + 1)], ["in%d_4" % q])
+        at("fl")
+        ts(T.cw[0:96, :], T.in1[0:96, 0:40], -1.5, ALU.add, r=IN[:15], w=["cw"])
+        at("fr")
+        tt(T.in1[0:96, 0:40], T.in1[0:96, 0:40], T.cw[0:96, :], ALU.subtract, ["cw"], IN[:15])
+        at("w6")
+        ts(T.cl[:, 0:1], T.n1[:, 6 * WA + PL:6 * WA + PL + 1], -1.5, ALU.add, r=["n6_1"], w=["cl0"])
+        at("u6")
+        ts(T.cl[0:32, 2:3], T.bb[0:32, 6 * WD + 32:6 * WD + 33], -1.5, ALU.add, r=["d6"], w=["cl2"])
+        at("T3")
+        for i in four: tt(T.in1[96:128, i::32], T.n1[quarter(i), 6 * WA + PL::WA], T.cl[quarter(i), 0:2], ALU.subtract, ["n7_1", "cl0", "cl1"], ["in3_%d" % i])
+        at("U3")
+        tt(T.in1[96:128, 4::32], T.bb[0:32, 6 * WD + 32::WD], T.cl[0:32, 2:4], ALU.subtract, ["d7", "cl2", "cl3"], ["in3_4"])
 
-        def turn2(q): copy("V" if q == 3 else "S", T.in1[quarter(q), 4::32], T.bb[0:32, 2 * q * WD + 32:(2 * q + 2) * WD:WD], ["d%d" % (2 * q + 1)], ["in%d_4" % q])
-
-        def beside(i):
-            if i > 1 and t == 0: constants(i)
-            if i == 0:
-                for h in range(2): whole(T.sw[:, SW * h + SH:SW * h + PV], PL, 0, ["sw%d" % h])
-            if i == 1:
-                for b in four:
-                    mm(4 + b, T.ec, T.es, 128 * b, wc, ws, LAND, K, ["ec%d" % b, "wl"])
-                    copy("S", T.vp[:, PV * b + SH + C:PV * b + PV], ps(4 + b, 0, K), ["ps%d" % (4 + b)], ["vp%d_2" % b])
-        step = dict(L=low, H=high, P=far, E=signs, F=lambda c: signs(7, c), X=own2, Q=far2, G=signs2, S=spread, A=arrived, k=keys, a=key1,
-                    b=lambda k: key1(k, 1), n=key2, g=gather2, M=merge2, T=turn, U=turn2, c=beside, O=lift)
-        for w in ORDER.split(): step[w[0]](int(w[1]))
-
+    odd_columns(0)
+    order = {e: [] for e in Q}
     for t in range(R):
         partner, giver = T.cores[(rank + 1 + t) % n], T.cores[(rank - 1 - t) % n]
         wc, ws = wcs[t]
         hc, hs = hcs[t]
         gs, gl = T["gs%d" % t], T["gl%d" % t]
         final = t == R - 1
+        now[0] = t
+        for e in Q:
+            order[e] += [(w.strip("+*"), t + w.count("+")) for w in (ORDER[e] + " " + (NEAR if topo.chip(core) == topo.chip(partner) else FAR)[e]).split()
+                         if t or "*" not in w]
+        at("we")
         quant(wc, ws, 0, K, T.xt[:, 0:4 * K], XE, ["we"])
-        send(giver, "at%d" % t, [(wc[:, LAND:].bitcast(dt.uint8), wc[:, 0:K].bitcast(dt.uint8)), (ws[:, LAND:], ws[:, 0:K])], ["we"])
-        arrives(partner, "at%d" % t, 2, ["wl"])
-        if t == 0:
-            constants(1)
-            for b in (2, 3): copy("V", T.xt[:, 4 * K + b:4 * C:4], T.xin[:, 4 + b::8], ["xin"], ["xo%d" % b])
-            for i in range(3): repeat(i, "S")
-            odd_columns(0)
-            constants(0)
-        mm(1, wc, ws, K, wc, ws, 0, K, ["wo", "we"])
-        tt(T.s1[:, 0:K], ps(0, 0, K), T.mk1[:], ALU.min, ["ps0", "mk1"], ["s1_0"])
-        if t == 0: repeated_columns(0)
-        mm(0, wc, ws, 288, wc, ws, 0, K, ["wo", "wr", "we"])
-        mm(2, wc, ws, K, wc, ws, 0, K, ["wo", "we"])
-        for q in range(2): copy("S", T.sa[quarter(q), BO:BO + 80], ps(0, 80 * q, 80 * q + 80, 32 * q, 32 * q + 32), ["ps0"], ["s2_%d" % q])
+        exchange(giver, partner, "at%d" % t, [(wc[:, LAND:].bitcast(dt.uint8), wc[:, 0:K].bitcast(dt.uint8)), (ws[:, LAND:], ws[:, 0:K])], ["we"], ["wl"])
+        for name, bank, a in (("meo", 1, K), ("mer", 0, 288), ("meo2", 2, K)):
+            at(name)
+            mm(bank, wc, ws, a, wc, ws, 0, K, ["wo", "we"])
+        at("r0")
+        copy("S", T.cv[0:64, 0:K], ps(0, 0, K, 0, 64), ["ps0"], ["cv0"])
+        at("s11")
         copy("S", T.s1[:, K:C], ps(2, 0, K), ["ps2"], ["s1_1"])
-        own = T.sa[96:128, BO + 48:BO + 80]
+        at("lo")
         tt(T.sa[:, LO:LO + K], ps(1, 0, K), T.s1[:, 0:K], ALU.min, ["ps1", "s1_0"], ["lo"])
+        at("hi")
         tt(T.sa[:, LO + K:LO + C], ps(1, 0, K), T.s1[:, 0:K], ALU.max, ["ps1", "s1_0"], ["hi"])
-        tt(own, own, T.mk2[96:128, :], ALU.min, ["s2_3", "mk2"], ["s2_3"])
         for b in four:
-            mm(4 + b, T.ec, T.es, 128 * b, wc, ws, 0, C, ["ec%d" % b, "we", "wo", "wr"])
+            at("dt")
+            mm(4 + b, T.ec, T.es, 128 * b, wc, ws, 0, C, ["ec%d" % b, "we", "wo"])
+            at("vp")
             for e in range(2):
                 copy("S", T.vp[:, PV * b + SH + e:PV * b + SH + C:2], ps(4 + b, K * e, K * e + K), ["ps%d" % (4 + b)], ["vp%d_%d" % (b, e)])
-        best_places(t, topo.chip(core) == topo.chip(partner))
+        at("sw")
+        for h in range(2): whole(T.sw[:, SW * h + SH:SW * h + PV], PL, 0, ["sw%d" % h])
+        best_places(t)
         lw = T.lwu[:, 0:10]
-        chain = [lambda: op("V", lambda: V.transpose(T.out1[:], T.in1[:]), IN, ["out1"]),
-                 lambda: [op("V", lambda e=e: V.transpose(T.o32[:, e::2], T.out1[:, e::2]), ["out1"], ["o32_%d" % e]) for e in range(2)],
-                 lambda: ts(T.lw0[:], T.o32[:, 0:16], 512.0, ALU.mult, r=["o32_0", "o32_1"], w=["lw0"]),
-                 lambda: ts(T.lwi[:], T.lw0[:], 511, ALU.bitwise_and, r=["lw0"], w=["lwi"]),
-                 lambda: copy("V", T.lwu[:], T.lwi[:], ["lwi"], ["lwu"]), None]
-        for f, h in zip(spare_first if t == 0 else spare_last if final else [None] * 6, chain):
-            if f: f()
-            if h: h()
-        copy("S", T.x1[:], T.idt[:].indirect(lw), ["lwu", "idt"], ["x1"])
-        for b in (0, 2, 1, 3):
+        at("out1")
+        op("V", lambda: V.transpose(T.out1[:], T.in1[:]), IN, ["out1"])
+        at("o32")
+        for e in range(2): op("V", lambda e=e: V.transpose(T.o32[:, e::2], T.out1[:, e::2]), ["out1"], ["o32_%d" % e])
+        for name in ("lwu", "lwi"):
+            at(name)
+            ts(T[name][:], T.o32[:, 0:16], 512.0, ALU.mult, -512.0, ALU.add, ["o32_0", "o32_1"], [name])
+        if final:
+            at("vc")
+            quant(T.vc, T.vs, 0, 128, T.vin[:], ["vin"], ["vc"])
+            at("opf")
+            affine(T.opf[:], T.out1[:], 512.0, -512.0 - SH, ["out1"], ["opf"])
+            at("op")
+            dma("Y", "dop", [(T.op[2 * q + h, :], T.opf[32 * q:32 * q + 5, 32 * h:32 * h + 32]) for q in four for h in range(2)], ["opf"])
+        at("zt")
+        for b in four:
             copy("VVSS"[b], T.zt[:, b::4], T.vp[:, PV * b:PV * b + PV].indirect(lw), ["lwu", "vz%d" % b] + ["vp%d_%d" % (b, i) for i in range(3)], ["zt%d" % b])
-        for e in range(2): tt(T.eq[:, K * e:K * e + K], T.lwi[:].indirect(T.selx[:, 10 * e:10 * e + 10]), T.x1[:], ALU.is_equal, ["lwi", "selx", "x1"], ["eq%d" % e])
+        at("zc")
         quant(T.zc, T.zs, 0, K, T.zt[:], ["zt%d" % b for b in four], ["zc"])
-        for b in (0, 2, 1, 3): mm(4 + b, T.lc, T.ls, 128 * b, T.zc, T.zs, 0, K, ["lc", "ls", "zc"])
-
-        def cast(b):
+        for b in (0, 2, 1, 3):
+            at("mh")
+            mm(4 + b, T.lc, T.ls, 128 * b, T.zc, T.zs, 0, K, ["lc", "ls", "zc"])
+            at("ht%d" % b)
             if b < 2: ts(T.ht[:, b::4], ps(4 + b, 0, K), 0.03125, ALU.mult, r=["ps%d" % (4 + b)], w=["ht%d" % b])
-            else: op("S", lambda: S.activation(T.ht[:, b::4], ps(4 + b, 0, K), ACT.Copy, scale=0.03125), ["ps%d" % (4 + b)], ["ht%d" % b])
-
-        def scatter(q):
-            h = q % 2
-            copy("V", T.sw[:, SW * h:SW * h + SW].indirect(T.so[:, 2 * q:2 * q + 2]), T.sval[:, 32 * q:32 * q + 32], ["so", "sval"], ["sw%d" % h])
-        scan(T.kp[:], T.cm[:], T.eq[:], 0.0, ALU.mult, ALU.max, ["eq0", "eq1"] + ["cm%d" % i for i in range(10)], ["kp"])
-        cast(2)
-        cast(3)
-        tt(T.sf[:], T.kp[:].indirect(T.selk[:, 0:1]), T.lwi[:], ALU.max, ["kp", "selk", "lwi"], ["sf"])
-        cast(0)
-        copy("V", T.so[:], T.sf[:], ["sf"], ["so"])
-        cast(1)
-        for q in (4, 3): scatter(q)
+            else: act(T.ht[:, b::4], ps(4 + b, 0, K), ACT.Copy, 0.03125, 0.0, ["ps%d" % (4 + b)], ["ht%d" % b])
+        at("ho")
         quant(hc, hs, 0, K, T.ht[:], ["ht%d" % b for b in four], ["ho"])
-        send(partner, "ah%d" % t, [(hc[:, K:C].bitcast(dt.uint8), hc[:, 0:K].bitcast(dt.uint8)), (hs[:, K:C], hs[:, 0:K])], ["ho"])
-        arrives(giver, "ah%d" % t, 2, ["hl"])
-        for q in (2, 1, 0): scatter(q)
+        exchange(partner, giver, "ah%d" % t, [(hc[:, K:C].bitcast(dt.uint8), hc[:, 0:K].bitcast(dt.uint8)), (hs[:, K:C], hs[:, 0:K])], ["ho"], ["hl"])
         for b in four:
+            at("mo")
             mm(4 + b, T.ec, T.es, 128 * b, hc, hs, 0, K, ["ec%d" % b, "ho"])
+            at("eo")
             copy("S", T.est[:, EW * b:EW * b + K], ps(4 + b, 0, K), ["ps%d" % (4 + b)], ["eo%d" % b])
+        at("x1")
+        copy("S", T.x1[:], T.idt[:].indirect(lw), ["lwu", "idt"], ["x1"])
+        for e in range(2):
+            at("eq%d" % e)
+            tt(T.eq[:, K * e:K * e + K], T.lwi[:].indirect(T.selx[:, 10 * e:10 * e + 10]), T.x1[:], ALU.is_equal, ["lwi", "selx", "x1"], ["eq%d" % e])
+        at("kp")
+        scan(T.kp[:], T.cm[:], T.eq[:], 0.0, ALU.mult, ALU.max, ["eq0", "eq1"] + ["cm%d" % i for i in range(10)], ["kp"])
+        at("sf")
+        tt(T.sf[:], T.kp[:].indirect(T.selk[:, 0:1]), T.lwi[:], ALU.max, ["kp", "selk", "lwi"], ["sf"])
+        at("so")
+        copy("V", T.so[:], T.sf[:], ["sf"], ["so"])
+        for q in (4, 3, 2, 1, 0):
+            at("sc%d" % q)
+            copy("V", T.sw[:, SW * (q % 2):SW * (q % 2) + SW].indirect(T.so[:, 2 * q:2 * q + 2]), T.sval[:, 32 * q:32 * q + 32], ["so", "sval"], ["sw%d" % (q % 2)])
+        nn = lambda i: gs[:, 0:10] if i == 2 else T.nn[:, 10 * i:10 * i + 10]
+        for i, (a, b, c) in ((2, (C, PL, 1)), (1, (1, C, 2)), (0, (0, C, 2))):
+            for h in range(2):
+                at("n%d%d" % (i, h))
+                o = SW * h + SH
+                scan(T.ns[:, PL * h + K * i:PL * h + K * i + K], T.c16[:], T.sw[:, o + a:o + b:c], 0.0, ALU.mult, ALU.max, ["sw%d" % h, "c16a", "c16b"], ["ns%d_%d" % (i, h)])
+            at("gs" if i == 2 else "nn%d" % i)
+            tt(nn(i), T.ns[:, K * i + 15:K * i + K:16], T.ns[:, PL + K * i + 15:PL + K * i + K:16], ALU.max, ["ns%d_0" % i, "ns%d_1" % i], ["gs" if i == 2 else "ns%d" % i])
+        exchange(partner, giver, "ag%d" % t, [(gl[:, 0:10], gs[:, 0:10])], ["gs"], ["gl"])
+        at("offo")
+        ts(T.offo[:, 0:10], nn(1), pf(13), ALU.mult, K + 0.4, ALU.add, ["ns1", "pf13"], ["offo"])
+        at("ff")
+        ts(T.ff[:, 0:10], nn(0), pf(14), ALU.is_ge, pf(15), ALU.mult, ["ns0", "pf14", "pf15"], ["ff"])
+        at("oo")
+        tt(T.oo[:, 0:10], T.ff[:, 0:10], nn(0), ALU.add, ["ff", "ns0"], ["oo"])
 
-        def first(h, i, a, b, c):
-            o = SW * h + SH
-            scan(T.ns[:, PL * h + K * i:PL * h + K * i + K], T.c16[:], T.sw[:, o + a:o + b:c], 0.0, ALU.mult, ALU.max, ["sw%d" % h, "c16"], ["ns%d_%d" % (i, h)])
-
-        def both(o, i, w): tt(o, T.ns[:, K * i + 15:K * i + K:16], T.ns[:, PL + K * i + 15:PL + K * i + K:16], ALU.max, ["ns%d_0" % i, "ns%d_1" % i], [w])
-        first(1, 2, C, PL, 1)
-        first(0, 2, C, PL, 1)
-        first(1, 1, 1, C, 2)
-        both(gs[:, 0:10], 2, "gs")
-        send(partner, "ag%d" % t, [(gl[:, 0:10], gs[:, 0:10])], ["gs"])
-        arrives(giver, "ag%d" % t, 1, ["gl"])
-        first(0, 1, 1, C, 2)
-        first(1, 0, 0, C, 2)
-        both(T.nn[:, 10:20], 1, "nn1")
-        first(0, 0, 0, C, 2)
-        ts(T.offo[:, 0:10], T.nn[:, 10:20], pf(13), ALU.mult, K + 0.4, ALU.add, ["nn1", "pf13"], ["offo"])
-        both(T.nn[:, 0:10], 0, "nn0")
-        for b in (2, 3):
-            mm(b, T.ec, T.es, 128 * b, wc, ws, K, K, ["ec%d" % b, "wo"])
-            copy("S", T.ao[:, K * b - C:K * b - K], T.est[:, EW * b:EW * b + K + 1].indirect(T.offo[:, 0:10]), ["offo", "eo%d" % b, "ez%d" % b], ["ao%d" % b])
+        def renew(e, how, width, off, buf, r):
+            for b in four:
+                a = T.est[:, EW * b:EW * b + width].indirect(off[:, 0:10])
+                o, w = (T.xf[:, 4 * e + b::8], "y") if final else (T.xt[:, 4 * K * e + b:4 * K * (e + 1):4], "x")
+                w, rb = [w + "eo"[e] + str(b)], [x % b if "%" in x else x for x in r]
+                if how[b] == "V":
+                    at("x" + "eo"[e] + str(b))
+                    tt(o, a, T.vp[:, PV * b + SH + e:PV * b + SH + C:2], ALU.add, rb + ["vp%d_%d" % (b, e)], w)
+                else:
+                    bank = b if e else (b + 2) % 4
+                    at("d" + "eo"[e])
+                    mm(bank, T.ec, T.es, 128 * b, wc, ws, K * e, K, ["ec%d" % b, "we", "wo"])
+                    at("a" + "eo"[e])
+                    copy("S", buf[:, K * b:K * b + K], a, rb, ["a%d%d" % (e, b)])
+                    at("x" + "eo"[e] + str(b))
+                    tt(o, ps(bank, 0, K), buf[:, K * b:K * b + K], ALU.add, ["ps%d" % bank, "a%d%d" % (e, b)], w)
+        renew(1, "VVSS", K + 1, T.offo, T.ao, ["offo", "eo%d", "ez%d"])
         for b in four:
-            o, w = (T.xf[:, 4 + b::8], ["yo%d" % b]) if final else (T.xt[:, 4 * K + b:4 * C:4], ["xo%d" % b])
-            if b > 1: tt(o, ps(b, 0, K), T.ao[:, K * b - C:K * b - K], ALU.add, ["ps%d" % b, "ao%d" % b], w)
-            else: tt(o, T.est[:, EW * b:EW * b + K + 1].indirect(T.offo[:, 0:10]), T.vp[:, PV * b + SH + 1:PV * b + SH + C:2], ALU.add,
-                     ["offo", "eo%d" % b, "ez%d" % b, "vp%d_1" % b], w)
-            if b == 1: ts(T.ff[:, 0:10], T.nn[:, 0:10], pf(14), ALU.is_ge, pf(15), ALU.mult, ["nn0", "pf14", "pf15"], ["ff"])
-            if b == 2: tt(T.oo[:, 0:10], T.ff[:, 0:10], T.nn[:, 0:10], ALU.add, ["ff", "nn0"], ["oo"])
-        for b in four:
+            at("mg")
             mm(4 + b, T.ec, T.es, 128 * b, hc, hs, K, K, ["ec%d" % b, "hl"])
+            at("eg")
             copy("S", T.est[:, EW * b + OWN:EW * b + OWN + K], ps(4 + b, 0, K), ["ps%d" % (4 + b)], ["eg%d" % b])
+        at("em")
         tt(T.em[:, 0:10], T.oo[:, 0:10], gl[:, 0:10], ALU.max, ["oo", "gl"], ["em"])
-        if not final:
-            for i in range(3): repeat(i, "G")
-            odd_columns(t + 1)
+        at("offe")
         ts(T.offe[:, 0:10], T.em[:, 0:10], pf(13), ALU.mult, OWN + K + 0.4, ALU.add, ["em", "pf13"], ["offe"])
-        mm(1, T.ec, T.es, 384, wc, ws, 0, K, ["ec3", "we"])
-        for b in (3, 0, 1, 2, 4):
-            a = T.est[:, EW * b:EW * b + OWN + 1 + K].indirect(T.offe[:, 0:10]) if b < 4 else None
-            r = ["offe", "eo%d" % b, "eg%d" % b, "ez", "ez%d" % b]
-            c = min(b, 3)
-            o, w = (T.xf[:, c::8], ["ye%d" % c]) if final else (T.xt[:, c:4 * K:4], ["xe%d" % c])
-            if b == 3: copy("S", T.ao[:, 0:K], a, r, ["ao2"])
-            elif b == 4: tt(o, ps(1, 0, K), T.ao[:, 0:K], ALU.add, ["ps1", "ao2"], w)
-            else: tt(o, a, T.vp[:, PV * b + SH:PV * b + SH + C:2], ALU.add, r + ["vp%d_0" % b], w)
-        if not final: repeated_columns(t + 1)
+        renew(0, "VVVS", OWN + 1 + K, T.offe, T.ae, ["offe", "eo%d", "eg%d", "ez", "ez%d"])
+        if not final: odd_columns(t + 1)
 
-    quant(T.fc, T.fs, 0, C, T.xf[:], ["ye%d" % b for b in four] + ["yo%d" % b for b in four], ["fc"])
-    for h in range(2): mm(h, T.vc, T.vs, 0, T.fc, T.fs, K * h, K, ["vc", "fc"])
-    dma("Y", "doc", [(T.oc[:], T.fc[:].bitcast(dt.uint8))], ["fc"])
-    dma("Y", "dos", [(T.osc[4 * q:4 * q + 4, :], T.fs[32 * q:32 * q + 4, :]) for q in four], ["fc"])
-    for h in range(2): copy("VS"[h], T.ysb[:, K * h:K * h + K], ps(h, 0, K), ["ps%d" % h], ["ysb%d" % h])
+    for h in range(2):
+        at("fc")
+        quant(T.fc, T.fs, K * h, K * h + K, T.xf[:, 4 * K * h:4 * K * (h + 1)], ["ye%d" % b for b in four] + ["yo%d" % b for b in four], ["fc%d" % h])
+        at("my")
+        mm(h, T.vc, T.vs, 0, T.fc, T.fs, K * h, K, ["vc", "fc%d" % h])
+        at("ysb")
+        copy("SV"[h], T.ysb[:, K * h:K * h + K], ps(h, 0, K), ["ps%d" % h], ["ysb%d" % h])
+    at("oc")
+    dma("Y", "doc", [(T.oc[:], T.fc[:].bitcast(dt.uint8))], ["fc0", "fc1"])
+    dma("Y", "dos", [(T.osc[4 * q:4 * q + 4, :], T.fs[32 * q:32 * q + 4, :]) for q in four], ["fc0", "fc1"])
+    at("y")
     dma("S", "dy", [(T.y[:], T.ysb[:])], ["ysb0", "ysb1"])
+
+    queue = {e: sorted((i for i, c in enumerate(calls) if c[0] == e), key=lambda i: (order[e].index(calls[i][1]), i), reverse=True) for e in Q}
+    queue[None] = [i for i, c in enumerate(calls) if c[0] is None]
+    done = {}
+    known = {e: 0 for e in queue}
+    count, last, waited = {}, {}, {}
+    while any(queue.values()):
+        e = [e for e in queue if queue[e] and calls[queue[e][-1]][3] <= done.keys()][-1]
+        i = queue[e].pop()
+        before = [p for p in done if done[p][0] == "g0"][-1:] if e == "G" else []
+        for p in sorted(calls[i][3] | {p for p in before if (p in narrow) != (i in narrow) and calls[i][1][0] not in ("at", "ah", "ag")}, key=lambda p: -done[p][3]):
+            if not known[e] >> p & 1:
+                s, c, k, _ = done[p]
+                Q[e].wait_ge(T.sem[s], c)
+                waited[s] = max(waited.get(s, 0), c)
+                known[e] |= k
+        _, s, c = calls[i][2]()
+        count[s] = count.get(s, 0) + c
+        last[s] = known[e] | 1 << i | last.get(s, 0)
+        done[i] = (s, count[s], last[s], len(done))
     for s in sorted(count, key=lambda s: s in DMAS):
         if waited.get(s, 0) < count[s]:
             Q[s[0].upper() if s in ("v0", "s0", "p0") else "G"].wait_ge(T.sem[s], count[s])

@@ -7,45 +7,50 @@ BIG = 1e29
 KB = 100.0
 W1, W3, WA, WK, WD = 484, 244, 484, 124, 36
 LOW, HI, PA = 1, 161, 321
-LAND = 416
 EW = 352
 OWN = 176
+LIFT = 1024.0
 SH = 16
-PV, SW = PL + SH, 640
+PV, SW = PL + SH, 768
+JOIN = (2, 4, 5, 6, 7, 8)
+XO, XE = "VVSS", "VVSV"
 X4, U8, BF, F32, F16, I32, U16 = "float8_e4m3fn_x4", "uint8", "bfloat16", "float32", "float16", "int32", "uint16"
 SCRATCH = {"ps": ("psum", [128, 4096], F32)}
 for _d, _l in {
-    BF: dict(xin=1280, xt=4 * LAND, xf=1280, vin=512, et=516, vp=4 * PV, zt=640, ht=640, est=4 * EW,
-             sval=K, ao=4 * K, ae=4 * K, eq=C, kp=C, cm=C, cb=64, i16=K, c16=K, ca=K, cc=K, sw=2 * SW, ns=2 * PL, d0=1800),
-    X4: dict(lc=512, vc=128, ec=512, fc=C, zc=K, wc0=576, wc1=576, wc2=576, hc0=C, hc1=C, hc2=C),
-    U8: dict(ls=512, vs=128, es=512, fs=C, zs=K, ws0=576, ws1=576, ws2=576, hs0=C, hs1=C, hs2=C),
-    F32: dict(ysb=C, s1=PL, sa=448, m1=8 * W1, cv=240, md=9 * W3, big=K, mk1=K, mk2=K, ob=16, vv=64,
-              idt=512, x1=K, sf=16, nn=20, ff=16, oo=16, em=16, pf=24, sxi=20, opf=64,
+    BF: dict(xin=1280, xt=4 * C, xf=1280, vin=512, et=516, vp=4 * PV, zt=640, ht=640, est=4 * EW,
+             sval=K, ao=4 * K, ae=4 * K, rt=768, ci=330, sw=2 * SW, d0=1800),
+    X4: dict(lc=512, rc=192, vc=128, ec=512, fc=C, zc=K, wc0=PL, wc1=PL, wc2=PL, hc0=C, hc1=C, hc2=C),
+    U8: dict(ls=512, rs=192, vs=128, es=512, fs=C, zs=K, ws0=PL, ws1=PL, ws2=PL, hs0=C, hs1=C, hs2=C),
+    F32: dict(ysb=C, s1=PL, sa=C, m1=8 * W1, cv=240, sb=128, md=9 * W3, big=256, mk1=K, mk2=K, ob=16, vv=64, in1=64, out1=64, o32=64,
+              idt=512, nb=16, nn=20, oo=16, em=16, pf=24, sri=10, opf=64,
               gs0=16, gs1=16, gs2=16, gl0=16, gl1=16, gl2=16),
-    F16: dict(neg=240, b2=128, bb=8 * WD, d1=1800, k1=1800, n1=8 * WA, n2=8 * WK, in1=64, out1=64, o32=64),
-    I32: dict(lwi=16, pi=8, cl=4, cw=40),
-    U16: dict(lwu=16, so=16, offe=16, offo=16, selk=2, selb=8, selx=20),
+    F16: dict(eq=330, kp=330, cm=496, ns=2 * PL, x0=K, x1=K, neg=240, b2=32 * len(JOIN), bb=8 * WD, d1=1800, k1=1800, n1=8 * WA, n2=8 * WK),
+    I32: dict(pi=8, cl=6, cw=40),
+    U16: dict(lwu=16, so=16, offe=16, offo=16, selb=8, selr=10),
 }.items():
     for _k, _n in _l.items(): SCRATCH[_k] = ("sbuf", [128, _n], _d)
-DMAS = ["dx", "dl", "dls", "dv", "dop", "doc", "dos", "dy"]
+DMAS = ["dx", "dc", "dl", "dls", "dv", "dop", "doc", "dos", "dy"]
 SEMAPHORES = ["v0", "s0", "p0", "g0"] + DMAS + ["sent"] + ["%s%d" % (k, t) for k in ("at", "ah", "ag") for t in range(R)]
-ORDER = {
-    "V": """c0 xe xo we wo wr s1 own* lo own hi l0 x0 l1 x1 h0 l2 x2 h1 l3 x3 h2 c3 x4 h3 Q0 p0 x5 Q1 p1 Q2 h4 x6 Q3 h5 p2 Q4 x7 v1 p3 Q5 h6 Q6
-         p4 Q7 v3 p5 h7 p6 v5 v7 p7 u7 w7 k4 k0 k1 n0 k2 a0 n1 a1 b0 n2 a2 b1 n3 d0 a3 n4 b2 a4 n5 d1 b3 a5 n6 d2 b4 a6 d3 n7 b5 d4 c8 b6 d5
-         a7 w6 d6 b7 u6 d7 fl T3 U3 fr c9 c7 out1 c6 vc o32 lwu lwi""",
-    "S": "xe xo xr c2 r0 s11 c0 vp cv s2p s12 e1 ob4 lift g1 e3 g0 ob8 g3 e5 g5 g7 f0 f1 f2 f3 c4 j0 vq j1 j2 U0 U1 j3 T2 U2 opf",
-    "G": "c0 at c1 sw T0 T1 c4",
-    "P": "moo meo mor mer meo2 dt mpr mp mp2 dp",
-    "Y": "x w op"}
+FAR = {
+    "V": """ca cb cc cd xe xo we wo ce wr s1 cf lo hi own l0 x0 l1 h0 l2 h1 x1 l3 h2 x2 h3 x3 p0 h4 Q0 p1 h5 Q1 p2 x4 Q2 p3 x5 Q3 p4 h6 Q4 x6
+         p5 Q5 v1 h7 p6 x7 Q6 p7 v3 Q7 v5 v7 w7 k0 k1 k4 a0 k2 n0 a1 b0 n1 a2 b1 n2 a3 b2 n3 d0 a4 b3 n4 d1 a5 b4 n5 d2 a6 b5 d3 n6 b6 d4 n7
+         a7 d5 u7 fl w6 b7 d6 c5 fr u6 d7 T3 U2 U3 out1 o32 lwu y1 zt0 zt1 zc kp ht0 so ht1 sc4 ho sc3 sc2 sc1 sc0 i01 i21 i20 i10 i11 gs
+         i00 nn1 nn0 offo vc xo1 xo0 xo2 em xo3 offe wo+ xe1 xe0 xe3 xe2 fc ysb""",
+    "S": """ca xe xo xr cd c2 s11 re vp0 c0 vp1 s12 cv e1 s2p lift ob4 e3 g1 e5 g0 f0 f1 g3 g5 g7 f2 f3 j0 j1 j2 U0 j3 T2 U1 j4 j5 vq y0
+         lwf nb zt3 zt2 eq1 eq0 ht2 ht3 eo ao2 oo ao3 eg0 eg1 eg2 opf eg3 ae2 ysb y""",
+    "G": "ca at cb c1 c3 T0 T1 sw ah ag xr+",
+    "P": "moo meo meo2 mor mer dt mp mpr mpr2 mp2 do dp mh mo mg moo+ my",
+    "Y": "x w c4 op oc os"}
 NEAR = {
-    "V": """zt eq1 eq0 zc kp sf ht0 so ht1 sc4 sc3 sc2 ho sc1 sc0 n11 n21 n10 n20 n00 n01 nn1 gs nn0 offo ff xo1 xo0 oo xo2 xo3
-         em offe wo+ xe0 xe2 xe1 xe3 wr+ fc ysb""",
-    "S": "x1 zt ht2 ht3 eo ao eg ae ysb y",
-    "G": "ah ag xr+",
-    "P": "do mh de mo mg moo+ mor+ my",
-    "Y": "oc"}
-FAR = dict(NEAR, V="""zt eq1 eq0 zc kp sf ht0 so ht1 sc4 sc3 ho sc2 sc1 sc0 n21 n11 n20 n10 n01 n00 gs nn1 nn0 offo ff xo1 xo0 oo xo2 xo3
-         em offe wo+ xe1 xe2 xe0 xe3 wr+ fc ysb""")
+    "V": """wr we s1 own lo hi l0 x0 l1 h0 x1 l2 h1 x2 l3 Q0 p0 h2 Q1 p1 h3 Q2 p2 x3 h4 p3 x4 Q3 h5 p4 Q4 x5 h6 p5 x6 h7 Q5 p6 x7 Q6 v1 p7 v3
+         Q7 v5 w7 v7 k0 k1 k2 a0 k4 u7 a1 n0 b0 a2 n1 b1 a3 n2 b2 a4 n3 d0 b3 a5 n4 d1 b4 a6 n5 d2 b5 n6 d3 b6 n7 d4 a7 w6 d5 fl b7 d6 fr u6
+         d7 T3 U2 U3 out1 o32 y1 lwu zt1 zt0 zt2 kp zc so sc4 sc3 sc2 ht0 sc1 sc0 ho i21 i10 i20 i11 gs nn1 i00 i01 offo nn0
+         xo0 xo1 xo2 em xo3 offe wo+ xe1 xe0 xe3 xe2""",
+    "S": """re s11 vp0 cv vp1 s12 s2p e1 ob4 lift e3 e5 g1 f0 f1 f2 f3 g3 g5 g7 g0 j0 j1 j2 U0 j3 T2 U1 j4 j5 vq y0 nb lwf eq0 eq1 zt3
+         ht2 ht1 ht3 eo ao2 oo ao3 eg1 eg2 eg0 eg3 ae2""",
+    "G": "at sw T0 T1 ah ag xr+",
+    "P": "mor meo mer meo2 dt mpr mp mp2 mpr2 do dp mh mo mg moo+",
+    "Y": ""}
 
 
 def rank_program(g, core, T, topo):
@@ -106,15 +111,18 @@ def rank_program(g, core, T, topo):
 
     def tt(o, a, b, o0, r, w): op("V", lambda: V.tensor_tensor(o, a, b, o0), r, w)
     def scan(o, a, b, init, o0, o1, r, w): op("V", lambda: V.tensor_tensor_scan(o, a, b, init, o0, o1), r, w)
+    def turn(o, i, r, w): op("V", lambda: V.transpose(o, i), r, w)
     def fill(o, c, w, r=()): op("V", lambda: V.memset(o, c), r, w)
     def act(o, i, func, scale, bias, r, w): op("S", lambda: S.activation(o, i, func, bias=bias, scale=scale), r, w)
     def affine(o, i, scale, bias, r, w): act(o, i, ACT.Identity, scale, bias, r, w)
     def sign(o, i, v, r, w): act(o, i, ACT.Sign, -1.0, v, r, w)
     def quant(c, s, a, b, i, r, w): op("V", lambda: V.quantize_mx(c[:, a:b], s[:, a:b], i), r, w)
 
-    def mm(bank, lc, ls, a, rc, rs, b, m, r):
-        op("P", lambda: g.tensor.matmul_mx(T.ps[:, 512 * bank:512 * bank + m], lc[:, a:a + 128], ls[:, a:a + 128],
-                                           rc[:, b:b + m], rs[:, b:b + m], True, True), r, ["ps%d" % bank])
+    def mms(bank, lc, ls, rc, rs, terms, m, r):
+        record("P", lambda: ([g.tensor.matmul_mx(T.ps[:, 512 * bank:512 * bank + m], lc[:, a:a + 128], ls[:, a:a + 128], rc[:, b:b + m], rs[:, b:b + m],
+                                                 i == 0, i == len(terms) - 1).then_inc(T.sem.p0, 1) for i, (a, b) in enumerate(terms)], "p0", len(terms)), r, ["ps%d" % bank])
+
+    def mm(bank, lc, ls, a, rc, rs, b, m, r): mms(bank, lc, ls, rc, rs, [(a, b)], m, r)
 
     def ps(bank, a, b, p=0, q=128): return T.ps[p:q, 512 * bank + a:512 * bank + b]
 
@@ -140,107 +148,100 @@ def rank_program(g, core, T, topo):
     ET = ["et0"]
     quarter = lambda q: slice(32 * q, 32 * q + 32)
     half = lambda h: slice(64 * h, 64 * h + 64)
-    BP, LO = 8, 128
-    XE, XO = ["xe%d" % b for b in four], ["xo%d" % b for b in four]
+    BP = 8
+    LOWER, UPPER = 64, 0
+    XEN, XON = ["xe%d" % b for b in four], ["xo%d" % b for b in four]
     F = ["f%d" % i for i in range(6)]
     IN = ["in%d_%d" % (q, i) for q in four for i in range(5)]
     M1, MD = ["c1", "c3", "big"], ["c4", "c9"]
 
     at("x")
     dma("Y", "dx", [(T.xin[:], T.x[:])], (), ["xin"])
-    at("c0")
+
+    def const(o, m, c, w): affine(o, T.big[:, 0:m], 0.0, c, ["big"], w)
+    at("ca")
     iota(T.pi[:, 0:1], [[0, 1]], 0, 1, ["pi0"], False)
-    iota(T.idt[:], [[1, 512]], 0, 0, ["idt"])
-    fill(T.et[:], 0.0, ["et"])
+    iota(T.idt[:, 0:128], [[1, 128]], 0, 0, ["id0"])
     fill(T.big[:], BIG, ["big"])
+    fill(T.et[:], 0.0, ["et"])
+    for c, w in enumerate([["xz0"], ["xr0", "xr1"], ["xz1"]]): const(T.rt[:, 256 * c:256 * c + 256], 256, 0.0, w)
+    const(T.m1[:, 4 * W1 + HI::W1], 4, -BIG, ["c1"])
+    const(T.m1[:, LOW::W1], 8, -BIG, ["c3"])
+    const(T.md[:, W3::W3], 8, -BIG, ["c9"])
+    const(T.md[:, 0:W3], W3, BIG, ["c4"])
     select(T.mk1[:], T.big[:, 0:K], [[-1, K]], ALU.not_equal, -BIG, 0, 1, ["big"], ["mk1"])
+    iota(T.idt[:, 128:], [[1, 384]], 128, 0, ["idt"])
+    at("cb")
     for q in (2, 3): select(T.mk2[quarter(q), :], T.big[quarter(q), 0:K], [[-1, K]], ALU.not_equal, -BIG, 128, 1, ["big"], ["mk%d" % q], True)
-    for c, (sh, m) in enumerate([(0, 15), (5, 3), (0, 1), (1, 7), (5, 1), (6, 1)]):
+    for c, (sh, m) in enumerate([(0, 15), (5, 3), (5, 1), (6, 1)]):
         ts(T.pi[:, c + 1:c + 2], T.pi[:, 0:1], sh, ALU.logical_shift_right, m, ALU.bitwise_and, ["pi0"], ["pi%d" % (c + 1)])
-    copy("V", T.pf[:, 0:7], T.pi[:, 0:7], ["pi%d" % c for c in range(7)], ["pf"])
-    fill(T.m1[:, 4 * W1 + HI::W1], -BIG, ["c1"])
-    fill(T.m1[:, LOW::W1], -BIG, ["c3"])
-    ts(pf(16), pf(5), float(K), ALU.mult, pf(6), ALU.add, ["pf"], ["pf16"])
-    ts(pf(17), qq, 40.0 / 512, ALU.mult, 1 + (C + SH) / 512, ALU.add, ["pf"], ["pf17"])
-    ts(pf(18), pf(5), 40.0, ALU.mult, j, ALU.add, ["pf"], ["pf18"])
-    fill(T.md[:, W3::W3], -BIG, ["c9"])
-    ts(pf(20), pf(5), 80.0, ALU.mult, j, ALU.add, ["pf"], ["pf20"])
-    ts(T.et[:, 3:515:4], T.idt[:, 0:128], pf(0), ALU.is_equal, r=["idt", "pf", "et"], w=ET)
-    ts(pf(16), pf(16), 512.0 + SH, ALU.add, 1.0 / 512, ALU.mult, ["pf16"], ["pf16"])
-    ts(pf(18), pf(18), K - 8.0, ALU.add, r=["pf18"], w=["pf18"])
+    at("cc")
+    copy("V", T.pf[:, 0:5], T.pi[:, 0:5], ["pi%d" % c for c in range(5)], ["pf"])
+    at("cd")
+    ts(T.et[:, 3:515:4], T.idt[:, 0:128], pf(0), ALU.is_equal, r=["id0", "pf", "et"], w=ET)
     ts(pf(19), j, 15.0, ALU.is_equal, r=["pf"], w=["pf19"])
+    quant(T.rc, T.rs, 0, 128, T.rt[:, 0:512], ["xz0", "xr0", "xr1"], ["wr"])
+    affine(pf(15), pf(4), 1.0 / 512, 1 + SH / 512, ["pf"], ["pf15"])
+    affine(pf(17), qq, 40.0 / 512, 1 + (C + SH) / 512, ["pf"], ["pf17"])
+    affine(pf(18), pf(3), 40.0, j, ["pf"], ["pf18"])
+    affine(pf(20), pf(3), 80.0, j, ["pf"], ["pf20"])
+    affine(pf(16), pf(3), K / 512, pf(15), ["pf15"], ["pf16"])
+    at("ce")
     for b in four: quant(T.ec, T.es, 128 * b, 128 * b + 128, T.et[:, 3 - b:515 - b], ET, ["ec%d" % b])
-    ts(T.selb[:, 0:3], T.idt[:, 0:48:16], pf(18), ALU.add, r=["idt", "pf18"], w=["selb"])
-    ts(T.selb[:, 3:8], T.idt[:, 0:80:16], pf(20), ALU.add, r=["idt", "pf20"], w=["selc"])
-    fill(T.in1[:], 0.0, IN)
+    at("cf")
+    ts(T.selb[:, 0:3], T.idt[:, 0:48:16], pf(18), ALU.add, K - 8.0, ALU.add, ["id0", "pf18"], ["selb"])
+    ts(T.selb[:, 3:8], T.idt[:, 0:80:16], pf(20), ALU.add, r=["id0", "pf20"], w=["selc"])
+    at("c0")
     for c, a in enumerate([T.idt[:, 1:C:2], T.idt[:, 0:C:2], T.idt[:, C:PL]]):
-        affine(T.d1[:, PL * c + 2:PL * c + PL:3], a, 1.0 / 512, 1 + SH / 512, ["idt"], ["f%d" % c])
-    affine(T.d1[:, 3 * PL + 2:3 * PL + 120:3], T.idt[:, 0:40], 1.0 / 512, pf(17), ["idt", "pf17"], ["f3"])
-    affine(T.d1[:, 3 * PL + 122::3], T.idt[:, 0:K:2], 1.0 / 512, pf(16), ["idt", "pf16"], ["f4"])
+        affine(T.d1[:, PL * c + 2:PL * c + PL:3], a, 1.0 / 512, 1 + SH / 512, ["id0", "idt"], ["f%d" % c])
+    affine(T.d1[:, 3 * PL + 2:3 * PL + 120:3], T.idt[:, 0:40], 1.0 / 512, pf(17), ["id0", "pf17"], ["f3"])
+    affine(T.d1[:, 3 * PL + 122::3], T.idt[:, 0:K:2], 1.0 / 512, pf(16), ["id0", "idt", "pf16"], ["f4"])
     at("xe")
     for b in four: copy("VVVS"[b], T.xt[:, b:4 * K:4], T.xin[:, b::8], ["xin"], ["xe%d" % b])
     at("xo")
     for b in four: copy("SSVV"[b], T.xt[:, 4 * K + b:4 * C:4], T.xin[:, 4 + b::8], ["xin"], ["xo%d" % b])
-
-    def const(o, m, c, w): affine(o, T.idt[:, 0:m], 0.0, c, ["idt"], w)
     at("c1")
-    iota(T.i16[:], [[0, 10], [1, 16]], 0, 0, ["i16"])
     whole(T.d0[:, 0::3], 600, 0, ["f5"])
-    iota(T.sxi[:], [[1, 2], [2, 5], [0, 2]], 0, 0, ["sxi"])
+    iota(T.sri[:], [[1, 5], [32, 2]], 0, 0, ["sri"])
     iota(T.sval[:], [[-1, K]], K, 0, ["sval"])
     for b in four:
         whole(T.vp[:, PV * b:PV * b + SH], SH, 0, ["vz%d" % b])
         whole(T.est[:, b * EW + K:b * EW + OWN], OWN - K, 0, ["ez%d" % b])
     whole(T.est[:, OWN + K::EW], 4, 0, ["ez"])
     at("c2")
-    for c, (o, m) in enumerate([(T.n1[:, 0::WA], 8), (T.n2[:, 0::WK], 8), (T.bb[:, 0::WD], 8), (T.b2[:], 128)]): const(o, m, KB, ["c%d" % (5 + c)])
-    const(T.md[:, 0:W3], W3, BIG, ["c4"])
+    for c, (o, m) in enumerate([(T.n1[:, 0::WA], 8), (T.n2[:, 0::WK], 8), (T.bb[:, 0::WD], 8), (T.b2[:], 32 * len(JOIN))]): const(o, m, KB, ["c%d" % (5 + c)])
     const(T.ob[:, 8:9], 1, BIG, ["ob"])
-    affine(pf(7), j, 1.0, 1.0, ["pf"], ["pf7"])
-    affine(pf(8), j, 4.0, 512.0, ["pf"], ["pf8"])
-    affine(pf(9), j, 4.0, 576.0, ["pf"], ["pf9"])
-    affine(pf(12), pf(19), 1 - 2.0 ** -12, 2.0 ** -12, ["pf19"], ["pf12"])
+    const(T.neg[:], 240, -KB, ["ck"])
+    const(T.in1[:], 64, 0.0, IN)
+    affine(pf(13), pf(19), -LIFT, LIFT + K, ["pf19"], ["pf13"])
+    affine(pf(14), pf(19), -LIFT, LIFT + K + OWN, ["pf19"], ["pf14"])
     at("c3")
-    for c, (a, by) in enumerate([(j, 4096.0), (j, pf(8)), (pf(7), 4096.0), (j, pf(9))]):
-        ts(T.cb[:, 16 * c:16 * c + 16], T.i16[:, 0:16], a, ALU.is_equal, by, ALU.mult, ["i16", "pf7", "pf8", "pf9"], ["cb%d" % c])
-    ts(T.ca[:], T.i16[:], j, ALU.not_equal, r=["i16", "pf"], w=["ca"])
-    ts(T.cc[:], T.i16[:], pf(7), ALU.is_equal, 512.0, ALU.mult, ["i16", "pf7"], ["cc"])
-    fill(T.neg[:], -KB, ["ck"], ["c5", "c6", "c7", "c8"])
-    ts(T.cb[:], T.cb[:], 1.0, ALU.max, r=["cb%d" % c for c in four], w=["cb"])
+    low = lambda a, b: T.cm[0:32, a:b]
+    iota(T.ci[:], [[0, 10], [-1, 33]], -64, 0, ["ci"])
+    select(low(0, 330), T.ci[0:32, :], [[0, 5], [-1, 2], [1, 33]], ALU.is_equal, 0.0, 0, -2, ["ci"], ["cm"], True)
+    select(low(0, 330), low(0, 330), [[0, 10], [1, 33]], ALU.not_equal, 60000.0, 0, 0, [], ["cm"], True)
+    select(low(336, 496), T.rt[0:32, 0:K], [[0, 10], [1, 16]], ALU.not_equal, -4 * LIFT, 0, -1, ["xz0"], ["cn"], True)
+    select(low(336, 496), low(336, 496), [[0, 10], [1, 16]], ALU.not_equal, LIFT, -1, -1, [], ["cn"], True)
     at("c4")
-    affine(T.cb[:, 0::32], T.cb[:, 0::32], 0.0, 0.0, ["cb"], ["cc0"])
-    affine(T.cb[:, 16:17], T.cb[:, 16:17], 2.0 ** -12, 0.0, ["cb"], ["cc1"])
-    affine(T.cb[:, 48:49], T.cb[:, 48:49], pf(12), 0.0, ["cb", "pf12"], ["cc2"])
-    for c in range(10): copy("G", T.cm[:, 32 * c:32 * c + 32], T.cb[:, 32 * (c // 5):32 * (c // 5) + 32], ["cc0", "cc1", "cc2"], ["cm%d" % c], 32)
-    affine(pf(10), pf(3), float(K), 31.0, ["pf"], ["pf10"])
-    affine(pf(11), pf(4), 32.0, pf(10), ["pf10"], ["pf11"])
-    affine(pf(13), pf(19), -511.0 / 512, -1.0 / 512, ["pf19"], ["pf13"])
-    affine(pf(14), pf(19), -255.5, 256.0, ["pf19"], ["pf14"])
-    affine(pf(15), pf(19), -511.0 * OWN, 512.0 * OWN, ["pf19"], ["pf15"])
-    at("c6")
-    copy("V", T.selx[:], T.sxi[:], ["sxi"], ["selx"])
-    at("c7")
-    tt(T.c16[:, 0:80], T.ca[:, 0:80], T.cc[:, 0:80], ALU.max, ["ca", "cc"], ["c16a"])
-    at("c8")
-    ts(T.selk[:, 0:1], pf(11), float(C - 1), ALU.min, r=["pf11"], w=["selk"])
-    at("c9")
-    tt(T.c16[:, 80:K], T.ca[:, 80:K], T.cc[:, 80:K], ALU.max, ["ca", "cc"], ["c16b"])
+    dma("Y", "dc", [(T.cm[16 * q:16 * q + 16, a:b], T.cm[0:16, a:b]) for q in range(1, 8) for a, b in ((0, 330), (336, 496))], [], ["cm", "cn"])
+    at("c5")
+    copy("V", T.selr[:], T.sri[:], ["sri"], ["selr"])
 
     def odd_columns(t):
         wc, ws = wcs[t]
         now[0] = t
-        at("xr")
-        for i in range(3): copy("G" if t else "S", T.xt[:, 4 * (C + 32 * i):4 * (C + 32 * i + 32)], T.xt[:, 4 * 288:4 * C], XO, ["xr%d" % i], 128)
         at("wo")
-        quant(wc, ws, K, C, T.xt[:, 4 * K:4 * C], XO, ["wo"])
+        quant(wc, ws, K, C, T.xt[:, 4 * K:4 * C], XON, ["wo"])
         at("moo")
         mm(0, wc, ws, K, wc, ws, K, K, ["wo"])
         at("s1")
         tt(T.s1[:, 0:K], ps(0, 0, K), T.mk1[:], ALU.min, ["ps0", "mk1"], ["s1_0"])
+        at("xr")
+        for i in range(2): copy("G" if t else "S", T.rt[:, 256 + 128 * i:384 + 128 * i], T.xt[:, 4 * 288:4 * C], XON, ["xr%d" % i], 128)
         at("wr")
-        quant(wc, ws, 288, LAND, T.xt[:, 4 * 288:], XO + ["xr0", "xr1", "xr2"], ["wo"])
+        quant(T.rc, T.rs, 64, 192, T.rt[:, 256:768], ["xr0", "xr1", "xz1"], ["wr"])
         at("mor")
-        mm(3, wc, ws, 288, wc, ws, K, K, ["wo"])
+        mm(3, T.rc, T.rs, UPPER, wc, ws, K, K, ["wr", "wo"])
         at("own")
         tt(T.cv[64:128, 0:K], ps(3, 0, K, 64), T.mk2[64:128, :], ALU.min, ["ps3", "mk2", "mk3"], ["cv1"])
         now[0] = max(t - 1, 0)
@@ -251,41 +252,45 @@ def rank_program(g, core, T, topo):
         S1 = ["s1_0", "s1_1", "s1_2"]
         for k in four:
             at("l%d" % k)
-            level(T.m1, W1, k, LOW, K, T.sa[:, LO:LO + K], big, None, UP, M1 + ["lo"] + below("l%d", k), "l%d" % k)
+            level(T.m1, W1, k, LOW, K, T.sa[:, 0:K], big, None, UP, M1 + ["lo"] + below("l%d", k), "l%d" % k)
         for k in eight:
             at("h%d" % k)
-            level(T.m1, W1, k, HI, K, T.sa[:, LO + K:LO + C], big, None, UP, M1 + ["hi", "l%d" % min(k, 3)] + below("h%d", k), "h%d" % k)
+            level(T.m1, W1, k, HI, K, T.sa[:, K:C], big, None, UP, M1 + ["hi", "l%d" % min(k, 3)] + below("h%d", k), "h%d" % k)
         for k in eight:
             at("x%d" % k)
             level(T.md, W3, k + 1, 0, K, T.cv[:, 0:K], None, T.md[:, (k + 1) * W3:(k + 1) * W3 + 1], UP, MD + ["cv0", "cv1"] + below("x%d", k), "x%d" % k)
-        for name, bank, a in (("mp", 2, K), ("mpr", 0, 288), ("mp2", 3, K)):
+        for name, bank in (("mp", 2), ("mpr", 0), ("mp2", 3), ("mpr2", 1)):
             at(name)
-            mm(bank, wc, ws, a, wc, ws, LAND, K, ["wo", "wl"])
+            if bank > 1: mm(bank, wc, ws, K, wc, ws, C, K, ["wo", "wl"])
+            else: mms(bank, T.rc, T.rs, wc, ws, [(LOWER, C - 48), (UPPER, C + 32)], 128, ["wr", "wo", "wl"])
         if t == 0:
             at("w")
             dma("Y", "dl", [(T.lc[:].bitcast(dt.uint8), T.wc[:])], ["wl"], ["lc"])
             dma("Y", "dls", [(T.ls[:], T.ws[:])], (), ["ls"])
             dma("Y", "dv", [(T.vin[:], T.v[:])], (), ["vin"])
         at("cv")
-        for h in range(2): copy("S", T.cv[half(h), K:240], ps(0, 80 * h, 80 * h + 80, 64 * h, 64 * h + 64), ["ps0"], ["cvp%d" % h])
+        copy("S", T.cv[:, K:240], ps(1, 48, 128), ["ps1"], ["cvp"])
         at("s12")
         copy("S", T.s1[:, C:PL], ps(3, 0, K), ["ps3"], ["s1_2"])
         at("s2p")
-        copy("S", T.sa[:, 0:LO], T.cv[:].indirect(T.selb[:]), ["cv0", "cv1", "cvp0", "cvp1", "selb", "selc"], ["s2p"])
+        copy("S", T.sb[:], T.cv[:].indirect(T.selb[:]), ["cv0", "cv1", "cvp", "selb", "selc"], ["s2p"])
         for k in eight:
             at("p%d" % k)
             level(T.m1, W1, k, PA, K, ps(2, 0, K), big, -BIG, UP, M1 + ["ps2", "h%d" % k] + below("p%d", k), "p%d" % k)
         for k in eight:
             at("Q%d" % k)
-            level(T.md, W3, k + 1, K, 80, T.cv[:, K:240], None, None, UP, MD + ["cvp0", "cvp1", "x%d" % k] + below("md%d", k), "md%d" % k)
-        for lo, hi in ((0, 4), (4, 8)):
-            at("ob%d" % hi)
-            for h in range(2): copy("S", T.ob[half(h), 8 - hi:8 - lo], T.md[half(1 - h), hi * W3 + 240:lo * W3 + 240:-W3], ["md%d" % (hi - 1)], ["ob%d_%d" % (h, hi)])
+            level(T.md, W3, k + 1, K, 80, ps(0, 48, 128), None, None, UP, MD + ["ps0", "x%d" % k] + below("md%d", k), "md%d" % k)
+        at("ob4")
+        for h in range(2): copy("S", T.ob[half(h), 4:8], T.md[half(1 - h), 4 * W3 + 240:240:-W3], ["md3"], ["ob%d" % h])
         vv = lambda k: T.vv[:, 9 * k - 7:9 * k - 6]
-        for k in (1, 3, 5, 7):
+        for k in (1, 3):
             at("v%d" % k)
-            scan(T.vv[:, 8 * k - 8:9 * k - 6], T.md[:, 240:(k + 1) * W3 + 241:W3], T.ob[:, 7 - k:9], -BIG, ALU.max, ALU.min,
-                 MD + ["ob", "md%d" % k] + ["ob%d_%d" % (h, hi) for h in range(2) for hi in (4, 8)[:k // 4 + 1]], ["v%d" % k])
+            scan(T.vv[:, 8 * k - 8:9 * k - 6], T.md[:, 240:(k + 1) * W3 + 241:W3], T.ob[:, 7 - k:9], -BIG, ALU.max, ALU.min, MD + ["ob", "ob0", "ob1"], ["v%d" % k, "v%d_" % k])
+        for k in (5, 7):
+            at("v%d" % k)
+            for h in range(2):
+                scan(T.vv[half(h), 8 * k - 8:9 * k - 6], T.md[half(h), 240:(k + 1) * W3 + 241:W3], T.md[half(1 - h), (k + 1) * W3 + 240:239:-W3], -BIG, ALU.max, ALU.min,
+                     MD + ["md%d" % k], ["v%d" % k + "_" * h])
         slot = {1: (T.d1, 1), 3: (T.d1, 0), 5: (T.d0, 2), 7: (T.d0, 1)}
         for k in (1, 3, 5, 7):
             d, a = slot[k]
@@ -296,16 +301,16 @@ def rank_program(g, core, T, topo):
             at("lift")
             if k == 1: affine(o, o, -1.0, 3.0, [], ["e1_1_0"])
             at("g%d" % k)
-            sign(d[:, 3 * PL + a::3], T.sa[:, BP:BP + 120], vv(k), ["s2p", "v%d" % k], ["e2_%d" % k])
+            sign(d[:, 3 * PL + a::3], T.sb[:, BP:BP + 120], vv(k), ["s2p", "v%d" % k, "v%d_" % k], ["e2_%d" % k])
         at("g0")
         affine(T.d1[:, 3 * PL + 1::3], T.d1[:, 3 * PL + 1::3], -1.0, 3.0, [], ["e2_1"])
         at("w7")
         ts(T.cl[:, 1:2], T.m1[:, 7 * W1 + PA + K:7 * W1 + PA + K + 1], T.m1[:, 5 * W1 + PA + K:5 * W1 + PA + K + 1], ALU.is_lt, 2.0, ALU.mult, ["p7"], ["cl1"])
         at("u7")
-        ts(T.cl[:, 3:4], vv(7), vv(5), ALU.is_lt, 2.0, ALU.mult, ["v5", "v7"], ["cl3"])
+        ts(T.cl[:, 5:6], vv(7), vv(5), ALU.is_lt, 2.0, ALU.mult, ["v5", "v7", "v5_", "v7_"], ["cl3"])
         for b in four:
             at("dp")
-            mm(4 + b, T.ec, T.es, 128 * b, wc, ws, LAND, K, ["ec%d" % b, "wl"])
+            mm(4 + b, T.ec, T.es, 128 * b, wc, ws, C, K, ["ec%d" % b, "wl"])
             at("vq")
             copy("S", T.vp[:, PV * b + SH + C:PV * b + PV], ps(4 + b, 0, K), ["ps%d" % (4 + b)], ["vp%d_2" % b])
         for c, m in ((0, 360), (1, 360), (2, 720), (4, 360)):
@@ -317,35 +322,36 @@ def rank_program(g, core, T, topo):
             for c in range(2):
                 at("ab"[c] + str(k))
                 level(T.n1, WA, k, 240 * c, 240, T.k1[:, 720 * c + 2:720 * c + 720:3], T.neg[:], KB, DOWN,
-                      ["ck", "k%d" % (2 * c), "k%d" % (c + 1)] + below("n%d_" + str(c), k) + (["n%d_0" % k] if c else []), "n%d_%d" % (k, c))
+                      ["ck", "c5", "k%d" % (2 * c), "k%d" % (c + 1)] + below("n%d_" + str(c), k) + (["n%d_0" % k] if c else []), "n%d_%d" % (k, c))
             at("n%d" % k)
-            level(T.n2, WK, k, 0, 120, T.k1[:, 3 * PL + 2::3], T.neg[:, 0:120], KB, DOWN, ["ck", "k4"] + below("q%d", k), "q%d" % k)
-        for s in four:
+            level(T.n2, WK, k, 0, 120, T.k1[:, 3 * PL + 2::3], T.neg[:, 0:120], KB, DOWN, ["ck", "c6", "k4"] + below("q%d", k), "q%d" % k)
+        for s, m in enumerate(JOIN):
             at("j%d" % s)
-            m = 2 * s + 2
-            for q in four: copy("S", T.b2[0:32, 32 * s + 8 * q:32 * s + 8 * q + m], T.n2[quarter(q), 120:m * WK:WK], ["ck", "q%d" % (m - 1)], ["b2_%d_%d" % (s, q)])
+            for q in four: copy("S", T.b2[0:32, 32 * s + 8 * q:32 * s + 8 * q + m], T.n2[quarter(q), 120:m * WK:WK], ["c8", "q%d" % (m - 1)], ["b2_%d_%d" % (s, q)])
         for k in eight:
-            s = k // 2
+            s = min(i for i, m in enumerate(JOIN) if m > k)
             at("d%d" % k)
-            level(T.bb, WD, k, 0, 32, T.b2[0:32, 32 * s:32 * s + 32], T.neg[0:32, 0:32], KB, DOWN, ["ck"] + ["b2_%d_%d" % (s, q) for q in four] + below("d%d", k), "d%d" % k, 32)
+            level(T.bb, WD, k, 0, 32, T.b2[0:32, 32 * s:32 * s + 32], T.neg[0:32, 0:32], KB, DOWN, ["ck", "c7"] + ["b2_%d_%d" % (s, q) for q in four] + below("d%d", k), "d%d" % k, 32)
         for q in range(3):
             at("T%d" % q)
             for i in four:
                 copy("GGS"[q], T.in1[quarter(q), i::32], T.n1[quarter(i), 2 * q * WA + PL:(2 * q + 2) * WA:WA], ["n%d_1" % (2 * q + 1)], ["in%d_%d" % (q, i)], 2, True)
             at("U%d" % q)
-            copy("S", T.in1[quarter(q), 4::32], T.bb[0:32, 2 * q * WD + 32:(2 * q + 2) * WD:WD], ["d%d" % (2 * q + 1)], ["in%d_4" % q])
+            if q < 2: copy("S", T.in1[quarter(q), 4::32], T.bb[0:32, 2 * q * WD + 32:(2 * q + 2) * WD:WD], ["d%d" % (2 * q + 1)], ["in%d_4" % q])
         at("fl")
-        ts(T.cw[0:96, :], T.in1[0:96, 0:40], -1.5, ALU.add, r=IN[:15], w=["cw"])
+        ts(T.cw[0:96, :], T.in1[0:96, 0:40], -1.5, ALU.add, r=IN[:14], w=["cw"])
         at("fr")
         tt(T.in1[0:96, 0:40], T.in1[0:96, 0:40], T.cw[0:96, :], ALU.subtract, ["cw"], IN[:15])
         at("w6")
         ts(T.cl[:, 0:1], T.n1[:, 6 * WA + PL:6 * WA + PL + 1], -1.5, ALU.add, r=["n6_1"], w=["cl0"])
         at("u6")
-        ts(T.cl[0:32, 2:3], T.bb[0:32, 6 * WD + 32:6 * WD + 33], -1.5, ALU.add, r=["d6"], w=["cl2"])
+        ts(T.cl[0:32, 2:5], T.bb[0:32, 4 * WD + 32:7 * WD:WD], -1.5, ALU.add, r=["d6"], w=["cl2"])
+        at("U2")
+        tt(T.in1[64:96, 4::32], T.bb[0:32, 4 * WD + 32:6 * WD:WD], T.cl[0:32, 2:4], ALU.subtract, ["cl2"], ["in2_4"])
         at("T3")
         for i in four: tt(T.in1[96:128, i::32], T.n1[quarter(i), 6 * WA + PL::WA], T.cl[quarter(i), 0:2], ALU.subtract, ["n7_1", "cl0", "cl1"], ["in3_%d" % i])
         at("U3")
-        tt(T.in1[96:128, 4::32], T.bb[0:32, 6 * WD + 32::WD], T.cl[0:32, 2:4], ALU.subtract, ["d7", "cl2", "cl3"], ["in3_4"])
+        tt(T.in1[96:128, 4::32], T.bb[0:32, 6 * WD + 32::WD], T.cl[0:32, 4:6], ALU.subtract, ["d7", "cl2", "cl3"], ["in3_4"])
 
     odd_columns(0)
     order = {e: [] for e in Q}
@@ -356,40 +362,45 @@ def rank_program(g, core, T, topo):
         gs, gl = T["gs%d" % t], T["gl%d" % t]
         final = t == R - 1
         now[0] = t
-        for e in Q:
-            order[e] += [(w.strip("+*"), t + w.count("+")) for w in (ORDER[e] + " " + (NEAR if topo.chip(core) == topo.chip(partner) else FAR)[e]).split()
-                         if t or "*" not in w]
+        steps = NEAR if topo.chip(core) == topo.chip(partner) else FAR
+        HT, ZT = (["V" if w + str(b) in steps["V"].split() else "S" for b in four] for w in ("ht", "zt"))
+        for e in Q: order[e] += [(w.strip("+"), t + w.count("+")) for w in steps[e].split()]
         at("we")
-        quant(wc, ws, 0, K, T.xt[:, 0:4 * K], XE, ["we"])
-        exchange(giver, partner, "at%d" % t, [(wc[:, LAND:].bitcast(dt.uint8), wc[:, 0:K].bitcast(dt.uint8)), (ws[:, LAND:], ws[:, 0:K])], ["we"], ["wl"])
-        for name, bank, a in (("meo", 1, K), ("mer", 0, 288), ("meo2", 2, K)):
+        quant(wc, ws, 0, K, T.xt[:, 0:4 * K], XEN, ["we"])
+        exchange(giver, partner, "at%d" % t, [(wc[:, C:].bitcast(dt.uint8), wc[:, 0:K].bitcast(dt.uint8)), (ws[:, C:], ws[:, 0:K])], ["we"], ["wl"])
+        for name, bank in (("meo", 1), ("meo2", 2)):
             at(name)
-            mm(bank, wc, ws, a, wc, ws, 0, K, ["wo", "we"])
-        at("r0")
+            mm(bank, wc, ws, K, wc, ws, 0, K, ["wo", "we"])
+        at("mer")
+        mm(0, T.rc, T.rs, LOWER, wc, ws, 0, K, ["wr", "we"])
+        at("re")
         copy("S", T.cv[0:64, 0:K], ps(0, 0, K, 0, 64), ["ps0"], ["cv0"])
         at("s11")
         copy("S", T.s1[:, K:C], ps(2, 0, K), ["ps2"], ["s1_1"])
         at("lo")
-        tt(T.sa[:, LO:LO + K], ps(1, 0, K), T.s1[:, 0:K], ALU.min, ["ps1", "s1_0"], ["lo"])
+        tt(T.sa[:, 0:K], ps(1, 0, K), T.s1[:, 0:K], ALU.min, ["ps1", "s1_0"], ["lo"])
         at("hi")
-        tt(T.sa[:, LO + K:LO + C], ps(1, 0, K), T.s1[:, 0:K], ALU.max, ["ps1", "s1_0"], ["hi"])
+        tt(T.sa[:, K:C], ps(1, 0, K), T.s1[:, 0:K], ALU.max, ["ps1", "s1_0"], ["hi"])
         for b in four:
             at("dt")
             mm(4 + b, T.ec, T.es, 128 * b, wc, ws, 0, C, ["ec%d" % b, "we", "wo"])
-            at("vp")
             for e in range(2):
+                at("vp%d" % e)
                 copy("S", T.vp[:, PV * b + SH + e:PV * b + SH + C:2], ps(4 + b, K * e, K * e + K), ["ps%d" % (4 + b)], ["vp%d_%d" % (b, e)])
         at("sw")
-        for h in range(2): whole(T.sw[:, SW * h + SH:SW * h + PV], PL, 0, ["sw%d" % h])
+        for h in range(2): iota(T.sw[:, SW * h + SH:SW * h + PV], [[0, PL // 2], [OWN, 2]], -OWN, 0, ["sw%d" % h])
         best_places(t)
         lw = T.lwu[:, 0:10]
         at("out1")
-        op("V", lambda: V.transpose(T.out1[:], T.in1[:]), IN, ["out1"])
+        turn(T.out1[:], T.in1[:], IN, ["out1"])
         at("o32")
-        for e in range(2): op("V", lambda e=e: V.transpose(T.o32[:, e::2], T.out1[:, e::2]), ["out1"], ["o32_%d" % e])
-        for name in ("lwu", "lwi"):
-            at(name)
-            ts(T[name][:], T.o32[:, 0:16], 512.0, ALU.mult, -512.0, ALU.add, ["o32_0", "o32_1"], [name])
+        for e in range(2): turn(T.o32[:, e::2], T.out1[:, e::2], ["out1"], ["o32_%d" % e])
+        at("lwu")
+        ts(T.lwu[:], T.o32[:, 0:16], 512.0, ALU.mult, -512.0, ALU.add, ["o32_0", "o32_1"], ["lwu"])
+        at("lwf")
+        affine(T.eq[:, 32::33], T.o32[:, 0:10], -64.0, 64.0, ["o32_0", "o32_1"], ["lwf"])
+        at("nb")
+        affine(T.nb[:], T.o32[:, 0:16], -2.0 ** 16, 0.0, ["o32_0", "o32_1"], ["nb"])
         if final:
             at("vc")
             quant(T.vc, T.vs, 0, 128, T.vin[:], ["vin"], ["vc"])
@@ -397,16 +408,16 @@ def rank_program(g, core, T, topo):
             affine(T.opf[:], T.out1[:], 512.0, -512.0 - SH, ["out1"], ["opf"])
             at("op")
             dma("Y", "dop", [(T.op[2 * q + h, :], T.opf[32 * q:32 * q + 5, 32 * h:32 * h + 32]) for q in four for h in range(2)], ["opf"])
-        at("zt")
         for b in four:
-            copy("VVSS"[b], T.zt[:, b::4], T.vp[:, PV * b:PV * b + PV].indirect(lw), ["lwu", "vz%d" % b] + ["vp%d_%d" % (b, i) for i in range(3)], ["zt%d" % b])
+            at("zt%d" % b)
+            copy(ZT[b], T.zt[:, b::4], T.vp[:, PV * b:PV * b + PV].indirect(lw), ["lwu", "vz%d" % b] + ["vp%d_%d" % (b, i) for i in range(3)], ["zt%d" % b])
         at("zc")
         quant(T.zc, T.zs, 0, K, T.zt[:], ["zt%d" % b for b in four], ["zc"])
         for b in (0, 2, 1, 3):
             at("mh")
             mm(4 + b, T.lc, T.ls, 128 * b, T.zc, T.zs, 0, K, ["lc", "ls", "zc"])
             at("ht%d" % b)
-            if b < 2: ts(T.ht[:, b::4], ps(4 + b, 0, K), 0.03125, ALU.mult, r=["ps%d" % (4 + b)], w=["ht%d" % b])
+            if HT[b] == "V": ts(T.ht[:, b::4], ps(4 + b, 0, K), 0.03125, ALU.mult, r=["ps%d" % (4 + b)], w=["ht%d" % b])
             else: act(T.ht[:, b::4], ps(4 + b, 0, K), ACT.Copy, 0.03125, 0.0, ["ps%d" % (4 + b)], ["ht%d" % b])
         at("ho")
         quant(hc, hs, 0, K, T.ht[:], ["ht%d" % b for b in four], ["ho"])
@@ -416,35 +427,33 @@ def rank_program(g, core, T, topo):
             mm(4 + b, T.ec, T.es, 128 * b, hc, hs, 0, K, ["ec%d" % b, "ho"])
             at("eo")
             copy("S", T.est[:, EW * b:EW * b + K], ps(4 + b, 0, K), ["ps%d" % (4 + b)], ["eo%d" % b])
-        at("x1")
-        copy("S", T.x1[:], T.idt[:].indirect(lw), ["lwu", "idt"], ["x1"])
-        for e in range(2):
-            at("eq%d" % e)
-            tt(T.eq[:, K * e:K * e + K], T.lwi[:].indirect(T.selx[:, 10 * e:10 * e + 10]), T.x1[:], ALU.is_equal, ["lwi", "selx", "x1"], ["eq%d" % e])
+        at("y0")
+        copy("S", T.x0[:], T.in1[:].indirect(T.selr[:]), IN + ["selr"], ["x0_"])
+        at("y1")
+        turn(T.x1[:], T.x0[:], ["x0_"], ["x1_"])
+        for c in range(10):
+            at("eq%d" % (c // 5))
+            act(T.eq[:, 33 * c:33 * c + 32], T.x1[:, 32 * (c // 2):32 * (c // 2) + 32], ACT.Abs, 2.0 ** 16, T.nb[:, c:c + 1], ["nb", "x1_"], ["eq%d" % c])
         at("kp")
-        scan(T.kp[:], T.cm[:], T.eq[:], 0.0, ALU.mult, ALU.max, ["eq0", "eq1"] + ["cm%d" % i for i in range(10)], ["kp"])
-        at("sf")
-        tt(T.sf[:], T.kp[:].indirect(T.selk[:, 0:1]), T.lwi[:], ALU.max, ["kp", "selk", "lwi"], ["sf"])
+        scan(T.kp[:], T.cm[:, 0:330], T.eq[:], 0.0, ALU.add, ALU.min, ["eq%d" % c for c in range(10)] + ["cm", "lwf"], ["kp"])
         at("so")
-        copy("V", T.so[:], T.sf[:], ["sf"], ["so"])
+        ts(T.so[:, 0:10], T.kp[:, 32::33], -8.0, ALU.mult, r=["kp"], w=["so"])
         for q in (4, 3, 2, 1, 0):
             at("sc%d" % q)
             copy("V", T.sw[:, SW * (q % 2):SW * (q % 2) + SW].indirect(T.so[:, 2 * q:2 * q + 2]), T.sval[:, 32 * q:32 * q + 32], ["so", "sval"], ["sw%d" % (q % 2)])
         nn = lambda i: gs[:, 0:10] if i == 2 else T.nn[:, 10 * i:10 * i + 10]
         for i, (a, b, c) in ((2, (C, PL, 1)), (1, (1, C, 2)), (0, (0, C, 2))):
             for h in range(2):
-                at("n%d%d" % (i, h))
+                at("i%d%d" % (i, h))
                 o = SW * h + SH
-                scan(T.ns[:, PL * h + K * i:PL * h + K * i + K], T.c16[:], T.sw[:, o + a:o + b:c], 0.0, ALU.mult, ALU.max, ["sw%d" % h, "c16a", "c16b"], ["ns%d_%d" % (i, h)])
+                scan(T.ns[:, PL * h + K * i:PL * h + K * i + K], T.cm[:, 336:496], T.sw[:, o + a:o + b:c], 0.0, ALU.add, ALU.max, ["sw%d" % h, "cn"], ["ns%d_%d" % (i, h)])
             at("gs" if i == 2 else "nn%d" % i)
             tt(nn(i), T.ns[:, K * i + 15:K * i + K:16], T.ns[:, PL + K * i + 15:PL + K * i + K:16], ALU.max, ["ns%d_0" % i, "ns%d_1" % i], ["gs" if i == 2 else "ns%d" % i])
         exchange(partner, giver, "ag%d" % t, [(gl[:, 0:10], gs[:, 0:10])], ["gs"], ["gl"])
         at("offo")
-        ts(T.offo[:, 0:10], nn(1), pf(13), ALU.mult, K + 0.4, ALU.add, ["ns1", "pf13"], ["offo"])
-        at("ff")
-        ts(T.ff[:, 0:10], nn(0), pf(14), ALU.is_ge, pf(15), ALU.mult, ["ns0", "pf14", "pf15"], ["ff"])
+        ts(T.offo[:, 0:10], nn(1), -1.0, ALU.mult, pf(13), ALU.add, ["ns1", "pf13"], ["offo"])
         at("oo")
-        tt(T.oo[:, 0:10], T.ff[:, 0:10], nn(0), ALU.add, ["ff", "ns0"], ["oo"])
+        affine(T.oo[:, 0:10], nn(0), 1.0, float(OWN), ["ns0"], ["oo"])
 
         def renew(e, how, width, off, buf, r):
             for b in four:
@@ -455,24 +464,26 @@ def rank_program(g, core, T, topo):
                     at("x" + "eo"[e] + str(b))
                     tt(o, a, T.vp[:, PV * b + SH + e:PV * b + SH + C:2], ALU.add, rb + ["vp%d_%d" % (b, e)], w)
                 else:
-                    bank = b if e else (b + 2) % 4
-                    at("d" + "eo"[e])
-                    mm(bank, T.ec, T.es, 128 * b, wc, ws, K * e, K, ["ec%d" % b, "we", "wo"])
-                    at("a" + "eo"[e])
+                    a0 = K * e if XE[b] == "S" else 0
+                    at("a" + "eo"[e] + str(b))
                     copy("S", buf[:, K * b:K * b + K], a, rb, ["a%d%d" % (e, b)])
                     at("x" + "eo"[e] + str(b))
-                    tt(o, ps(bank, 0, K), buf[:, K * b:K * b + K], ALU.add, ["ps%d" % bank, "a%d%d" % (e, b)], w)
-        renew(1, "VVSS", K + 1, T.offo, T.ao, ["offo", "eo%d", "ez%d"])
+                    tt(o, ps(b, a0, a0 + K), buf[:, K * b:K * b + K], ALU.add, ["ps%d" % b, "a%d%d" % (e, b)], w)
+        at("do")
+        for b in four:
+            if XE[b] == "S": mm(b, T.ec, T.es, 128 * b, wc, ws, 0, C, ["ec%d" % b, "we", "wo"])
+            elif XO[b] == "S": mm(b, T.ec, T.es, 128 * b, wc, ws, K, K, ["ec%d" % b, "wo"])
+        renew(1, XO, K + 1, T.offo, T.ao, ["offo", "eo%d", "ez%d"])
         for b in four:
             at("mg")
             mm(4 + b, T.ec, T.es, 128 * b, hc, hs, K, K, ["ec%d" % b, "hl"])
-            at("eg")
+            at("eg%d" % b)
             copy("S", T.est[:, EW * b + OWN:EW * b + OWN + K], ps(4 + b, 0, K), ["ps%d" % (4 + b)], ["eg%d" % b])
         at("em")
         tt(T.em[:, 0:10], T.oo[:, 0:10], gl[:, 0:10], ALU.max, ["oo", "gl"], ["em"])
         at("offe")
-        ts(T.offe[:, 0:10], T.em[:, 0:10], pf(13), ALU.mult, OWN + K + 0.4, ALU.add, ["em", "pf13"], ["offe"])
-        renew(0, "VVVS", OWN + 1 + K, T.offe, T.ae, ["offe", "eo%d", "eg%d", "ez", "ez%d"])
+        ts(T.offe[:, 0:10], T.em[:, 0:10], -1.0, ALU.mult, pf(14), ALU.add, ["em", "pf14"], ["offe"])
+        renew(0, XE, OWN + 1 + K, T.offe, T.ae, ["offe", "eo%d", "eg%d", "ez", "ez%d"])
         if not final: odd_columns(t + 1)
 
     for h in range(2):
@@ -484,9 +495,10 @@ def rank_program(g, core, T, topo):
         copy("SV"[h], T.ysb[:, K * h:K * h + K], ps(h, 0, K), ["ps%d" % h], ["ysb%d" % h])
     at("oc")
     dma("Y", "doc", [(T.oc[:], T.fc[:].bitcast(dt.uint8))], ["fc0", "fc1"])
-    dma("Y", "dos", [(T.osc[4 * q:4 * q + 4, :], T.fs[32 * q:32 * q + 4, :]) for q in four], ["fc0", "fc1"])
     at("y")
     dma("S", "dy", [(T.y[:], T.ysb[:])], ["ysb0", "ysb1"])
+    at("os")
+    dma("Y", "dos", [(T.osc[4 * q:4 * q + 4, :], T.fs[32 * q:32 * q + 4, :]) for q in four], ["fc0", "fc1"])
 
     queue = {e: sorted((i for i, c in enumerate(calls) if c[0] == e), key=lambda i: (order[e].index(calls[i][1]), i), reverse=True) for e in Q}
     queue[None] = [i for i, c in enumerate(calls) if c[0] is None]

from concourse.mybir import dt, AluOpType, ActivationFunctionType

ALU = AluOpType
ACT = ActivationFunctionType
C, K, PL, R = 320, 160, 480, 3
BIG = 1e29
KB = 100.0
W1, W3, WA, WK, WD = 484, 244, 484, 124, 36
LOW, HI, PA = 1, 161, 321
EW = 352
OWN = 176
LIFT = 1024.0
SH = 16
PV, SW = PL + SH, 768
JOIN = (2, 4, 5, 6, 7, 8)
XO, XE = "VVSS", "VVSV"
X4, U8, BF, F32, F16, I32, U16 = "float8_e4m3fn_x4", "uint8", "bfloat16", "float32", "float16", "int32", "uint16"
SCRATCH = {"ps": ("psum", [128, 4096], F32)}
for _d, _l in {
    BF: dict(xin=1280, xt=4 * C, xf=1280, vin=512, et=516, vp=4 * PV, zt=640, ht=640, est=4 * EW,
             sval=K, ao=4 * K, ae=4 * K, rt=768, ci=330, sw=2 * SW, d0=1800),
    X4: dict(lc=512, rc=192, vc=128, ec=512, fc=C, zc=K, wc0=PL, wc1=PL, wc2=PL, hc0=C, hc1=C, hc2=C),
    U8: dict(ls=512, rs=192, vs=128, es=512, fs=C, zs=K, ws0=PL, ws1=PL, ws2=PL, hs0=C, hs1=C, hs2=C),
    F32: dict(ysb=C, s1=PL, sa=C, m1=8 * W1, cv=240, sb=128, md=9 * W3, big=256, mk1=K, mk2=K, ob=16, vv=64, in1=64, out1=64, o32=64,
              idt=512, nb=16, nn=20, oo=16, em=16, pf=24, sri=10, opf=64,
              gs0=16, gs1=16, gs2=16, gl0=16, gl1=16, gl2=16),
    F16: dict(eq=330, kp=330, cm=496, ns=2 * PL, x0=K, x1=K, neg=240, b2=32 * len(JOIN), bb=8 * WD, d1=1800, k1=1800, n1=8 * WA, n2=8 * WK),
    I32: dict(pi=8, cl=6, cw=40),
    U16: dict(lwu=16, so=16, offe=16, offo=16, selb=8, selr=10),
}.items():
    for _k, _n in _l.items(): SCRATCH[_k] = ("sbuf", [128, _n], _d)
DMAS = ["dx", "dc", "dl", "dls", "dv", "dop", "doc", "dos", "dy"]
SEMAPHORES = ["v0", "s0", "p0", "g0"] + DMAS + ["sent"] + ["%s%d" % (k, t) for k in ("at", "ah", "ag") for t in range(R)]
FAR = {
    "V": """ca cb cc cd xe xo we wo ce wr s1 cf lo hi own l0 x0 l1 h0 l2 h1 x1 l3 h2 x2 h3 x3 p0 h4 Q0 p1 h5 Q1 p2 x4 Q2 p3 x5 Q3 p4 h6 Q4 x6
         p5 Q5 v1 h7 p6 x7 Q6 p7 v3 Q7 v5 v7 w7 k0 k1 k4 a0 k2 n0 a1 b0 n1 a2 b1 n2 a3 b2 n3 d0 a4 b3 n4 d1 a5 b4 n5 d2 a6 b5 d3 n6 b6 d4 n7
         a7 d5 u7 fl w6 b7 d6 c5 fr u6 d7 T3 U2 U3 out1 o32 lwu y1 zt0 zt1 zc kp ht0 so ht1 sc4 ho sc3 sc2 sc1 sc0 i01 i21 i20 i10 i11 gs
         i00 nn1 nn0 offo vc xo1 xo0 xo2 em xo3 offe wo+ xe1 xe0 xe3 xe2 fc ysb""",
    "S": """ca xe xo xr cd c2 s11 re vp0 c0 vp1 s12 cv e1 s2p lift ob4 e3 g1 e5 g0 f0 f1 g3 g5 g7 f2 f3 j0 j1 j2 U0 j3 T2 U1 j4 j5 vq y0
         lwf nb zt3 zt2 eq1 eq0 ht2 ht3 eo ao2 oo ao3 eg0 eg1 eg2 opf eg3 ae2 ysb y""",
    "G": "ca at cb c1 c3 T0 T1 sw ah ag xr+",
    "P": "moo meo meo2 mor mer dt mp mpr mpr2 mp2 do dp mh mo mg moo+ my",
    "Y": "x w c4 op oc os"}
NEAR = {
    "V": """wr we s1 own lo hi l0 x0 l1 h0 x1 l2 h1 x2 l3 Q0 p0 h2 Q1 p1 h3 Q2 p2 x3 h4 p3 x4 Q3 h5 p4 Q4 x5 h6 p5 x6 h7 Q5 p6 x7 Q6 v1 p7 v3
         Q7 v5 w7 v7 k0 k1 k2 a0 k4 u7 a1 n0 b0 a2 n1 b1 a3 n2 b2 a4 n3 d0 b3 a5 n4 d1 b4 a6 n5 d2 b5 n6 d3 b6 n7 d4 a7 w6 d5 fl b7 d6 fr u6
         d7 T3 U2 U3 out1 o32 y1 lwu zt1 zt0 zt2 kp zc so sc4 sc3 sc2 ht0 sc1 sc0 ho i21 i10 i20 i11 gs nn1 i00 i01 offo nn0
         xo0 xo1 xo2 em xo3 offe wo+ xe1 xe0 xe3 xe2""",
    "S": """re s11 vp0 cv vp1 s12 s2p e1 ob4 lift e3 e5 g1 f0 f1 f2 f3 g3 g5 g7 g0 j0 j1 j2 U0 j3 T2 U1 j4 j5 vq y0 nb lwf eq0 eq1 zt3
         ht2 ht1 ht3 eo ao2 oo ao3 eg1 eg2 eg0 eg3 ae2""",
    "G": "at sw T0 T1 ah ag xr+",
    "P": "mor meo mer meo2 dt mpr mp mp2 mpr2 do dp mh mo mg moo+",
    "Y": ""}


def rank_program(g, core, T, topo):
    rank = T.rank_of(core)
    if rank is None:
        return
    n = len(T.cores)
    Q = {"V": g.vector, "S": g.scalar, "P": g.tensor, "G": g, "Y": g.sync}
    calls = []
    wr, rd = {}, {}
    narrow = set()
    now, step = [0], [None]

    def record(e, issue, r, w):
        r, w = ([x + str(now[0]) if x in ("we", "wo", "wl", "ho", "hl", "gs", "gl") else x for x in a] for a in (r, w))
        d = set()
        for t in r:
            if t in wr: d.add(wr[t])
            if t.startswith("ps"): d.update(j for (q, j) in rd.get(t, []) if q != e)
        for t in w:
            if t in wr: d.add(wr[t])
            d.update(j for (q, j) in rd.get(t, []))
        calls.append((e, (step[0], now[0]), issue, d))
        for t in r: rd.setdefault(t, []).append((e, len(calls) - 1))
        for t in w:
            wr[t] = len(calls) - 1
            rd[t] = []

    def at(name): step[0] = name

    def op(e, fn, r=(), w=()):
        s = e.lower() + "0"
        record(e, lambda: (fn().then_inc(T.sem[s], 1), s, 1), r, w)

    def dma(e, s, pairs, r=(), w=()):
        record(e, lambda: ([Q[e].dma_start(o, i).then_inc(T.sem[s], 16) for o, i in pairs], s, 16 * len(pairs)), r, w)

    def exchange(dst, src, s, pairs, r, w):
        rid, pid, _ = topo.addr(dst)
        at(s[:2])
        record("G", lambda: ([g.remote_dma(o, a, T.sem[s], T.sem.sent, pid, rid, topo.mask(core, dst)) for o, a in pairs],
                             "sent", len(pairs) * len(topo.engines(core, dst))), r, ())
        record(None, lambda: (None, s, len(pairs) * len(topo.engines(src, core))), (), w)
    V, S = g.vector, g.scalar

    def select(o, i, pat, cmp, c, base, cm, r, w, part=False):
        op("G", lambda: g.affine_select(o, i, pat, cmp, c, base, cm), r, w)
        if part: narrow.add(len(calls) - 1)

    def copy(e, o, i, r, w, m=0, part=False):
        if e == "V": op("V", lambda: V.tensor_copy(o, i), r, w)
        elif e == "G": select(o, i, [[0, m]], ALU.is_equal, 0.0, 0, 0, r, w, part)
        else: op("S", lambda: S.activation(o, i, ACT.Copy), r, w)

    def ts(o, i, a, o0, b=None, o1=None, r=(), w=()):
        if o1 is None: op("V", lambda: V.tensor_scalar(o, i, a, None, o0), r, w)
        else: op("V", lambda: V.tensor_scalar(o, i, a, b, o0, o1), r, w)

    def tt(o, a, b, o0, r, w): op("V", lambda: V.tensor_tensor(o, a, b, o0), r, w)
    def scan(o, a, b, init, o0, o1, r, w): op("V", lambda: V.tensor_tensor_scan(o, a, b, init, o0, o1), r, w)
    def turn(o, i, r, w): op("V", lambda: V.transpose(o, i), r, w)
    def fill(o, c, w, r=()): op("V", lambda: V.memset(o, c), r, w)
    def act(o, i, func, scale, bias, r, w): op("S", lambda: S.activation(o, i, func, bias=bias, scale=scale), r, w)
    def affine(o, i, scale, bias, r, w): act(o, i, ACT.Identity, scale, bias, r, w)
    def sign(o, i, v, r, w): act(o, i, ACT.Sign, -1.0, v, r, w)
    def quant(c, s, a, b, i, r, w): op("V", lambda: V.quantize_mx(c[:, a:b], s[:, a:b], i), r, w)

    def mms(bank, lc, ls, rc, rs, terms, m, r):
        record("P", lambda: ([g.tensor.matmul_mx(T.ps[:, 512 * bank:512 * bank + m], lc[:, a:a + 128], ls[:, a:a + 128], rc[:, b:b + m], rs[:, b:b + m],
                                                 i == 0, i == len(terms) - 1).then_inc(T.sem.p0, 1) for i, (a, b) in enumerate(terms)], "p0", len(terms)), r, ["ps%d" % bank])

    def mm(bank, lc, ls, a, rc, rs, b, m, r): mms(bank, lc, ls, rc, rs, [(a, b)], m, r)

    def ps(bank, a, b, p=0, q=128): return T.ps[p:q, 512 * bank + a:512 * bank + b]

    def iota(o, pat, base, cm, w, flag=True):
        if flag: op("G", lambda: g.iota(o, pat, base, cm, allow_small_or_imprecise_dtypes=True), (), w)
        else: op("G", lambda: g.iota(o, pat, base, cm), (), w)

    def whole(o, m, c, w): iota(o, [[0, m]], c, 0, w)

    def level(buf, width, k, a, m, data, first, lo, ops2, r, w, p=128):
        o = k * width
        prev = first if k == 0 else buf[0:p, o - width + a:o - width + a + m]
        init = lo if a == 0 else buf[0:p, o + a:o + a + 1]
        scan(buf[0:p, o + a + 1:o + a + 1 + m], data, prev, init, ops2[0], ops2[1], r, [w])

    def below(tok, k): return [tok % (k - 1)] if k else []
    UP, DOWN = (ALU.max, ALU.min), (ALU.min, ALU.max)
    wcs = [(T["wc%d" % t], T["ws%d" % t]) for t in range(R)]
    hcs = [(T["hc%d" % t], T["hs%d" % t]) for t in range(R)]
    four, eight = range(4), range(8)
    pf = lambda c: T.pf[:, c:c + 1]
    j, qq = pf(1), pf(2)
    ET = ["et0"]
    quarter = lambda q: slice(32 * q, 32 * q + 32)
    half = lambda h: slice(64 * h, 64 * h + 64)
    BP = 8
    LOWER, UPPER = 64, 0
    XEN, XON = ["xe%d" % b for b in four], ["xo%d" % b for b in four]
    F = ["f%d" % i for i in range(6)]
    IN = ["in%d_%d" % (q, i) for q in four for i in range(5)]
    M1, MD = ["c1", "c3", "big"], ["c4", "c9"]

    at("x")
    dma("Y", "dx", [(T.xin[:], T.x[:])], (), ["xin"])

    def const(o, m, c, w): affine(o, T.big[:, 0:m], 0.0, c, ["big"], w)
    at("ca")
    iota(T.pi[:, 0:1], [[0, 1]], 0, 1, ["pi0"], False)
    iota(T.idt[:, 0:128], [[1, 128]], 0, 0, ["id0"])
    fill(T.big[:], BIG, ["big"])
    fill(T.et[:], 0.0, ["et"])
    for c, w in enumerate([["xz0"], ["xr0", "xr1"], ["xz1"]]): const(T.rt[:, 256 * c:256 * c + 256], 256, 0.0, w)
    const(T.m1[:, 4 * W1 + HI::W1], 4, -BIG, ["c1"])
    const(T.m1[:, LOW::W1], 8, -BIG, ["c3"])
    const(T.md[:, W3::W3], 8, -BIG, ["c9"])
    const(T.md[:, 0:W3], W3, BIG, ["c4"])
    select(T.mk1[:], T.big[:, 0:K], [[-1, K]], ALU.not_equal, -BIG, 0, 1, ["big"], ["mk1"])
    iota(T.idt[:, 128:], [[1, 384]], 128, 0, ["idt"])
    at("cb")
    for q in (2, 3): select(T.mk2[quarter(q), :], T.big[quarter(q), 0:K], [[-1, K]], ALU.not_equal, -BIG, 128, 1, ["big"], ["mk%d" % q], True)
    for c, (sh, m) in enumerate([(0, 15), (5, 3), (5, 1), (6, 1)]):
        ts(T.pi[:, c + 1:c + 2], T.pi[:, 0:1], sh, ALU.logical_shift_right, m, ALU.bitwise_and, ["pi0"], ["pi%d" % (c + 1)])
    at("cc")
    copy("V", T.pf[:, 0:5], T.pi[:, 0:5], ["pi%d" % c for c in range(5)], ["pf"])
    at("cd")
    ts(T.et[:, 3:515:4], T.idt[:, 0:128], pf(0), ALU.is_equal, r=["id0", "pf", "et"], w=ET)
    ts(pf(19), j, 15.0, ALU.is_equal, r=["pf"], w=["pf19"])
    quant(T.rc, T.rs, 0, 128, T.rt[:, 0:512], ["xz0", "xr0", "xr1"], ["wr"])
    affine(pf(15), pf(4), 1.0 / 512, 1 + SH / 512, ["pf"], ["pf15"])
    affine(pf(17), qq, 40.0 / 512, 1 + (C + SH) / 512, ["pf"], ["pf17"])
    affine(pf(18), pf(3), 40.0, j, ["pf"], ["pf18"])
    affine(pf(20), pf(3), 80.0, j, ["pf"], ["pf20"])
    affine(pf(16), pf(3), K / 512, pf(15), ["pf15"], ["pf16"])
    at("ce")
    for b in four: quant(T.ec, T.es, 128 * b, 128 * b + 128, T.et[:, 3 - b:515 - b], ET, ["ec%d" % b])
    at("cf")
    ts(T.selb[:, 0:3], T.idt[:, 0:48:16], pf(18), ALU.add, K - 8.0, ALU.add, ["id0", "pf18"], ["selb"])
    ts(T.selb[:, 3:8], T.idt[:, 0:80:16], pf(20), ALU.add, r=["id0", "pf20"], w=["selc"])
    at("c0")
    for c, a in enumerate([T.idt[:, 1:C:2], T.idt[:, 0:C:2], T.idt[:, C:PL]]):
        affine(T.d1[:, PL * c + 2:PL * c + PL:3], a, 1.0 / 512, 1 + SH / 512, ["id0", "idt"], ["f%d" % c])
    affine(T.d1[:, 3 * PL + 2:3 * PL + 120:3], T.idt[:, 0:40], 1.0 / 512, pf(17), ["id0", "pf17"], ["f3"])
    affine(T.d1[:, 3 * PL + 122::3], T.idt[:, 0:K:2], 1.0 / 512, pf(16), ["id0", "idt", "pf16"], ["f4"])
    at("xe")
    for b in four: copy("VVVS"[b], T.xt[:, b:4 * K:4], T.xin[:, b::8], ["xin"], ["xe%d" % b])
    at("xo")
    for b in four: copy("SSVV"[b], T.xt[:, 4 * K + b:4 * C:4], T.xin[:, 4 + b::8], ["xin"], ["xo%d" % b])
    at("c1")
    whole(T.d0[:, 0::3], 600, 0, ["f5"])
    iota(T.sri[:], [[1, 5], [32, 2]], 0, 0, ["sri"])
    iota(T.sval[:], [[-1, K]], K, 0, ["sval"])
    for b in four:
        whole(T.vp[:, PV * b:PV * b + SH], SH, 0, ["vz%d" % b])
        whole(T.est[:, b * EW + K:b * EW + OWN], OWN - K, 0, ["ez%d" % b])
    whole(T.est[:, OWN + K::EW], 4, 0, ["ez"])
    at("c2")
    for c, (o, m) in enumerate([(T.n1[:, 0::WA], 8), (T.n2[:, 0::WK], 8), (T.bb[:, 0::WD], 8), (T.b2[:], 32 * len(JOIN))]): const(o, m, KB, ["c%d" % (5 + c)])
    const(T.ob[:, 8:9], 1, BIG, ["ob"])
    const(T.neg[:], 240, -KB, ["ck"])
    const(T.in1[:], 64, 0.0, IN)
    affine(pf(13), pf(19), -LIFT, LIFT + K, ["pf19"], ["pf13"])
    affine(pf(14), pf(19), -LIFT, LIFT + K + OWN, ["pf19"], ["pf14"])
    at("c3")
    low = lambda a, b: T.cm[0:32, a:b]
    iota(T.ci[:], [[0, 10], [-1, 33]], -64, 0, ["ci"])
    select(low(0, 330), T.ci[0:32, :], [[0, 5], [-1, 2], [1, 33]], ALU.is_equal, 0.0, 0, -2, ["ci"], ["cm"], True)
    select(low(0, 330), low(0, 330), [[0, 10], [1, 33]], ALU.not_equal, 60000.0, 0, 0, [], ["cm"], True)
    select(low(336, 496), T.rt[0:32, 0:K], [[0, 10], [1, 16]], ALU.not_equal, -4 * LIFT, 0, -1, ["xz0"], ["cn"], True)
    select(low(336, 496), low(336, 496), [[0, 10], [1, 16]], ALU.not_equal, LIFT, -1, -1, [], ["cn"], True)
    at("c4")
    dma("Y", "dc", [(T.cm[16 * q:16 * q + 16, a:b], T.cm[0:16, a:b]) for q in range(1, 8) for a, b in ((0, 330), (336, 496))], [], ["cm", "cn"])
    at("c5")
    copy("V", T.selr[:], T.sri[:], ["sri"], ["selr"])

    def odd_columns(t):
        wc, ws = wcs[t]
        now[0] = t
        at("wo")
        quant(wc, ws, K, C, T.xt[:, 4 * K:4 * C], XON, ["wo"])
        at("moo")
        mm(0, wc, ws, K, wc, ws, K, K, ["wo"])
        at("s1")
        tt(T.s1[:, 0:K], ps(0, 0, K), T.mk1[:], ALU.min, ["ps0", "mk1"], ["s1_0"])
        at("xr")
        for i in range(2): copy("G" if t else "S", T.rt[:, 256 + 128 * i:384 + 128 * i], T.xt[:, 4 * 288:4 * C], XON, ["xr%d" % i], 128)
        at("wr")
        quant(T.rc, T.rs, 64, 192, T.rt[:, 256:768], ["xr0", "xr1", "xz1"], ["wr"])
        at("mor")
        mm(3, T.rc, T.rs, UPPER, wc, ws, K, K, ["wr", "wo"])
        at("own")
        tt(T.cv[64:128, 0:K], ps(3, 0, K, 64), T.mk2[64:128, :], ALU.min, ["ps3", "mk2", "mk3"], ["cv1"])
        now[0] = max(t - 1, 0)

    def best_places(t):
        wc, ws = wcs[t]
        big = T.big[:, 0:K]
        S1 = ["s1_0", "s1_1", "s1_2"]
        for k in four:
            at("l%d" % k)
            level(T.m1, W1, k, LOW, K, T.sa[:, 0:K], big, None, UP, M1 + ["lo"] + below("l%d", k), "l%d" % k)
        for k in eight:
            at("h%d" % k)
            level(T.m1, W1, k, HI, K, T.sa[:, K:C], big, None, UP, M1 + ["hi", "l%d" % min(k, 3)] + below("h%d", k), "h%d" % k)
        for k in eight:
            at("x%d" % k)
            level(T.md, W3, k + 1, 0, K, T.cv[:, 0:K], None, T.md[:, (k + 1) * W3:(k + 1) * W3 + 1], UP, MD + ["cv0", "cv1"] + below("x%d", k), "x%d" % k)
        for name, bank in (("mp", 2), ("mpr", 0), ("mp2", 3), ("mpr2", 1)):
            at(name)
            if bank > 1: mm(bank, wc, ws, K, wc, ws, C, K, ["wo", "wl"])
            else: mms(bank, T.rc, T.rs, wc, ws, [(LOWER, C - 48), (UPPER, C + 32)], 128, ["wr", "wo", "wl"])
        if t == 0:
            at("w")
            dma("Y", "dl", [(T.lc[:].bitcast(dt.uint8), T.wc[:])], ["wl"], ["lc"])
            dma("Y", "dls", [(T.ls[:], T.ws[:])], (), ["ls"])
            dma("Y", "dv", [(T.vin[:], T.v[:])], (), ["vin"])
        at("cv")
        copy("S", T.cv[:, K:240], ps(1, 48, 128), ["ps1"], ["cvp"])
        at("s12")
        copy("S", T.s1[:, C:PL], ps(3, 0, K), ["ps3"], ["s1_2"])
        at("s2p")
        copy("S", T.sb[:], T.cv[:].indirect(T.selb[:]), ["cv0", "cv1", "cvp", "selb", "selc"], ["s2p"])
        for k in eight:
            at("p%d" % k)
            level(T.m1, W1, k, PA, K, ps(2, 0, K), big, -BIG, UP, M1 + ["ps2", "h%d" % k] + below("p%d", k), "p%d" % k)
        for k in eight:
            at("Q%d" % k)
            level(T.md, W3, k + 1, K, 80, ps(0, 48, 128), None, None, UP, MD + ["ps0", "x%d" % k] + below("md%d", k), "md%d" % k)
        at("ob4")
        for h in range(2): copy("S", T.ob[half(h), 4:8], T.md[half(1 - h), 4 * W3 + 240:240:-W3], ["md3"], ["ob%d" % h])
        vv = lambda k: T.vv[:, 9 * k - 7:9 * k - 6]
        for k in (1, 3):
            at("v%d" % k)
            scan(T.vv[:, 8 * k - 8:9 * k - 6], T.md[:, 240:(k + 1) * W3 + 241:W3], T.ob[:, 7 - k:9], -BIG, ALU.max, ALU.min, MD + ["ob", "ob0", "ob1"], ["v%d" % k, "v%d_" % k])
        for k in (5, 7):
            at("v%d" % k)
            for h in range(2):
                scan(T.vv[half(h), 8 * k - 8:9 * k - 6], T.md[half(h), 240:(k + 1) * W3 + 241:W3], T.md[half(1 - h), (k + 1) * W3 + 240:239:-W3], -BIG, ALU.max, ALU.min,
                     MD + ["md%d" % k], ["v%d" % k + "_" * h])
        slot = {1: (T.d1, 1), 3: (T.d1, 0), 5: (T.d0, 2), 7: (T.d0, 1)}
        for k in (1, 3, 5, 7):
            d, a = slot[k]
            for c, m in ([(0, PL)] if k < 7 else [(c, 120) for c in four]):
                at("e%d" % k if k < 7 else "f%d" % c)
                o = d[:, 360 * c + a:360 * c + 3 * m:3]
                sign(o, T.s1[:, 120 * c:120 * c + m], T.m1[:, k * W1 + PA + K:k * W1 + PA + K + 1], S1 + ["p%d" % k], ["e1_%d_%d" % (k, c)])
            at("lift")
            if k == 1: affine(o, o, -1.0, 3.0, [], ["e1_1_0"])
            at("g%d" % k)
            sign(d[:, 3 * PL + a::3], T.sb[:, BP:BP + 120], vv(k), ["s2p", "v%d" % k, "v%d_" % k], ["e2_%d" % k])
        at("g0")
        affine(T.d1[:, 3 * PL + 1::3], T.d1[:, 3 * PL + 1::3], -1.0, 3.0, [], ["e2_1"])
        at("w7")
        ts(T.cl[:, 1:2], T.m1[:, 7 * W1 + PA + K:7 * W1 + PA + K + 1], T.m1[:, 5 * W1 + PA + K:5 * W1 + PA + K + 1], ALU.is_lt, 2.0, ALU.mult, ["p7"], ["cl1"])
        at("u7")
        ts(T.cl[:, 5:6], vv(7), vv(5), ALU.is_lt, 2.0, ALU.mult, ["v5", "v7", "v5_", "v7_"], ["cl3"])
        for b in four:
            at("dp")
            mm(4 + b, T.ec, T.es, 128 * b, wc, ws, C, K, ["ec%d" % b, "wl"])
            at("vq")
            copy("S", T.vp[:, PV * b + SH + C:PV * b + PV], ps(4 + b, 0, K), ["ps%d" % (4 + b)], ["vp%d_2" % b])
        for c, m in ((0, 360), (1, 360), (2, 720), (4, 360)):
            at("k%d" % c)
            run = slice(360 * c, 360 * c + m)
            scan(T.k1[:, run], T.d0[:, run], T.d1[:, run], 0.0, ALU.mult, ALU.add,
                 F + (["e1_1_0", "e1_3_0", "e1_5_0", "e1_7_%d" % c, "e1_7_%d" % (c + c // 2)] if c < 4 else ["e2_%d" % i for i in (1, 3, 5, 7)]), ["k%d" % c])
        for k in eight:
            for c in range(2):
                at("ab"[c] + str(k))
                level(T.n1, WA, k, 240 * c, 240, T.k1[:, 720 * c + 2:720 * c + 720:3], T.neg[:], KB, DOWN,
                      ["ck", "c5", "k%d" % (2 * c), "k%d" % (c + 1)] + below("n%d_" + str(c), k) + (["n%d_0" % k] if c else []), "n%d_%d" % (k, c))
            at("n%d" % k)
            level(T.n2, WK, k, 0, 120, T.k1[:, 3 * PL + 2::3], T.neg[:, 0:120], KB, DOWN, ["ck", "c6", "k4"] + below("q%d", k), "q%d" % k)
        for s, m in enumerate(JOIN):
            at("j%d" % s)
            for q in four: copy("S", T.b2[0:32, 32 * s + 8 * q:32 * s + 8 * q + m], T.n2[quarter(q), 120:m * WK:WK], ["c8", "q%d" % (m - 1)], ["b2_%d_%d" % (s, q)])
        for k in eight:
            s = min(i for i, m in enumerate(JOIN) if m > k)
            at("d%d" % k)
            level(T.bb, WD, k, 0, 32, T.b2[0:32, 32 * s:32 * s + 32], T.neg[0:32, 0:32], KB, DOWN, ["ck", "c7"] + ["b2_%d_%d" % (s, q) for q in four] + below("d%d", k), "d%d" % k, 32)
        for q in range(3):
            at("T%d" % q)
            for i in four:
                copy("GGS"[q], T.in1[quarter(q), i::32], T.n1[quarter(i), 2 * q * WA + PL:(2 * q + 2) * WA:WA], ["n%d_1" % (2 * q + 1)], ["in%d_%d" % (q, i)], 2, True)
            at("U%d" % q)
            if q < 2: copy("S", T.in1[quarter(q), 4::32], T.bb[0:32, 2 * q * WD + 32:(2 * q + 2) * WD:WD], ["d%d" % (2 * q + 1)], ["in%d_4" % q])
        at("fl")
        ts(T.cw[0:96, :], T.in1[0:96, 0:40], -1.5, ALU.add, r=IN[:14], w=["cw"])
        at("fr")
        tt(T.in1[0:96, 0:40], T.in1[0:96, 0:40], T.cw[0:96, :], ALU.subtract, ["cw"], IN[:15])
        at("w6")
        ts(T.cl[:, 0:1], T.n1[:, 6 * WA + PL:6 * WA + PL + 1], -1.5, ALU.add, r=["n6_1"], w=["cl0"])
        at("u6")
        ts(T.cl[0:32, 2:5], T.bb[0:32, 4 * WD + 32:7 * WD:WD], -1.5, ALU.add, r=["d6"], w=["cl2"])
        at("U2")
        tt(T.in1[64:96, 4::32], T.bb[0:32, 4 * WD + 32:6 * WD:WD], T.cl[0:32, 2:4], ALU.subtract, ["cl2"], ["in2_4"])
        at("T3")
        for i in four: tt(T.in1[96:128, i::32], T.n1[quarter(i), 6 * WA + PL::WA], T.cl[quarter(i), 0:2], ALU.subtract, ["n7_1", "cl0", "cl1"], ["in3_%d" % i])
        at("U3")
        tt(T.in1[96:128, 4::32], T.bb[0:32, 6 * WD + 32::WD], T.cl[0:32, 4:6], ALU.subtract, ["d7", "cl2", "cl3"], ["in3_4"])

    odd_columns(0)
    order = {e: [] for e in Q}
    for t in range(R):
        partner, giver = T.cores[(rank + 1 + t) % n], T.cores[(rank - 1 - t) % n]
        wc, ws = wcs[t]
        hc, hs = hcs[t]
        gs, gl = T["gs%d" % t], T["gl%d" % t]
        final = t == R - 1
        now[0] = t
        steps = NEAR if topo.chip(core) == topo.chip(partner) else FAR
        HT, ZT = (["V" if w + str(b) in steps["V"].split() else "S" for b in four] for w in ("ht", "zt"))
        for e in Q: order[e] += [(w.strip("+"), t + w.count("+")) for w in steps[e].split()]
        at("we")
        quant(wc, ws, 0, K, T.xt[:, 0:4 * K], XEN, ["we"])
        exchange(giver, partner, "at%d" % t, [(wc[:, C:].bitcast(dt.uint8), wc[:, 0:K].bitcast(dt.uint8)), (ws[:, C:], ws[:, 0:K])], ["we"], ["wl"])
        for name, bank in (("meo", 1), ("meo2", 2)):
            at(name)
            mm(bank, wc, ws, K, wc, ws, 0, K, ["wo", "we"])
        at("mer")
        mm(0, T.rc, T.rs, LOWER, wc, ws, 0, K, ["wr", "we"])
        at("re")
        copy("S", T.cv[0:64, 0:K], ps(0, 0, K, 0, 64), ["ps0"], ["cv0"])
        at("s11")
        copy("S", T.s1[:, K:C], ps(2, 0, K), ["ps2"], ["s1_1"])
        at("lo")
        tt(T.sa[:, 0:K], ps(1, 0, K), T.s1[:, 0:K], ALU.min, ["ps1", "s1_0"], ["lo"])
        at("hi")
        tt(T.sa[:, K:C], ps(1, 0, K), T.s1[:, 0:K], ALU.max, ["ps1", "s1_0"], ["hi"])
        for b in four:
            at("dt")
            mm(4 + b, T.ec, T.es, 128 * b, wc, ws, 0, C, ["ec%d" % b, "we", "wo"])
            for e in range(2):
                at("vp%d" % e)
                copy("S", T.vp[:, PV * b + SH + e:PV * b + SH + C:2], ps(4 + b, K * e, K * e + K), ["ps%d" % (4 + b)], ["vp%d_%d" % (b, e)])
        at("sw")
        for h in range(2): iota(T.sw[:, SW * h + SH:SW * h + PV], [[0, PL // 2], [OWN, 2]], -OWN, 0, ["sw%d" % h])
        best_places(t)
        lw = T.lwu[:, 0:10]
        at("out1")
        turn(T.out1[:], T.in1[:], IN, ["out1"])
        at("o32")
        for e in range(2): turn(T.o32[:, e::2], T.out1[:, e::2], ["out1"], ["o32_%d" % e])
        at("lwu")
        ts(T.lwu[:], T.o32[:, 0:16], 512.0, ALU.mult, -512.0, ALU.add, ["o32_0", "o32_1"], ["lwu"])
        at("lwf")
        affine(T.eq[:, 32::33], T.o32[:, 0:10], -64.0, 64.0, ["o32_0", "o32_1"], ["lwf"])
        at("nb")
        affine(T.nb[:], T.o32[:, 0:16], -2.0 ** 16, 0.0, ["o32_0", "o32_1"], ["nb"])
        if final:
            at("vc")
            quant(T.vc, T.vs, 0, 128, T.vin[:], ["vin"], ["vc"])
            at("opf")
            affine(T.opf[:], T.out1[:], 512.0, -512.0 - SH, ["out1"], ["opf"])
            at("op")
            dma("Y", "dop", [(T.op[2 * q + h, :], T.opf[32 * q:32 * q + 5, 32 * h:32 * h + 32]) for q in four for h in range(2)], ["opf"])
        for b in four:
            at("zt%d" % b)
            copy(ZT[b], T.zt[:, b::4], T.vp[:, PV * b:PV * b + PV].indirect(lw), ["lwu", "vz%d" % b] + ["vp%d_%d" % (b, i) for i in range(3)], ["zt%d" % b])
        at("zc")
        quant(T.zc, T.zs, 0, K, T.zt[:], ["zt%d" % b for b in four], ["zc"])
        for b in (0, 2, 1, 3):
            at("mh")
            mm(4 + b, T.lc, T.ls, 128 * b, T.zc, T.zs, 0, K, ["lc", "ls", "zc"])
            at("ht%d" % b)
            if HT[b] == "V": ts(T.ht[:, b::4], ps(4 + b, 0, K), 0.03125, ALU.mult, r=["ps%d" % (4 + b)], w=["ht%d" % b])
            else: act(T.ht[:, b::4], ps(4 + b, 0, K), ACT.Copy, 0.03125, 0.0, ["ps%d" % (4 + b)], ["ht%d" % b])
        at("ho")
        quant(hc, hs, 0, K, T.ht[:], ["ht%d" % b for b in four], ["ho"])
        exchange(partner, giver, "ah%d" % t, [(hc[:, K:C].bitcast(dt.uint8), hc[:, 0:K].bitcast(dt.uint8)), (hs[:, K:C], hs[:, 0:K])], ["ho"], ["hl"])
        for b in four:
            at("mo")
            mm(4 + b, T.ec, T.es, 128 * b, hc, hs, 0, K, ["ec%d" % b, "ho"])
            at("eo")
            copy("S", T.est[:, EW * b:EW * b + K], ps(4 + b, 0, K), ["ps%d" % (4 + b)], ["eo%d" % b])
        at("y0")
        copy("S", T.x0[:], T.in1[:].indirect(T.selr[:]), IN + ["selr"], ["x0_"])
        at("y1")
        turn(T.x1[:], T.x0[:], ["x0_"], ["x1_"])
        for c in range(10):
            at("eq%d" % (c // 5))
            act(T.eq[:, 33 * c:33 * c + 32], T.x1[:, 32 * (c // 2):32 * (c // 2) + 32], ACT.Abs, 2.0 ** 16, T.nb[:, c:c + 1], ["nb", "x1_"], ["eq%d" % c])
        at("kp")
        scan(T.kp[:], T.cm[:, 0:330], T.eq[:], 0.0, ALU.add, ALU.min, ["eq%d" % c for c in range(10)] + ["cm", "lwf"], ["kp"])
        at("so")
        ts(T.so[:, 0:10], T.kp[:, 32::33], -8.0, ALU.mult, r=["kp"], w=["so"])
        for q in (4, 3, 2, 1, 0):
            at("sc%d" % q)
            copy("V", T.sw[:, SW * (q % 2):SW * (q % 2) + SW].indirect(T.so[:, 2 * q:2 * q + 2]), T.sval[:, 32 * q:32 * q + 32], ["so", "sval"], ["sw%d" % (q % 2)])
        nn = lambda i: gs[:, 0:10] if i == 2 else T.nn[:, 10 * i:10 * i + 10]
        for i, (a, b, c) in ((2, (C, PL, 1)), (1, (1, C, 2)), (0, (0, C, 2))):
            for h in range(2):
                at("i%d%d" % (i, h))
                o = SW * h + SH
                scan(T.ns[:, PL * h + K * i:PL * h + K * i + K], T.cm[:, 336:496], T.sw[:, o + a:o + b:c], 0.0, ALU.add, ALU.max, ["sw%d" % h, "cn"], ["ns%d_%d" % (i, h)])
            at("gs" if i == 2 else "nn%d" % i)
            tt(nn(i), T.ns[:, K * i + 15:K * i + K:16], T.ns[:, PL + K * i + 15:PL + K * i + K:16], ALU.max, ["ns%d_0" % i, "ns%d_1" % i], ["gs" if i == 2 else "ns%d" % i])
        exchange(partner, giver, "ag%d" % t, [(gl[:, 0:10], gs[:, 0:10])], ["gs"], ["gl"])
        at("offo")
        ts(T.offo[:, 0:10], nn(1), -1.0, ALU.mult, pf(13), ALU.add, ["ns1", "pf13"], ["offo"])
        at("oo")
        affine(T.oo[:, 0:10], nn(0), 1.0, float(OWN), ["ns0"], ["oo"])

        def renew(e, how, width, off, buf, r):
            for b in four:
                a = T.est[:, EW * b:EW * b + width].indirect(off[:, 0:10])
                o, w = (T.xf[:, 4 * e + b::8], "y") if final else (T.xt[:, 4 * K * e + b:4 * K * (e + 1):4], "x")
                w, rb = [w + "eo"[e] + str(b)], [x % b if "%" in x else x for x in r]
                if how[b] == "V":
                    at("x" + "eo"[e] + str(b))
                    tt(o, a, T.vp[:, PV * b + SH + e:PV * b + SH + C:2], ALU.add, rb + ["vp%d_%d" % (b, e)], w)
                else:
                    a0 = K * e if XE[b] == "S" else 0
                    at("a" + "eo"[e] + str(b))
                    copy("S", buf[:, K * b:K * b + K], a, rb, ["a%d%d" % (e, b)])
                    at("x" + "eo"[e] + str(b))
                    tt(o, ps(b, a0, a0 + K), buf[:, K * b:K * b + K], ALU.add, ["ps%d" % b, "a%d%d" % (e, b)], w)
        at("do")
        for b in four:
            if XE[b] == "S": mm(b, T.ec, T.es, 128 * b, wc, ws, 0, C, ["ec%d" % b, "we", "wo"])
            elif XO[b] == "S": mm(b, T.ec, T.es, 128 * b, wc, ws, K, K, ["ec%d" % b, "wo"])
        renew(1, XO, K + 1, T.offo, T.ao, ["offo", "eo%d", "ez%d"])
        for b in four:
            at("mg")
            mm(4 + b, T.ec, T.es, 128 * b, hc, hs, K, K, ["ec%d" % b, "hl"])
            at("eg%d" % b)
            copy("S", T.est[:, EW * b + OWN:EW * b + OWN + K], ps(4 + b, 0, K), ["ps%d" % (4 + b)], ["eg%d" % b])
        at("em")
        tt(T.em[:, 0:10], T.oo[:, 0:10], gl[:, 0:10], ALU.max, ["oo", "gl"], ["em"])
        at("offe")
        ts(T.offe[:, 0:10], T.em[:, 0:10], -1.0, ALU.mult, pf(14), ALU.add, ["em", "pf14"], ["offe"])
        renew(0, XE, OWN + 1 + K, T.offe, T.ae, ["offe", "eo%d", "eg%d", "ez", "ez%d"])
        if not final: odd_columns(t + 1)

    for h in range(2):
        at("fc")
        quant(T.fc, T.fs, K * h, K * h + K, T.xf[:, 4 * K * h:4 * K * (h + 1)], ["ye%d" % b for b in four] + ["yo%d" % b for b in four], ["fc%d" % h])
        at("my")
        mm(h, T.vc, T.vs, 0, T.fc, T.fs, K * h, K, ["vc", "fc%d" % h])
        at("ysb")
        copy("SV"[h], T.ysb[:, K * h:K * h + K], ps(h, 0, K), ["ps%d" % h], ["ysb%d" % h])
    at("oc")
    dma("Y", "doc", [(T.oc[:], T.fc[:].bitcast(dt.uint8))], ["fc0", "fc1"])
    at("y")
    dma("S", "dy", [(T.y[:], T.ysb[:])], ["ysb0", "ysb1"])
    at("os")
    dma("Y", "dos", [(T.osc[4 * q:4 * q + 4, :], T.fs[32 * q:32 * q + 4, :]) for q in four], ["fc0", "fc1"])

    queue = {e: sorted((i for i, c in enumerate(calls) if c[0] == e), key=lambda i: (order[e].index(calls[i][1]), i), reverse=True) for e in Q}
    queue[None] = [i for i, c in enumerate(calls) if c[0] is None]
    done = {}
    known = {e: 0 for e in queue}
    count, last, waited = {}, {}, {}
    while any(queue.values()):
        e = [e for e in queue if queue[e] and calls[queue[e][-1]][3] <= done.keys()][-1]
        i = queue[e].pop()
        before = [p for p in done if done[p][0] == "g0"][-1:] if e == "G" else []
        for p in sorted(calls[i][3] | {p for p in before if (p in narrow) != (i in narrow) and calls[i][1][0] not in ("at", "ah", "ag")}, key=lambda p: -done[p][3]):
            if not known[e] >> p & 1:
                s, c, k, _ = done[p]
                Q[e].wait_ge(T.sem[s], c)
                waited[s] = max(waited.get(s, 0), c)
                known[e] |= k
        _, s, c = calls[i][2]()
        count[s] = count.get(s, 0) + c
        last[s] = known[e] | 1 << i | last.get(s, 0)
        done[i] = (s, count[s], last[s], len(done))
    for s in sorted(count, key=lambda s: s in DMAS):
        if waited.get(s, 0) < count[s]:
            Q[s[0].upper() if s in ("v0", "s0", "p0") else "G"].wait_ge(T.sem[s], count[s])
